import numpy as np
import ml_dtypes


def mxq(x, axis, fmt="e4m3"):
    dtype, down = {"e4m3": (ml_dtypes.float8_e4m3fn, 7), "e5m2": (ml_dtypes.float8_e5m2, 14)}[fmt]
    v = np.moveaxis(np.asarray(x, np.float32).astype(ml_dtypes.bfloat16).astype(np.float64), axis, -1)
    blocks = v.reshape(v.shape[:-1] + (-1, 32))
    amax = np.abs(blocks).max(-1, keepdims=True)
    byte = np.maximum(np.where(amax > 0, np.frexp(amax)[1] - 1 + 127, 0) - down, 1)
    scale = np.exp2(byte - 127.0)
    codes = (blocks / scale).astype(np.float32).astype(dtype).astype(np.float64)
    return np.moveaxis((codes * scale).reshape(v.shape), -1, axis)


WIDE = False


def mx_kscale(k):
    if not WIDE:
        return np.ones(k)
    levels = np.array([10, -10, 5, -5, 0])
    if k % 512:
        return np.exp2(np.random.permutation(np.resize(levels, k // 32))).repeat(32)
    a = np.empty((k // 512, 16))
    for p in range(k // 512):
        a[p, :8] = np.random.permutation(np.resize(levels, 8))
        for g in range(8):
            far = levels[np.abs(levels - a[p, g]) >= 10]
            a[p, g + 8] = far[np.random.randint(len(far))]
    return np.exp2(a.ravel()).repeat(32)


def f64(x):
    return np.asarray(x).astype(np.float64)


def striped(idx):
    return np.tile(idx.reshape(-1, 16).T, (8, 1)).astype(np.uint16)


def unstriped(offs):
    return offs[:16].T.reshape(-1).astype(np.int64)


def pack_weight(w):
    k, n = w.shape
    w = f64(np.asarray(w, np.float32).astype(ml_dtypes.bfloat16)).reshape(k // 32, 32, n)
    amax = np.abs(w).max(1)
    byte = np.clip(np.where(amax > 0, np.frexp(amax)[1] - 1 + 127 - 7, 1), 1, 254)
    scaled = (w * np.exp2(127.0 - byte)[:, None, :]).reshape(k, n).astype(np.float32)
    words = np.ascontiguousarray(scaled.reshape(k // 512, 128, 4, n).transpose(0, 1, 3, 2)).astype(ml_dtypes.float8_e4m3fn).view(np.uint8)
    return words, np.ascontiguousarray(byte.astype(np.uint8).reshape(k // 512, 16, n))


def unpack_weight(words, scales):
    g, p, n, _ = words.shape
    vals = np.ascontiguousarray(words).view(ml_dtypes.float8_e4m3fn).astype(np.float64) * np.repeat(np.exp2(scales.astype(np.float64) - 127.0), 8, axis=1)[..., None]
    return vals.transpose(0, 1, 3, 2).reshape(g * 512, n)


def relu(v):
    return np.maximum(v, 0.0)


K, T, S, D, V, H, N, U = 512, 2048, 1024, 3, 512, 512, 128, 256
P = 2 ** 7


def setup_inputs():
    n = np.random.standard_normal
    s = mx_kscale(K)[:, None]
    u = mx_kscale(H)
    packed_xT = pack_weight(n((K, T)) * s)
    packed_w2 = pack_weight(n((H, N)) / np.sqrt(H) / u[:, None])
    return {
        "x_words": packed_xT[0],
        "x_scales": packed_xT[1],
        "w1": (n((K, H)) / np.sqrt(K) / s * u).astype(np.float32),
        "w2_words": packed_w2[0],
        "w2_scales": packed_w2[1],
        "gate": (np.tile(np.random.uniform(0.2, 1.0, (D, 1, V)) / np.sqrt(D), (1, P, 1))).astype(np.float32),
        "gate2": (np.tile(np.random.uniform(0.2, 1.0, (D, 1, U)) / np.sqrt(D), (1, P, 1))).astype(np.float32),
        "offs": striped(np.random.permutation(T)[:S]),
        "pos1": striped(np.random.permutation(S)[:V]),
        "pos2": striped(np.random.permutation(S)[:V]),
        "pos3": striped(np.random.permutation(S)[:V]),
        "nxt1": striped(np.random.permutation(V)[:U]),
        "nxt2": striped(np.random.permutation(V)[:U]),
        "nxt3": striped(np.random.permutation(V)[:U]),
    }


def reference(x_words, x_scales, w1, w2_words, w2_scales, gate, gate2, offs, pos1, pos2, pos3, nxt1, nxt2, nxt3):
    xq = unpack_weight(x_words, x_scales)[:, unstriped(offs)]
    h = relu(mxq(f64(w1), 0, "e4m3").T @ xq)
    z = h[:, unstriped(pos1)] * f64(gate)[0, :1] + h[:, unstriped(pos2)] * f64(gate)[1, :1] + h[:, unstriped(pos3)] * f64(gate)[2, :1]
    g = relu(unpack_weight(w2_words, w2_scales).T @ mxq(z, 0, "e4m3"))
    return g[:, unstriped(nxt1)] * f64(gate2)[0, :1] + g[:, unstriped(nxt2)] * f64(gate2)[1, :1] + g[:, unstriped(nxt3)] * f64(gate2)[2, :1]

@@ -1,0 +1,201 @@
+from contextlib import ExitStack
+
+import concourse.mybir as mybir
+from concourse.masks import make_identity
+
+K, T, S, D, V, H, N, U = 512, 2048, 1024, 3, 512, 512, 128, 256
+P = 128
+FLOPS = 2 * K * H * S + 2 * H * N * V
+
+F32 = mybir.dt.float32
+BF16 = mybir.dt.bfloat16
+I32 = mybir.dt.int32
+U32 = mybir.dt.uint32
+U16 = mybir.dt.uint16
+U8 = mybir.dt.uint8
+FP8X4 = mybir.dt.float8_e4m3fn_x4
+ALU = mybir.AluOpType
+ACT = mybir.ActivationFunctionType
+
+CHUNKS = [(0, 256), (256, 384), (384, 512)]
+
+
+def tile_picked_hop2_relu_p_kernel(
+    tc, x_words, x_scales, w1, w2_words, w2_scales, gate, gate2, offs, pos1, pos2, pos3, nxt1, nxt2, nxt3, out
+):
+    nc = tc.nc
+    with ExitStack() as ctx:
+        keep = ctx.enter_context(tc.tile_pool(name="keep", bufs=1))
+        ring = ctx.enter_context(tc.tile_pool(name="ring", bufs=6))
+        work = ctx.enter_context(tc.tile_pool(name="work", bufs=3))
+        ps_h = ctx.enter_context(tc.psum_pool(name="ps_h", bufs=2))
+        ps_sum = ctx.enter_context(tc.psum_pool(name="ps_sum", bufs=3))
+        ps_back = ctx.enter_context(tc.psum_pool(name="ps_back", bufs=2))
+        ps_g = ctx.enter_context(tc.psum_pool(name="ps_g", bufs=1))
+
+        def load_list(src, name):
+            tile = keep.tile(list(src.shape), U16, name=name)
+            nc.sync.dma_start(tile[:], src)
+            return tile
+
+        def load_scale_rows(src, width, name):
+            plane = keep.tile([P, width], U8, name=name, align_bytes=64)
+            nc.vector.memset(plane[:].bitcast(I32), 0)
+            for q in range(4):
+                queue = nc.sync if q < 2 else nc.scalar
+                queue.dma_start(
+                    plane[32 * q : 32 * q + 4, :].bitcast(I32), src[0, 4 * q : 4 * q + 4, :].bitcast(I32)
+                )
+            return plane
+
+        def load_words(src, width, name):
+            words = keep.tile([P, width], I32, name=name, align_bytes=64)
+            nc.sync.dma_start(words[:], src[0].rearrange("p n t -> p (n t)").bitcast(I32))
+            return words
+
+        offs_sb = load_list(offs, "offs_sb")
+        x_scale_table = load_scale_rows(x_scales, T, "x_scale_table")
+        pos_sb = [load_list(src, "pos_sb%d" % d) for d, src in enumerate((pos1, pos2))]
+        x_word_table = load_words(x_words, T, "x_word_table")
+        w1_rows = w1.rearrange("(p t) c -> p t c", t=4)
+        w1_raw = []
+        for half in range(2):
+            raw = keep.tile([P, 4, H // 2], F32, name="w1_raw%d" % half)
+            nc.sync.dma_start(raw[:], w1_rows[:, :, half * (H // 2) : (half + 1) * (H // 2)])
+            w1_raw.append(raw)
+        pos_sb.append(load_list(pos3, "pos_sb2"))
+        gate_sb = []
+        for half in range(2):
+            tile = keep.tile([P, D, V // 2], F32, name="gate_sb%d" % half)
+            nc.sync.dma_start(
+                tile[:], gate.rearrange("d p v -> p d v")[:, :, half * (V // 2) : (half + 1) * (V // 2)]
+            )
+            gate_sb.append(tile)
+        w2_word_sb = load_words(w2_words, N, "w2_word_sb")
+        w2_scale_sb = load_scale_rows(w2_scales, N, "w2_scale_sb")
+        nxt_sb = [load_list(src, "nxt_sb%d" % d) for d, src in enumerate((nxt1, nxt2, nxt3))]
+        gate2_sb = keep.tile([P, D, U], F32)
+        nc.sync.dma_start(gate2_sb[:], gate2.rearrange("d p r -> p d r"))
+
+        ident = keep.tile([P, P], F32)
+        make_identity(nc, ident[:])
+
+        x_scale = keep.tile([P, S], U8, align_bytes=64)
+        nc.vector.tensor_copy(x_scale[:], x_scale_table[:].indirect(offs_sb[:]))
+        x_word = [keep.tile([P, S // 2], U32, name="x_word%d" % half, align_bytes=64) for half in range(2)]
+
+        def gather_words(a, b):
+            half, lo = divmod(a, S // 2)
+            nc.vector.tensor_copy(
+                x_word[half][:, lo : lo + b - a],
+                x_word_table[:].bitcast(U32).indirect(offs_sb[:, a // 16 : b // 16]),
+            )
+
+        w1_word, w1_scale = [], []
+
+        def quantize_w1(j):
+            half, lo = divmod(j * P, H // 2)
+            grouped = work.tile([P, P, 4], BF16, name="w1_grouped", align_bytes=64)
+            nc.scalar.activation(
+                grouped[:].rearrange("p (c i) t -> p c t i", i=4),
+                w1_raw[half][:, :, lo : lo + P].rearrange("p t (c i) -> p c t i", i=4),
+                ACT.Copy,
+            )
+            word = keep.tile([P, P], U32, name="w1_word%d" % j, align_bytes=64)
+            scale = keep.tile([P, P], U8, name="w1_scale%d" % j, align_bytes=64)
+            nc.vector.quantize_mx(
+                out=word[:].bitcast(FP8X4), scales=scale[:], in_=grouped[:].rearrange("p c t -> p (c t)")
+            )
+            w1_word.append(word)
+            w1_scale.append(scale)
+
+        h = [keep.tile([P, S], F32, name="h%d" % j) for j in range(H // P)]
+
+        def first_product(j, a, b):
+            half, lo = divmod(a, S // 2)
+            acc = ps_h.tile([P, b - a], F32, name="h_acc")
+            nc.tensor.matmul_mx(
+                out=acc[:],
+                lhsT=w1_word[j][:].bitcast(FP8X4),
+                lhsT_scale=w1_scale[j][:],
+                rhs=x_word[half][:, lo : lo + b - a].bitcast(FP8X4),
+                rhs_scale=x_scale[:, a:b],
+                start=True,
+                stop=True,
+            )
+            nc.scalar.activation(h[j][:, a:b], acc[:], ACT.Relu)
+
+        gather_words(0, 512)
+        quantize_w1(0)
+        first_product(0, 0, 512)
+        gather_words(512, 768)
+        first_product(0, 512, 768)
+        gather_words(768, 1024)
+        first_product(0, 768, 1024)
+        for j in range(1, H // P):
+            quantize_w1(j)
+            first_product(j, 0, 512)
+            first_product(j, 512, 1024)
+
+        g = keep.tile([P, V], F32)
+        for a, b in CHUNKS:
+            blocks = (b - a) // P
+            half, lo = divmod(a, V // 2)
+            sums = [ps_sum.tile([P, H], F32, name="z_sum") for block in range(blocks)]
+            for j in range(H // P):
+                for d in range(D):
+                    term = ring.tile([P, b - a], F32, name="term")
+                    nc.vector.tensor_tensor(
+                        term[:],
+                        h[j][:].indirect(pos_sb[d][:, a // 16 : b // 16]),
+                        gate_sb[half][:, d, lo : lo + b - a],
+                        ALU.mult,
+                    )
+                    for i in range(blocks):
+                        nc.tensor.matmul(
+                            sums[i][:, j * P : (j + 1) * P],
+                            term[:, i * P : (i + 1) * P],
+                            ident[:],
+                            start=(d == 0),
+                            stop=(d == D - 1),
+                            is_transpose=True,
+                        )
+            z_grouped = work.tile([P, b - a, 4], BF16, name="z_grouped", align_bytes=64)
+            for i in range(blocks):
+                z_rows = work.tile([P, 2, P, 2], BF16, name="z_rows")
+                nc.scalar.activation(
+                    z_rows[:], sums[i][:].rearrange("v (p u e) -> v u p e", u=2, e=2), ACT.Copy
+                )
+                pairs = z_rows[:].rearrange("v u p e -> v (u p e)").bitcast(F32)
+                back = ps_back.tile([P, 2, P], F32, name="back")
+                for u in range(2):
+                    nc.tensor.transpose(back[:, u, :], pairs[:, u * P : (u + 1) * P], ident[:])
+                nc.scalar.copy(
+                    z_grouped[:, i * P : (i + 1) * P, :].bitcast(F32),
+                    back[:].rearrange("p u v -> p v u"),
+                )
+            z_word = work.tile([P, b - a], U32, name="z_word", align_bytes=64)
+            z_scale = work.tile([P, b - a], U8, name="z_scale", align_bytes=64)
+            nc.vector.quantize_mx(
+                out=z_word[:].bitcast(FP8X4), scales=z_scale[:], in_=z_grouped[:].rearrange("p v t -> p (v t)")
+            )
+            acc = ps_g.tile([P, b - a], F32, name="g_acc")
+            nc.tensor.matmul_mx(
+                out=acc[:],
+                lhsT=w2_word_sb[:].bitcast(FP8X4),
+                lhsT_scale=w2_scale_sb[:],
+                rhs=z_word[:].bitcast(FP8X4),
+                rhs_scale=z_scale[:],
+                start=True,
+                stop=True,
+            )
+            nc.scalar.activation(g[:, a:b], acc[:], ACT.Relu)
+
+        terms = [keep.tile([P, U], F32, name="root_term%d" % d) for d in range(D)]
+        for d in range(D):
+            nc.vector.tensor_tensor(terms[d][:], g[:].indirect(nxt_sb[d][:]), gate2_sb[:, d, :], ALU.mult)
+        partial = keep.tile([P, U], F32)
+        nc.vector.tensor_tensor(partial[:], terms[0][:], terms[1][:], ALU.add)
+        result = keep.tile([P, U], F32)
+        nc.vector.tensor_tensor(result[:], partial[:], terms[2][:], ALU.add)
+        nc.sync.dma_start(out, result[:])

@@ -17,7 +17,8 @@ FP8X4 = mybir.dt.float8_e4m3fn_x4
 ALU = mybir.AluOpType
 ACT = mybir.ActivationFunctionType
 
-CHUNKS = [(0, 256), (256, 384), (384, 512)]
+TILES = H // P
+MAIN = V - P
 
 
 def tile_picked_hop2_relu_p_kernel(
@@ -28,51 +29,55 @@ def tile_picked_hop2_relu_p_kernel(
         keep = ctx.enter_context(tc.tile_pool(name="keep", bufs=1))
         ring = ctx.enter_context(tc.tile_pool(name="ring", bufs=6))
         work = ctx.enter_context(tc.tile_pool(name="work", bufs=3))
-        ps_h = ctx.enter_context(tc.psum_pool(name="ps_h", bufs=2))
-        ps_sum = ctx.enter_context(tc.psum_pool(name="ps_sum", bufs=3))
+        ps_a = ctx.enter_context(tc.psum_pool(name="ps_a", bufs=3))
+        ps_b = ctx.enter_context(tc.psum_pool(name="ps_b", bufs=3))
         ps_back = ctx.enter_context(tc.psum_pool(name="ps_back", bufs=2))
-        ps_g = ctx.enter_context(tc.psum_pool(name="ps_g", bufs=1))
 
         def load_list(src, name):
             tile = keep.tile(list(src.shape), U16, name=name)
             nc.sync.dma_start(tile[:], src)
             return tile
 
-        def load_scale_rows(src, width, name):
-            plane = keep.tile([P, width], U8, name=name, align_bytes=64)
-            nc.vector.memset(plane[:].bitcast(I32), 0)
+        def load_scale_rows(plane, src, queues):
             for q in range(4):
-                queue = nc.sync if q < 2 else nc.scalar
-                queue.dma_start(
+                queues[q].dma_start(
                     plane[32 * q : 32 * q + 4, :].bitcast(I32), src[0, 4 * q : 4 * q + 4, :].bitcast(I32)
                 )
-            return plane
 
         def load_words(src, width, name):
             words = keep.tile([P, width], I32, name=name, align_bytes=64)
             nc.sync.dma_start(words[:], src[0].rearrange("p n t -> p (n t)").bitcast(I32))
             return words
 
-        offs_sb = load_list(offs, "offs_sb")
-        x_scale_table = load_scale_rows(x_scales, T, "x_scale_table")
-        pos_sb = [load_list(src, "pos_sb%d" % d) for d, src in enumerate((pos1, pos2))]
-        x_word_table = load_words(x_words, T, "x_word_table")
         w1_rows = w1.rearrange("(p t) c -> p t c", t=4)
-        w1_raw = []
-        for half in range(2):
-            raw = keep.tile([P, 4, H // 2], F32, name="w1_raw%d" % half)
-            nc.sync.dma_start(raw[:], w1_rows[:, :, half * (H // 2) : (half + 1) * (H // 2)])
-            w1_raw.append(raw)
-        pos_sb.append(load_list(pos3, "pos_sb2"))
-        gate_sb = []
-        for half in range(2):
-            tile = keep.tile([P, D, V // 2], F32, name="gate_sb%d" % half)
-            nc.sync.dma_start(
-                tile[:], gate.rearrange("d p v -> p d v")[:, :, half * (V // 2) : (half + 1) * (V // 2)]
-            )
-            gate_sb.append(tile)
+
+        def load_w1(first, count):
+            raw = keep.tile([P, 4, count * P], F32, name="w1_raw%d" % first)
+            nc.sync.dma_start(raw[:], w1_rows[:, :, first * P : (first + count) * P])
+            return raw
+
+        def load_gate(a, b):
+            tile = keep.tile([P, D, b - a], F32, name="gate_sb%d" % a)
+            nc.sync.dma_start(tile[:], gate.rearrange("d p v -> p d v")[:, :, a:b])
+            return tile
+
+        offs_sb = load_list(offs, "offs_sb")
+        x_scale_table = keep.tile([P, T], U8, align_bytes=64)
+        nc.vector.memset(x_scale_table[:, : T // 2].bitcast(I32), 0)
+        nc.gpsimd.memset(x_scale_table[:, T // 2 :].bitcast(I32), 0)
+        load_scale_rows(x_scale_table, x_scales, (nc.sync, nc.scalar, nc.sync, nc.scalar))
+        w1_raw0 = load_w1(0, 1)
+        pos_sb = [load_list(pos1, "pos_sb0")]
+        x_word_table = load_words(x_words, T, "x_word_table")
+        w1_raw1 = load_w1(1, 1)
+        w1_raw2 = load_w1(2, 2)
+        pos_sb.extend([load_list(pos2, "pos_sb1"), load_list(pos3, "pos_sb2")])
+        gate_main = load_gate(0, MAIN)
+        gate_last = load_gate(MAIN, V)
         w2_word_sb = load_words(w2_words, N, "w2_word_sb")
-        w2_scale_sb = load_scale_rows(w2_scales, N, "w2_scale_sb")
+        w2_scale_sb = keep.tile([P, N], U8, align_bytes=64)
+        nc.vector.memset(w2_scale_sb[:].bitcast(I32), 0)
+        load_scale_rows(w2_scale_sb, w2_scales, (nc.sync,) * 4)
         nxt_sb = [load_list(src, "nxt_sb%d" % d) for d, src in enumerate((nxt1, nxt2, nxt3))]
         gate2_sb = keep.tile([P, D, U], F32)
         nc.sync.dma_start(gate2_sb[:], gate2.rearrange("d p r -> p d r"))
@@ -80,106 +85,94 @@ def tile_picked_hop2_relu_p_kernel(
         ident = keep.tile([P, P], F32)
         make_identity(nc, ident[:])
 
-        x_scale = keep.tile([P, S], U8, align_bytes=64)
-        nc.vector.tensor_copy(x_scale[:], x_scale_table[:].indirect(offs_sb[:]))
-        x_word = [keep.tile([P, S // 2], U32, name="x_word%d" % half, align_bytes=64) for half in range(2)]
+        w1_word = keep.tile([P, H], U32, align_bytes=64)
+        w1_scale = keep.tile([P, H], U8, align_bytes=64)
 
-        def gather_words(a, b):
-            half, lo = divmod(a, S // 2)
-            nc.vector.tensor_copy(
-                x_word[half][:, lo : lo + b - a],
-                x_word_table[:].bitcast(U32).indirect(offs_sb[:, a // 16 : b // 16]),
-            )
-
-        w1_word, w1_scale = [], []
-
-        def quantize_w1(j):
-            half, lo = divmod(j * P, H // 2)
-            grouped = work.tile([P, P, 4], BF16, name="w1_grouped", align_bytes=64)
-            nc.scalar.activation(
-                grouped[:].rearrange("p (c i) t -> p c t i", i=4),
-                w1_raw[half][:, :, lo : lo + P].rearrange("p t (c i) -> p c t i", i=4),
-                ACT.Copy,
-            )
-            word = keep.tile([P, P], U32, name="w1_word%d" % j, align_bytes=64)
-            scale = keep.tile([P, P], U8, name="w1_scale%d" % j, align_bytes=64)
+        def quantize_w1(raw, first, on_scalar):
+            width = raw.shape[2]
+            grouped = keep.tile([P, width, 4], BF16, name="w1_grouped%d" % first, align_bytes=64)
+            dst = grouped[:].rearrange("p (c i) t -> p c t i", i=4)
+            src = raw[:].rearrange("p t (c i) -> p c t i", i=4)
+            if on_scalar:
+                nc.scalar.activation(dst, src, ACT.Copy)
+            else:
+                nc.vector.tensor_copy(dst, src)
+            cols = slice(first * P, first * P + width)
             nc.vector.quantize_mx(
-                out=word[:].bitcast(FP8X4), scales=scale[:], in_=grouped[:].rearrange("p c t -> p (c t)")
+                out=w1_word[:, cols].bitcast(FP8X4),
+                scales=w1_scale[:, cols],
+                in_=grouped[:].rearrange("p c t -> p (c t)"),
             )
-            w1_word.append(word)
-            w1_scale.append(scale)
 
-        h = [keep.tile([P, S], F32, name="h%d" % j) for j in range(H // P)]
+        x_scale = keep.tile([P, S], U8, align_bytes=64)
+        x_word = keep.tile([P, S], U32, align_bytes=64)
+        h = [keep.tile([P, S], F32, name="h%d" % j) for j in range(TILES)]
 
         def first_product(j, a, b):
-            half, lo = divmod(a, S // 2)
-            acc = ps_h.tile([P, b - a], F32, name="h_acc")
+            acc = ps_a.tile([P, b - a], F32, name="h_acc", tag="a")
             nc.tensor.matmul_mx(
                 out=acc[:],
-                lhsT=w1_word[j][:].bitcast(FP8X4),
-                lhsT_scale=w1_scale[j][:],
-                rhs=x_word[half][:, lo : lo + b - a].bitcast(FP8X4),
+                lhsT=w1_word[:, j * P : (j + 1) * P].bitcast(FP8X4),
+                lhsT_scale=w1_scale[:, j * P : (j + 1) * P],
+                rhs=x_word[:, a:b].bitcast(FP8X4),
                 rhs_scale=x_scale[:, a:b],
                 start=True,
                 stop=True,
             )
             nc.scalar.activation(h[j][:, a:b], acc[:], ACT.Relu)
 
-        gather_words(0, 512)
-        quantize_w1(0)
-        first_product(0, 0, 512)
-        gather_words(512, 768)
-        first_product(0, 512, 768)
-        gather_words(768, 1024)
-        first_product(0, 768, 1024)
-        for j in range(1, H // P):
-            quantize_w1(j)
-            first_product(j, 0, 512)
-            first_product(j, 512, 1024)
+        nc.vector.tensor_copy(x_scale[:], x_scale_table[:].indirect(offs_sb[:]))
+        quantize_w1(w1_raw0, 0, True)
+        for a, b in ((0, 512), (512, 768), (768, 1024)):
+            nc.vector.tensor_copy(
+                x_word[:, a:b], x_word_table[:].bitcast(U32).indirect(offs_sb[:, a // 16 : b // 16])
+            )
+            first_product(0, a, b)
+        quantize_w1(w1_raw1, 1, True)
+        quantize_w1(w1_raw2, 2, False)
+        for j in range(1, TILES):
+            first_product(j, 0, S // 2)
+            first_product(j, S // 2, S)
 
         g = keep.tile([P, V], F32)
-        for a, b in CHUNKS:
-            blocks = (b - a) // P
-            half, lo = divmod(a, V // 2)
-            sums = [ps_sum.tile([P, H], F32, name="z_sum") for block in range(blocks)]
-            for j in range(H // P):
-                for d in range(D):
-                    term = ring.tile([P, b - a], F32, name="term")
-                    nc.vector.tensor_tensor(
-                        term[:],
-                        h[j][:].indirect(pos_sb[d][:, a // 16 : b // 16]),
-                        gate_sb[half][:, d, lo : lo + b - a],
-                        ALU.mult,
+
+        def add_terms(j, a, b, gate_sb, targets):
+            for d in range(D):
+                term = ring.tile([P, b - a], F32, name="term")
+                nc.vector.tensor_tensor(
+                    term[:], h[j][:].indirect(pos_sb[d][:, a // 16 : b // 16]), gate_sb[:, d, :], ALU.mult
+                )
+                for i, target in enumerate(targets):
+                    nc.tensor.matmul(
+                        target,
+                        term[:, i * P : (i + 1) * P],
+                        ident[:],
+                        start=(d == 0),
+                        stop=(d == D - 1),
+                        is_transpose=True,
                     )
-                    for i in range(blocks):
-                        nc.tensor.matmul(
-                            sums[i][:, j * P : (j + 1) * P],
-                            term[:, i * P : (i + 1) * P],
-                            ident[:],
-                            start=(d == 0),
-                            stop=(d == D - 1),
-                            is_transpose=True,
-                        )
-            z_grouped = work.tile([P, b - a, 4], BF16, name="z_grouped", align_bytes=64)
-            for i in range(blocks):
-                z_rows = work.tile([P, 2, P, 2], BF16, name="z_rows")
-                nc.scalar.activation(
-                    z_rows[:], sums[i][:].rearrange("v (p u e) -> v u p e", u=2, e=2), ACT.Copy
-                )
-                pairs = z_rows[:].rearrange("v u p e -> v (u p e)").bitcast(F32)
-                back = ps_back.tile([P, 2, P], F32, name="back")
-                for u in range(2):
-                    nc.tensor.transpose(back[:, u, :], pairs[:, u * P : (u + 1) * P], ident[:])
-                nc.scalar.copy(
-                    z_grouped[:, i * P : (i + 1) * P, :].bitcast(F32),
-                    back[:].rearrange("p u v -> p v u"),
-                )
+            return term
+
+        def round_rows(z_rows, p0, sums):
+            count = sums.shape[1] // 4
+            nc.scalar.activation(
+                z_rows[:, :, p0 : p0 + count, :], sums.rearrange("v (p u e) -> v u p e", u=2, e=2), ACT.Copy
+            )
+
+        def turn_back(z_rows, z_grouped):
+            pairs = z_rows[:].rearrange("v u p e -> v (u p e)").bitcast(F32)
+            back = ps_back.tile([P, 2, P], F32, name="back")
+            for u in range(2):
+                nc.tensor.transpose(back[:, u, :], pairs[:, u * P : (u + 1) * P], ident[:])
+            nc.scalar.copy(z_grouped.bitcast(F32), back[:].rearrange("p u v -> p v u"))
+
+        def second_product(z_grouped, a, b):
             z_word = work.tile([P, b - a], U32, name="z_word", align_bytes=64)
             z_scale = work.tile([P, b - a], U8, name="z_scale", align_bytes=64)
             nc.vector.quantize_mx(
-                out=z_word[:].bitcast(FP8X4), scales=z_scale[:], in_=z_grouped[:].rearrange("p v t -> p (v t)")
+                out=z_word[:].bitcast(FP8X4), scales=z_scale[:], in_=z_grouped.rearrange("p v t -> p (v t)")
             )
-            acc = ps_g.tile([P, b - a], F32, name="g_acc")
+            acc = ps_b.tile([P, b - a], F32, name="g_acc", tag="b")
             nc.tensor.matmul_mx(
                 out=acc[:],
                 lhsT=w2_word_sb[:].bitcast(FP8X4),
@@ -190,6 +183,29 @@ def tile_picked_hop2_relu_p_kernel(
                 stop=True,
             )
             nc.scalar.activation(g[:, a:b], acc[:], ACT.Relu)
+
+        z_all = keep.tile([P, V, 4], BF16, align_bytes=64)
+
+        sums = [ps_b.tile([P, H], F32, name="z_sum", tag="b") for block in range(MAIN // P)]
+        for j in range(TILES):
+            add_terms(j, 0, MAIN, gate_main, [acc[:, j * P : (j + 1) * P] for acc in sums])
+        for i, acc in enumerate(sums):
+            z_rows = work.tile([P, 2, P, 2], BF16, name="z_rows")
+            round_rows(z_rows, 0, acc[:])
+            turn_back(z_rows, z_all[:, i * P : (i + 1) * P, :])
+        second_product(z_all[:, : 2 * P, :], 0, 2 * P)
+        second_product(z_all[:, 2 * P : MAIN, :], 2 * P, MAIN)
+
+        early = ps_a.tile([P, H - P], F32, name="z_early", tag="a")
+        late = ps_a.tile([P, P], F32, name="z_late", tag="a")
+        z_rows = work.tile([P, 2, P, 2], BF16, name="z_rows")
+        for j in range(TILES - 1):
+            add_terms(j, MAIN, V, gate_last, [early[:, j * P : (j + 1) * P]])
+        round_rows(z_rows, 0, early[:])
+        last_term = add_terms(TILES - 1, MAIN, V, gate_last, [late[:]])
+        round_rows(z_rows, (H - P) // 4, late[:])
+        turn_back(z_rows, z_all[:, MAIN:, :])
+        second_product(z_all[:, MAIN:, :], MAIN, V)
 
         terms = [keep.tile([P, U], F32, name="root_term%d" % d) for d in range(D)]
         for d in range(D):

@@ -19,6 +19,7 @@ ACT = mybir.ActivationFunctionType
 
 TILES = H // P
 MAIN = V - P
+EARLY = 768
 
 
 def tile_picked_hop2_relu_p_kernel(
@@ -27,6 +28,7 @@ def tile_picked_hop2_relu_p_kernel(
     nc = tc.nc
     with ExitStack() as ctx:
         keep = ctx.enter_context(tc.tile_pool(name="keep", bufs=1))
+        stage = ctx.enter_context(tc.tile_pool(name="stage", bufs=1))
         ring = ctx.enter_context(tc.tile_pool(name="ring", bufs=6))
         work = ctx.enter_context(tc.tile_pool(name="work", bufs=3))
         ps_a = ctx.enter_context(tc.psum_pool(name="ps_a", bufs=3))
@@ -44,37 +46,34 @@ def tile_picked_hop2_relu_p_kernel(
                     plane[32 * q : 32 * q + 4, :].bitcast(I32), src[0, 4 * q : 4 * q + 4, :].bitcast(I32)
                 )
 
-        def load_words(src, width, name):
-            words = keep.tile([P, width], I32, name=name, align_bytes=64)
+        def load_words(words, src):
             nc.sync.dma_start(words[:], src[0].rearrange("p n t -> p (n t)").bitcast(I32))
-            return words
 
         w1_rows = w1.rearrange("(p t) c -> p t c", t=4)
 
-        def load_w1(first, count):
-            raw = keep.tile([P, 4, count * P], F32, name="w1_raw%d" % first)
-            nc.sync.dma_start(raw[:], w1_rows[:, :, first * P : (first + count) * P])
-            return raw
+        def load_w1(half):
+            raw = keep.tile([P, 4, H // 2], F32, name="w1_raw%d" % half)
+            nc.sync.dma_start(raw[:], w1_rows[:, :, half * (H // 2) : (half + 1) * (H // 2)])
+            return raw[:].rearrange("p t (q u e) -> p u q t e", u=2, e=2)
 
-        def load_gate(a, b):
-            tile = keep.tile([P, D, b - a], F32, name="gate_sb%d" % a)
-            nc.sync.dma_start(tile[:], gate.rearrange("d p v -> p d v")[:, :, a:b])
+        def load_gate(d):
+            tile = keep.tile([P, V], F32, name="gate_sb%d" % d)
+            nc.sync.dma_start(tile[:], gate[d])
             return tile
 
         offs_sb = load_list(offs, "offs_sb")
         x_scale_table = keep.tile([P, T], U8, align_bytes=64)
-        nc.vector.memset(x_scale_table[:, : T // 2].bitcast(I32), 0)
-        nc.gpsimd.memset(x_scale_table[:, T // 2 :].bitcast(I32), 0)
+        nc.vector.memset(x_scale_table[:].bitcast(I32), 0)
         load_scale_rows(x_scale_table, x_scales, (nc.sync, nc.scalar, nc.sync, nc.scalar))
-        w1_raw0 = load_w1(0, 1)
-        pos_sb = [load_list(pos1, "pos_sb0")]
-        x_word_table = load_words(x_words, T, "x_word_table")
-        w1_raw1 = load_w1(1, 1)
-        w1_raw2 = load_w1(2, 2)
-        pos_sb.extend([load_list(pos2, "pos_sb1"), load_list(pos3, "pos_sb2")])
-        gate_main = load_gate(0, MAIN)
-        gate_last = load_gate(MAIN, V)
-        w2_word_sb = load_words(w2_words, N, "w2_word_sb")
+        pos_sb = [load_list(pos1, "pos_sb0"), load_list(pos2, "pos_sb1")]
+        x_word_table = keep.tile([P, T], I32, align_bytes=64)
+        load_words(x_word_table, x_words)
+        w1_raw = [load_w1(0), load_w1(1)]
+        gate_sb = [load_gate(0)]
+        pos_sb.append(load_list(pos3, "pos_sb2"))
+        gate_sb.extend([load_gate(1), load_gate(2)])
+        w2_word_sb = keep.tile([P, N], I32, align_bytes=64)
+        load_words(w2_word_sb, w2_words)
         w2_scale_sb = keep.tile([P, N], U8, align_bytes=64)
         nc.vector.memset(w2_scale_sb[:].bitcast(I32), 0)
         load_scale_rows(w2_scale_sb, w2_scales, (nc.sync,) * 4)
@@ -88,60 +87,66 @@ def tile_picked_hop2_relu_p_kernel(
         w1_word = keep.tile([P, H], U32, align_bytes=64)
         w1_scale = keep.tile([P, H], U8, align_bytes=64)
 
-        def quantize_w1(raw, first, on_scalar):
-            width = raw.shape[2]
-            grouped = keep.tile([P, width, 4], BF16, name="w1_grouped%d" % first, align_bytes=64)
-            dst = grouped[:].rearrange("p (c i) t -> p c t i", i=4)
-            src = raw[:].rearrange("p t (c i) -> p c t i", i=4)
-            if on_scalar:
-                nc.scalar.activation(dst, src, ACT.Copy)
-            else:
-                nc.vector.tensor_copy(dst, src)
-            cols = slice(first * P, first * P + width)
-            nc.vector.quantize_mx(
-                out=w1_word[:, cols].bitcast(FP8X4),
-                scales=w1_scale[:, cols],
-                in_=grouped[:].rearrange("p c t -> p (c t)"),
-            )
+        def quantize_w1(grouped, first):
+            cols = slice(first * P, first * P + grouped.shape[1] // 4)
+            nc.vector.quantize_mx(out=w1_word[:, cols].bitcast(FP8X4), scales=w1_scale[:, cols], in_=grouped)
 
         x_scale = keep.tile([P, S], U8, align_bytes=64)
-        x_word = keep.tile([P, S], U32, align_bytes=64)
         h = [keep.tile([P, S], F32, name="h%d" % j) for j in range(TILES)]
+        x_word = {}
 
-        def first_product(j, a, b):
+        def gather_words(words, a):
+            b = a + words.shape[1]
+            nc.vector.tensor_copy(words[:], x_word_table[:].bitcast(U32).indirect(offs_sb[:, a // 16 : b // 16]))
+            x_word[a] = words
+
+        def first_product(j, edges):
+            a, b = edges[0], edges[-1]
             acc = ps_a.tile([P, b - a], F32, name="h_acc", tag="a")
-            nc.tensor.matmul_mx(
-                out=acc[:],
-                lhsT=w1_word[:, j * P : (j + 1) * P].bitcast(FP8X4),
-                lhsT_scale=w1_scale[:, j * P : (j + 1) * P],
-                rhs=x_word[:, a:b].bitcast(FP8X4),
-                rhs_scale=x_scale[:, a:b],
-                start=True,
-                stop=True,
-            )
+            for lo, hi in zip(edges, edges[1:]):
+                base = 0 if lo < EARLY else EARLY
+                nc.tensor.matmul_mx(
+                    out=acc[:, lo - a : hi - a],
+                    lhsT=w1_word[:, j * P : (j + 1) * P].bitcast(FP8X4),
+                    lhsT_scale=w1_scale[:, j * P : (j + 1) * P],
+                    rhs=x_word[base][:, lo - base : hi - base].bitcast(FP8X4),
+                    rhs_scale=x_scale[:, lo:hi],
+                    start=True,
+                    stop=True,
+                )
             nc.scalar.activation(h[j][:, a:b], acc[:], ACT.Relu)
 
         nc.vector.tensor_copy(x_scale[:], x_scale_table[:].indirect(offs_sb[:]))
-        quantize_w1(w1_raw0, 0, True)
-        for a, b in ((0, 512), (512, 768), (768, 1024)):
-            nc.vector.tensor_copy(
-                x_word[:, a:b], x_word_table[:].bitcast(U32).indirect(offs_sb[:, a // 16 : b // 16])
-            )
-            first_product(0, a, b)
-        quantize_w1(w1_raw1, 1, True)
-        quantize_w1(w1_raw2, 2, False)
+        gather_words(keep.tile([P, EARLY], U32, name="x_word_early", align_bytes=64), 0)
+        first = stage.tile([P, P * 4], BF16, offset=512, align_bytes=64)
+        nc.scalar.activation(first[:].rearrange("p (q e t) -> p q t e", e=2, t=4), w1_raw[0][:, 0], ACT.Copy)
+        quantize_w1(first[:], 0)
+        first_product(0, (0, S // 2))
+        first_product(0, (S // 2, EARLY))
+        gather_words(stage.tile([P, S - EARLY], U32, name="x_word_late", offset=0, align_bytes=64), EARLY)
+        first_product(0, (EARLY, S))
+        rest = stage.tile([P, 3 * P * 4], BF16, offset=1024, align_bytes=64)
+        nc.vector.tensor_copy(rest[:, : P * 4].rearrange("p (q e t) -> p q t e", e=2, t=4), w1_raw[1][:, 0])
+        single = rest[:, P * 4 :].rearrange("p (e half q t) -> p half q t e", e=2, half=2, t=4)
+        nc.scalar.activation(single[:, 0], w1_raw[0][:, 1], ACT.Copy)
+        nc.vector.tensor_copy(single[:, 1], w1_raw[1][:, 1])
+        quantize_w1(rest[:, : P * 4], 1)
+        quantize_w1(rest[:, P * 4 :], 2)
         for j in range(1, TILES):
-            first_product(j, 0, S // 2)
-            first_product(j, S // 2, S)
+            first_product(j, (0, S // 2))
+            first_product(j, (S // 2, EARLY, S))
 
         g = keep.tile([P, V], F32)
 
-        def add_terms(j, a, b, gate_sb, targets):
+        def weighted_gather(term, j, d, a, b):
+            nc.vector.tensor_tensor(
+                term, h[j][:].indirect(pos_sb[d][:, a // 16 : b // 16]), gate_sb[d][:, a:b], ALU.mult
+            )
+
+        def add_terms(j, a, b, targets):
             for d in range(D):
                 term = ring.tile([P, b - a], F32, name="term")
-                nc.vector.tensor_tensor(
-                    term[:], h[j][:].indirect(pos_sb[d][:, a // 16 : b // 16]), gate_sb[:, d, :], ALU.mult
-                )
+                weighted_gather(term[:], j, d, a, b)
                 for i, target in enumerate(targets):
                     nc.tensor.matmul(
                         target,
@@ -151,20 +156,17 @@ def tile_picked_hop2_relu_p_kernel(
                         stop=(d == D - 1),
                         is_transpose=True,
                     )
-            return term
 
-        def round_rows(z_rows, p0, sums):
-            count = sums.shape[1] // 4
-            nc.scalar.activation(
-                z_rows[:, :, p0 : p0 + count, :], sums.rearrange("v (p u e) -> v u p e", u=2, e=2), ACT.Copy
-            )
-
-        def turn_back(z_rows, z_grouped):
+        def turn_back(sums, z_block):
+            count = len(sums)
+            z_rows = work.tile([P, count, P, 2], BF16, name="z_rows")
+            for u in range(count):
+                nc.scalar.activation(z_rows[:, u], sums[u], ACT.Copy)
             pairs = z_rows[:].rearrange("v u p e -> v (u p e)").bitcast(F32)
-            back = ps_back.tile([P, 2, P], F32, name="back")
-            for u in range(2):
+            back = ps_back.tile([P, count, P], F32, name="back")
+            for u in range(count):
                 nc.tensor.transpose(back[:, u, :], pairs[:, u * P : (u + 1) * P], ident[:])
-            nc.scalar.copy(z_grouped.bitcast(F32), back[:].rearrange("p u v -> p v u"))
+            nc.scalar.copy(z_block.bitcast(F32)[:, :, :count], back[:].rearrange("p u v -> p v u"))
 
         def second_product(z_grouped, a, b):
             z_word = work.tile([P, b - a], U32, name="z_word", align_bytes=64)
@@ -184,28 +186,41 @@ def tile_picked_hop2_relu_p_kernel(
             )
             nc.scalar.activation(g[:, a:b], acc[:], ACT.Relu)
 
-        z_all = keep.tile([P, V, 4], BF16, align_bytes=64)
+        z_all = keep.tile([P, MAIN, 4], BF16, align_bytes=64)
+        z_last = keep.tile([P, P, 4], BF16, align_bytes=64)
 
         sums = [ps_b.tile([P, H], F32, name="z_sum", tag="b") for block in range(MAIN // P)]
         for j in range(TILES):
-            add_terms(j, 0, MAIN, gate_main, [acc[:, j * P : (j + 1) * P] for acc in sums])
+            add_terms(j, 0, MAIN, [acc[:, j * P : (j + 1) * P] for acc in sums])
         for i, acc in enumerate(sums):
-            z_rows = work.tile([P, 2, P, 2], BF16, name="z_rows")
-            round_rows(z_rows, 0, acc[:])
-            turn_back(z_rows, z_all[:, i * P : (i + 1) * P, :])
+            low = acc[:, : 2 * P].rearrange("v (p e) -> v p e", e=2)
+            high = acc[:, 2 * P :].rearrange("v (e p) -> v p e", e=2)
+            turn_back([low, high], z_all[:, i * P : (i + 1) * P, :])
         second_product(z_all[:, : 2 * P, :], 0, 2 * P)
-        second_product(z_all[:, 2 * P : MAIN, :], 2 * P, MAIN)
 
-        early = ps_a.tile([P, H - P], F32, name="z_early", tag="a")
-        late = ps_a.tile([P, P], F32, name="z_late", tag="a")
-        z_rows = work.tile([P, 2, P, 2], BF16, name="z_rows")
-        for j in range(TILES - 1):
-            add_terms(j, MAIN, V, gate_last, [early[:, j * P : (j + 1) * P]])
-        round_rows(z_rows, 0, early[:])
-        last_term = add_terms(TILES - 1, MAIN, V, gate_last, [late[:]])
-        round_rows(z_rows, (H - P) // 4, late[:])
-        turn_back(z_rows, z_all[:, MAIN:, :])
-        second_product(z_all[:, MAIN:, :], MAIN, V)
+        acc = ps_a.tile([P, 2 * P], F32, name="z_sum_last", tag="a")
+        for j in range(2):
+            add_terms(j, MAIN, V, [acc[:, j * P : (j + 1) * P]])
+        turn_back([acc[:].rearrange("v (p e) -> v p e", e=2)], z_last[:])
+        direct = [ring.tile([P, 2, P], F32, name="term") for d in range(D)]
+        for d in range(D - 1):
+            for e in range(2):
+                weighted_gather(direct[d][:, e, :], 2 + e, d, MAIN, V)
+        weighted_gather(direct[2][:, 0, :], 2, 2, MAIN, V)
+        two = keep.tile([P, 2, P], F32)
+        nc.vector.tensor_tensor(two[:], direct[0][:], direct[1][:], ALU.add)
+        for lo in (0, P // 2):
+            weighted_gather(direct[2][:, 1, lo : lo + P // 2], 3, 2, MAIN + lo, MAIN + lo + P // 2)
+        for lo in (0, P // 2):
+            part = slice(lo, lo + P // 2)
+            nc.vector.tensor_tensor(
+                z_last[:, part, 2:],
+                two[:, :, part].rearrange("p e v -> p v e"),
+                direct[2][:, :, part].rearrange("p e v -> p v e"),
+                ALU.add,
+            )
+        second_product(z_all[:, 2 * P :, :], 2 * P, MAIN)
+        second_product(z_last[:], MAIN, V)
 
         terms = [keep.tile([P, U], F32, name="root_term%d" % d) for d in range(D)]
         for d in range(D):

@@ -18,8 +18,8 @@ ALU = mybir.AluOpType
 ACT = mybir.ActivationFunctionType
 
 TILES = H // P
-MAIN = V - P
-EARLY = 768
+BLOCKS = V // P
+BANK = 2048
 
 
 def tile_picked_hop2_relu_p_kernel(
@@ -29,11 +29,10 @@ def tile_picked_hop2_relu_p_kernel(
     with ExitStack() as ctx:
         keep = ctx.enter_context(tc.tile_pool(name="keep", bufs=1))
         stage = ctx.enter_context(tc.tile_pool(name="stage", bufs=1))
-        ring = ctx.enter_context(tc.tile_pool(name="ring", bufs=6))
-        work = ctx.enter_context(tc.tile_pool(name="work", bufs=3))
-        ps_a = ctx.enter_context(tc.psum_pool(name="ps_a", bufs=3))
-        ps_b = ctx.enter_context(tc.psum_pool(name="ps_b", bufs=3))
-        ps_back = ctx.enter_context(tc.psum_pool(name="ps_back", bufs=2))
+        psum = ctx.enter_context(tc.psum_pool(name="psum", bufs=1))
+
+        def bank(b, shape, name):
+            return psum.tile(shape, F32, name=name, offset=b * BANK)
 
         def load_list(src, name):
             tile = keep.tile(list(src.shape), U16, name=name)
@@ -51,9 +50,9 @@ def tile_picked_hop2_relu_p_kernel(
 
         w1_rows = w1.rearrange("(p t) c -> p t c", t=4)
 
-        def load_w1(half):
-            raw = keep.tile([P, 4, H // 2], F32, name="w1_raw%d" % half)
-            nc.sync.dma_start(raw[:], w1_rows[:, :, half * (H // 2) : (half + 1) * (H // 2)])
+        def load_w1(a, b, pool=keep, offset=None):
+            raw = pool.tile([P, 4, b - a], F32, name="w1_raw%d" % a, offset=offset, align_bytes=64)
+            nc.sync.dma_start(raw[:], w1_rows[:, :, a:b])
             return raw[:].rearrange("p t (q u e) -> p u q t e", u=2, e=2)
 
         def load_gate(d):
@@ -65,13 +64,16 @@ def tile_picked_hop2_relu_p_kernel(
         x_scale_table = keep.tile([P, T], U8, align_bytes=64)
         nc.vector.memset(x_scale_table[:].bitcast(I32), 0)
         load_scale_rows(x_scale_table, x_scales, (nc.sync, nc.scalar, nc.sync, nc.scalar))
-        pos_sb = [load_list(pos1, "pos_sb0"), load_list(pos2, "pos_sb1")]
+        w1_raw = [load_w1(0, P)]
+        pos_sb = [load_list(pos1, "pos_sb0")]
         x_word_table = keep.tile([P, T], I32, align_bytes=64)
         load_words(x_word_table, x_words)
-        w1_raw = [load_w1(0), load_w1(1)]
+        w1_raw.extend([load_w1(P, 2 * P, stage, 0), load_w1(2 * P, H)])
         gate_sb = [load_gate(0)]
+        pos_sb.append(load_list(pos2, "pos_sb1"))
+        gate_sb.append(load_gate(1))
         pos_sb.append(load_list(pos3, "pos_sb2"))
-        gate_sb.extend([load_gate(1), load_gate(2)])
+        gate_sb.append(load_gate(2))
         w2_word_sb = keep.tile([P, N], I32, align_bytes=64)
         load_words(w2_word_sb, w2_words)
         w2_scale_sb = keep.tile([P, N], U8, align_bytes=64)
@@ -93,48 +95,64 @@ def tile_picked_hop2_relu_p_kernel(
 
         x_scale = keep.tile([P, S], U8, align_bytes=64)
         h = [keep.tile([P, S], F32, name="h%d" % j) for j in range(TILES)]
-        x_word = {}
+        x_early = keep.tile([P, S // 2], U32, align_bytes=64)
 
-        def gather_words(words, a):
-            b = a + words.shape[1]
-            nc.vector.tensor_copy(words[:], x_word_table[:].bitcast(U32).indirect(offs_sb[:, a // 16 : b // 16]))
-            x_word[a] = words
+        def gather_words(words, a, b):
+            nc.vector.tensor_copy(words, x_word_table[:].bitcast(U32).indirect(offs_sb[:, a // 16 : b // 16]))
 
-        def first_product(j, edges):
-            a, b = edges[0], edges[-1]
-            acc = ps_a.tile([P, b - a], F32, name="h_acc", tag="a")
-            for lo, hi in zip(edges, edges[1:]):
-                base = 0 if lo < EARLY else EARLY
-                nc.tensor.matmul_mx(
-                    out=acc[:, lo - a : hi - a],
-                    lhsT=w1_word[:, j * P : (j + 1) * P].bitcast(FP8X4),
-                    lhsT_scale=w1_scale[:, j * P : (j + 1) * P],
-                    rhs=x_word[base][:, lo - base : hi - base].bitcast(FP8X4),
-                    rhs_scale=x_scale[:, lo:hi],
-                    start=True,
-                    stop=True,
-                )
-            nc.scalar.activation(h[j][:, a:b], acc[:], ACT.Relu)
+        def product(acc, lhs_word, lhs_scale, rhs_word, rhs_scale):
+            nc.tensor.matmul_mx(
+                out=acc,
+                lhsT=lhs_word.bitcast(FP8X4),
+                lhsT_scale=lhs_scale,
+                rhs=rhs_word.bitcast(FP8X4),
+                rhs_scale=rhs_scale,
+                start=True,
+                stop=True,
+            )
+
+        def relu(dst, acc, on_vector):
+            if on_vector:
+                nc.vector.tensor_scalar(dst, acc, 0.0, None, ALU.max)
+            else:
+                nc.scalar.activation(dst, acc, ACT.Relu)
+
+        def first_product(j, words, a, b, where, on_vector=False):
+            acc = bank(where, [P, b - a], "h_acc%d_%d" % (j, a))
+            cols = slice(j * P, (j + 1) * P)
+            product(acc[:], w1_word[:, cols], w1_scale[:, cols], words, x_scale[:, a:b])
+            relu(h[j][:, a:b], acc[:], on_vector)
 
         nc.vector.tensor_copy(x_scale[:], x_scale_table[:].indirect(offs_sb[:]))
-        gather_words(keep.tile([P, EARLY], U32, name="x_word_early", align_bytes=64), 0)
-        first = stage.tile([P, P * 4], BF16, offset=512, align_bytes=64)
-        nc.scalar.activation(first[:].rearrange("p (q e t) -> p q t e", e=2, t=4), w1_raw[0][:, 0], ACT.Copy)
+        gather_words(x_early[:], 0, S // 2)
+        first = keep.tile([P, P * 4], BF16, align_bytes=64)
+        first_view = first[:].rearrange("p (q e t) -> p q t e", e=2, t=4)
+        nc.scalar.activation(first_view[:, :32], w1_raw[0][:, 0], ACT.Copy)
+        nc.scalar.activation(first_view[:, 32:], w1_raw[1][:, 0], ACT.Copy)
         quantize_w1(first[:], 0)
-        first_product(0, (0, S // 2))
-        first_product(0, (S // 2, EARLY))
-        gather_words(stage.tile([P, S - EARLY], U32, name="x_word_late", offset=0, align_bytes=64), EARLY)
-        first_product(0, (EARLY, S))
-        rest = stage.tile([P, 3 * P * 4], BF16, offset=1024, align_bytes=64)
-        nc.vector.tensor_copy(rest[:, : P * 4].rearrange("p (q e t) -> p q t e", e=2, t=4), w1_raw[1][:, 0])
-        single = rest[:, P * 4 :].rearrange("p (e half q t) -> p half q t e", e=2, half=2, t=4)
-        nc.scalar.activation(single[:, 0], w1_raw[0][:, 1], ACT.Copy)
-        nc.vector.tensor_copy(single[:, 1], w1_raw[1][:, 1])
-        quantize_w1(rest[:, : P * 4], 1)
-        quantize_w1(rest[:, P * 4 :], 2)
-        for j in range(1, TILES):
-            first_product(j, (0, S // 2))
-            first_product(j, (S // 2, EARLY, S))
+        upper = keep.tile([P, 2 * P * 4], BF16, align_bytes=64)
+        upper_view = upper[:].rearrange("p (e q t) -> p q t e", e=2, t=4)
+        nc.scalar.activation(upper_view[:, :32], w1_raw[0][:, 1], ACT.Copy)
+        nc.scalar.activation(upper_view[:, 32:64], w1_raw[1][:, 1], ACT.Copy)
+        first_product(0, x_early[:, :256], 0, 256, 0)
+        first_product(0, x_early[:, 256:], 256, 512, 1)
+        x_late = stage.tile([P, S // 2], U32, offset=0, align_bytes=64)
+        gather_words(x_late[:, :256], 512, 768)
+        first_product(0, x_late[:, :256], 512, 768, 2)
+        gather_words(x_late[:, 256:], 768, S)
+        first_product(0, x_late[:, 256:384], 768, 896, 3)
+        first_product(0, x_late[:, 384:], 896, S, 4, on_vector=True)
+
+        second = keep.tile([P, P * 4], BF16, align_bytes=64)
+        nc.scalar.activation(second[:].rearrange("p (q e t) -> p q t e", e=2, t=4), w1_raw[2][:, 0], ACT.Copy)
+        nc.scalar.activation(upper_view[:, 64:], w1_raw[2][:, 1], ACT.Copy)
+        quantize_w1(upper[:], 2)
+        quantize_w1(second[:], 1)
+        first_product(1, x_early[:], 0, S // 2, 0)
+        first_product(1, x_late[:], S // 2, S, 1)
+        for j in range(2, TILES):
+            first_product(j, x_early[:], 0, S // 2, 2 * j - 2)
+            first_product(j, x_late[:], S // 2, S, 2 * j - 1)
 
         g = keep.tile([P, V], F32)
 
@@ -145,88 +163,104 @@ def tile_picked_hop2_relu_p_kernel(
 
         def add_terms(j, a, b, targets):
             for d in range(D):
-                term = ring.tile([P, b - a], F32, name="term")
+                term = keep.tile([P, b - a], F32, name="term%d_%d_%d" % (j, d, a))
                 weighted_gather(term[:], j, d, a, b)
                 for i, target in enumerate(targets):
                     nc.tensor.matmul(
                         target,
                         term[:, i * P : (i + 1) * P],
                         ident[:],
-                        start=(d == 0),
-                        stop=(d == D - 1),
+                        start=(d == 0 and i == 0),
+                        stop=(d == D - 1 and i == len(targets) - 1),
                         is_transpose=True,
                     )
 
-        def turn_back(sums, z_block):
-            count = len(sums)
-            z_rows = work.tile([P, count, P, 2], BF16, name="z_rows")
-            for u in range(count):
-                nc.scalar.activation(z_rows[:, u], sums[u], ACT.Copy)
-            pairs = z_rows[:].rearrange("v u p e -> v (u p e)").bitcast(F32)
-            back = ps_back.tile([P, count, P], F32, name="back")
-            for u in range(count):
-                nc.tensor.transpose(back[:, u, :], pairs[:, u * P : (u + 1) * P], ident[:])
-            nc.scalar.copy(z_block.bitcast(F32)[:, :, :count], back[:].rearrange("p u v -> p v u"))
+        def turn_back(z_rows, where, z_parts, word, name):
+            count = z_rows.shape[1]
+            back = bank(where, [P, count, P], name)
+            pairs = z_rows.rearrange("v i p e -> v (i p e)").bitcast(F32)
+            for i in range(count):
+                nc.tensor.transpose(back[:, i, :], pairs[:, i * P : (i + 1) * P], ident[:])
+            lo = 0
+            for part in z_parts:
+                hi = lo + part.shape[1]
+                nc.scalar.copy(part[:].bitcast(F32)[:, :, word], back[:].rearrange("p i v -> p (i v)")[:, lo:hi])
+                lo = hi
 
-        def second_product(z_grouped, a, b):
-            z_word = work.tile([P, b - a], U32, name="z_word", align_bytes=64)
-            z_scale = work.tile([P, b - a], U8, name="z_scale", align_bytes=64)
+        def second_product(z_grouped, a, b, where, on_vector=False):
+            z_word = keep.tile([P, b - a], U32, name="z_word%d" % a, align_bytes=64)
+            z_scale = keep.tile([P, b - a], U8, name="z_scale%d" % a, align_bytes=64)
             nc.vector.quantize_mx(
                 out=z_word[:].bitcast(FP8X4), scales=z_scale[:], in_=z_grouped.rearrange("p v t -> p (v t)")
             )
-            acc = ps_b.tile([P, b - a], F32, name="g_acc", tag="b")
-            nc.tensor.matmul_mx(
-                out=acc[:],
-                lhsT=w2_word_sb[:].bitcast(FP8X4),
-                lhsT_scale=w2_scale_sb[:],
-                rhs=z_word[:].bitcast(FP8X4),
-                rhs_scale=z_scale[:],
-                start=True,
-                stop=True,
-            )
-            nc.scalar.activation(g[:, a:b], acc[:], ACT.Relu)
+            acc = bank(where, [P, b - a], "g_acc%d" % a)
+            product(acc[:], w2_word_sb[:], w2_scale_sb[:], z_word[:], z_scale[:])
+            relu(g[:, a:b], acc[:], on_vector)
 
-        z_all = keep.tile([P, MAIN, 4], BF16, align_bytes=64)
-        z_last = keep.tile([P, P, 4], BF16, align_bytes=64)
+        z = [keep.tile([P, n, 4], BF16, name="z%d" % i, align_bytes=64) for i, n in enumerate((2 * P, P, P))]
 
-        sums = [ps_b.tile([P, H], F32, name="z_sum", tag="b") for block in range(MAIN // P)]
-        for j in range(TILES):
-            add_terms(j, 0, MAIN, [acc[:, j * P : (j + 1) * P] for acc in sums])
-        for i, acc in enumerate(sums):
-            low = acc[:, : 2 * P].rearrange("v (p e) -> v p e", e=2)
-            high = acc[:, 2 * P :].rearrange("v (e p) -> v p e", e=2)
-            turn_back([low, high], z_all[:, i * P : (i + 1) * P, :])
-        second_product(z_all[:, : 2 * P, :], 0, 2 * P)
-
-        acc = ps_a.tile([P, 2 * P], F32, name="z_sum_last", tag="a")
+        low_rows = keep.tile([P, BLOCKS, P, 2], BF16)
         for j in range(2):
-            add_terms(j, MAIN, V, [acc[:, j * P : (j + 1) * P]])
-        turn_back([acc[:].rearrange("v (p e) -> v p e", e=2)], z_last[:])
-        direct = [ring.tile([P, 2, P], F32, name="term") for d in range(D)]
+            acc = bank(6 + j, [P, BLOCKS, P], "low_sum%d" % j)
+            add_terms(j, 0, V, [acc[:, i, :] for i in range(BLOCKS)])
+            nc.scalar.activation(
+                low_rows[:, :, 64 * j : 64 * (j + 1), :], acc[:].rearrange("v i (q e) -> v i q e", e=2), ACT.Copy
+            )
+        turn_back(low_rows[:], 0, z, 0, "low_back")
+
+        rows_a = keep.tile([P, 2, P, 2], BF16)
+        for e in range(2):
+            acc = bank(6 + e, [P, 2, P], "high_sum_a%d" % e)
+            add_terms(2 + e, 0, 2 * P, [acc[:, i, :] for i in range(2)])
+            nc.scalar.activation(rows_a[:, :, :, e], acc[:], ACT.Copy)
+        turn_back(rows_a[:], 2, z[:1], 1, "high_back_a")
+        second_product(z[0][:], 0, 2 * P, 3)
+
+        third = keep.tile([P, 2 * P], F32)
+        rows_b = third[:, P:].bitcast(BF16).rearrange("v (i p e) -> v i p e", i=1, e=2)
+        for e in range(2):
+            acc = bank(6 + e, [P, P], "high_sum_b%d" % e)
+            add_terms(2 + e, 2 * P, 3 * P, [acc[:]])
+            nc.scalar.activation(rows_b[:, 0, :, e], acc[:], ACT.Copy)
+        turn_back(rows_b, 5, z[1:2], 1, "high_back_b")
+
+        last = 3 * P
+        direct = [keep.tile([P, 2, P], F32, name="direct%d" % d) for d in range(D - 1)]
+        direct.append(third[:].rearrange("p (e v) -> p e v", e=2))
         for d in range(D - 1):
             for e in range(2):
-                weighted_gather(direct[d][:, e, :], 2 + e, d, MAIN, V)
-        weighted_gather(direct[2][:, 0, :], 2, 2, MAIN, V)
+                weighted_gather(direct[d][:, e, :], 2 + e, d, last, V)
+        weighted_gather(direct[2][:, 0, :], 2, 2, last, V)
         two = keep.tile([P, 2, P], F32)
         nc.vector.tensor_tensor(two[:], direct[0][:], direct[1][:], ALU.add)
         for lo in (0, P // 2):
-            weighted_gather(direct[2][:, 1, lo : lo + P // 2], 3, 2, MAIN + lo, MAIN + lo + P // 2)
+            weighted_gather(direct[2][:, 1, lo : lo + P // 2], 3, 2, last + lo, last + lo + P // 2)
         for lo in (0, P // 2):
             part = slice(lo, lo + P // 2)
             nc.vector.tensor_tensor(
-                z_last[:, part, 2:],
+                z[2][:, part, 2:],
                 two[:, :, part].rearrange("p e v -> p v e"),
                 direct[2][:, :, part].rearrange("p e v -> p v e"),
                 ALU.add,
             )
-        second_product(z_all[:, 2 * P :, :], 2 * P, MAIN)
-        second_product(z_last[:], MAIN, V)
+        second_product(z[1][:], 2 * P, last, 4)
+        second_product(z[2][:], last, V, 1, on_vector=True)
 
         terms = [keep.tile([P, U], F32, name="root_term%d" % d) for d in range(D)]
-        for d in range(D):
-            nc.vector.tensor_tensor(terms[d][:], g[:].indirect(nxt_sb[d][:]), gate2_sb[:, d, :], ALU.mult)
+
+        def root_gather(d, a, b):
+            nc.vector.tensor_tensor(
+                terms[d][:, a:b], g[:].indirect(nxt_sb[d][:, a // 16 : b // 16]), gate2_sb[:, d, a:b], ALU.mult
+            )
+
+        root_gather(0, 0, U)
+        root_gather(1, 0, U)
+        root_gather(2, 0, U // 2)
         partial = keep.tile([P, U], F32)
         nc.vector.tensor_tensor(partial[:], terms[0][:], terms[1][:], ALU.add)
+        root_gather(2, U // 2, U)
         result = keep.tile([P, U], F32)
-        nc.vector.tensor_tensor(result[:], partial[:], terms[2][:], ALU.add)
-        nc.sync.dma_start(out, result[:])
+        for a in (0, U // 2):
+            part = slice(a, a + U // 2)
+            nc.vector.tensor_tensor(result[:, part], partial[:, part], terms[2][:, part], ALU.add)
+            nc.sync.dma_start(out[:, part], result[:, part])

@@ -20,6 +20,7 @@ ACT = mybir.ActivationFunctionType
 TILES = H // P
 BLOCKS = V // P
 BANK = 2048
+EARLY = 768
 
 
 def tile_picked_hop2_relu_p_kernel(
@@ -50,8 +51,8 @@ def tile_picked_hop2_relu_p_kernel(
 
         w1_rows = w1.rearrange("(p t) c -> p t c", t=4)
 
-        def load_w1(a, b, pool=keep, offset=None):
-            raw = pool.tile([P, 4, b - a], F32, name="w1_raw%d" % a, offset=offset, align_bytes=64)
+        def load_w1(a, b):
+            raw = keep.tile([P, 4, b - a], F32, name="w1_raw%d" % a)
             nc.sync.dma_start(raw[:], w1_rows[:, :, a:b])
             return raw[:].rearrange("p t (q u e) -> p u q t e", u=2, e=2)
 
@@ -64,16 +65,13 @@ def tile_picked_hop2_relu_p_kernel(
         x_scale_table = keep.tile([P, T], U8, align_bytes=64)
         nc.vector.memset(x_scale_table[:].bitcast(I32), 0)
         load_scale_rows(x_scale_table, x_scales, (nc.sync, nc.scalar, nc.sync, nc.scalar))
-        w1_raw = [load_w1(0, P)]
-        pos_sb = [load_list(pos1, "pos_sb0")]
+        pos_sb = [load_list(pos1, "pos_sb0"), load_list(pos2, "pos_sb1")]
         x_word_table = keep.tile([P, T], I32, align_bytes=64)
         load_words(x_word_table, x_words)
-        w1_raw.extend([load_w1(P, 2 * P, stage, 0), load_w1(2 * P, H)])
+        w1_raw = [load_w1(0, H // 2), load_w1(H // 2, H)]
         gate_sb = [load_gate(0)]
-        pos_sb.append(load_list(pos2, "pos_sb1"))
-        gate_sb.append(load_gate(1))
         pos_sb.append(load_list(pos3, "pos_sb2"))
-        gate_sb.append(load_gate(2))
+        gate_sb.extend([load_gate(1), load_gate(2)])
         w2_word_sb = keep.tile([P, N], I32, align_bytes=64)
         load_words(w2_word_sb, w2_words)
         w2_scale_sb = keep.tile([P, N], U8, align_bytes=64)
@@ -95,7 +93,7 @@ def tile_picked_hop2_relu_p_kernel(
 
         x_scale = keep.tile([P, S], U8, align_bytes=64)
         h = [keep.tile([P, S], F32, name="h%d" % j) for j in range(TILES)]
-        x_early = keep.tile([P, S // 2], U32, align_bytes=64)
+        x_early = keep.tile([P, EARLY], U32, align_bytes=64)
 
         def gather_words(words, a, b):
             nc.vector.tensor_copy(words, x_word_table[:].bitcast(U32).indirect(offs_sb[:, a // 16 : b // 16]))
@@ -117,42 +115,36 @@ def tile_picked_hop2_relu_p_kernel(
             else:
                 nc.scalar.activation(dst, acc, ACT.Relu)
 
-        def first_product(j, words, a, b, where, on_vector=False):
+        def first_product(j, edges, where, on_vector=False):
+            a, b = edges[0], edges[-1]
             acc = bank(where, [P, b - a], "h_acc%d_%d" % (j, a))
             cols = slice(j * P, (j + 1) * P)
-            product(acc[:], w1_word[:, cols], w1_scale[:, cols], words, x_scale[:, a:b])
+            for lo, hi in zip(edges, edges[1:]):
+                words = x_early[:, lo:hi] if lo < EARLY else x_late[:, lo - EARLY : hi - EARLY]
+                product(acc[:, lo - a : hi - a], w1_word[:, cols], w1_scale[:, cols], words, x_scale[:, lo:hi])
             relu(h[j][:, a:b], acc[:], on_vector)
 
         nc.vector.tensor_copy(x_scale[:], x_scale_table[:].indirect(offs_sb[:]))
-        gather_words(x_early[:], 0, S // 2)
-        first = keep.tile([P, P * 4], BF16, align_bytes=64)
-        first_view = first[:].rearrange("p (q e t) -> p q t e", e=2, t=4)
-        nc.scalar.activation(first_view[:, :32], w1_raw[0][:, 0], ACT.Copy)
-        nc.scalar.activation(first_view[:, 32:], w1_raw[1][:, 0], ACT.Copy)
+        gather_words(x_early[:], 0, EARLY)
+        first = stage.tile([P, P * 4], BF16, offset=512, align_bytes=64)
+        nc.scalar.activation(first[:].rearrange("p (q e t) -> p q t e", e=2, t=4), w1_raw[0][:, 0], ACT.Copy)
         quantize_w1(first[:], 0)
+        x_late = stage.tile([P, S - EARLY], U32, offset=0, align_bytes=64)
+        for i in range(3):
+            first_product(0, (256 * i, 256 * (i + 1)), i)
+        gather_words(x_late[:], EARLY, S)
+        first_product(0, (EARLY, S), 3, on_vector=True)
         upper = keep.tile([P, 2 * P * 4], BF16, align_bytes=64)
-        upper_view = upper[:].rearrange("p (e q t) -> p q t e", e=2, t=4)
-        nc.scalar.activation(upper_view[:, :32], w1_raw[0][:, 1], ACT.Copy)
-        nc.scalar.activation(upper_view[:, 32:64], w1_raw[1][:, 1], ACT.Copy)
-        first_product(0, x_early[:, :256], 0, 256, 0)
-        first_product(0, x_early[:, 256:], 256, 512, 1)
-        x_late = stage.tile([P, S // 2], U32, offset=0, align_bytes=64)
-        gather_words(x_late[:, :256], 512, 768)
-        first_product(0, x_late[:, :256], 512, 768, 2)
-        gather_words(x_late[:, 256:], 768, S)
-        first_product(0, x_late[:, 256:384], 768, 896, 3)
-        first_product(0, x_late[:, 384:], 896, S, 4, on_vector=True)
-
-        second = keep.tile([P, P * 4], BF16, align_bytes=64)
-        nc.scalar.activation(second[:].rearrange("p (q e t) -> p q t e", e=2, t=4), w1_raw[2][:, 0], ACT.Copy)
-        nc.scalar.activation(upper_view[:, 64:], w1_raw[2][:, 1], ACT.Copy)
+        upper_view = upper[:].rearrange("p (e half q t) -> p half q t e", e=2, half=2, t=4)
+        for half in range(2):
+            nc.scalar.activation(upper_view[:, half], w1_raw[half][:, 1], ACT.Copy)
+        second = stage.tile([P, P * 4], BF16, offset=1024, align_bytes=64)
+        nc.vector.tensor_copy(second[:].rearrange("p (q e t) -> p q t e", e=2, t=4), w1_raw[1][:, 0])
         quantize_w1(upper[:], 2)
         quantize_w1(second[:], 1)
-        first_product(1, x_early[:], 0, S // 2, 0)
-        first_product(1, x_late[:], S // 2, S, 1)
-        for j in range(2, TILES):
-            first_product(j, x_early[:], 0, S // 2, 2 * j - 2)
-            first_product(j, x_late[:], S // 2, S, 2 * j - 1)
+        for j in range(1, TILES):
+            first_product(j, (0, S // 2), (2 * j + 2) % 6)
+            first_product(j, (S // 2, EARLY, S), (2 * j + 3) % 6)
 
         g = keep.tile([P, V], F32)
 
@@ -161,106 +153,103 @@ def tile_picked_hop2_relu_p_kernel(
                 term, h[j][:].indirect(pos_sb[d][:, a // 16 : b // 16]), gate_sb[d][:, a:b], ALU.mult
             )
 
-        def add_terms(j, a, b, targets):
+        def add_terms(j, a, b, targets, one_bank):
             for d in range(D):
                 term = keep.tile([P, b - a], F32, name="term%d_%d_%d" % (j, d, a))
-                weighted_gather(term[:], j, d, a, b)
+                weighted_gather(term[:, :], j, d, a, b)
                 for i, target in enumerate(targets):
                     nc.tensor.matmul(
                         target,
                         term[:, i * P : (i + 1) * P],
                         ident[:],
-                        start=(d == 0 and i == 0),
-                        stop=(d == D - 1 and i == len(targets) - 1),
+                        start=(d == 0 and (i == 0 or not one_bank)),
+                        stop=(d == D - 1 and (i == len(targets) - 1 or not one_bank)),
                         is_transpose=True,
                     )
 
-        def turn_back(z_rows, where, z_parts, word, name):
-            count = z_rows.shape[1]
-            back = bank(where, [P, count, P], name)
-            pairs = z_rows.rearrange("v i p e -> v (i p e)").bitcast(F32)
-            for i in range(count):
-                nc.tensor.transpose(back[:, i, :], pairs[:, i * P : (i + 1) * P], ident[:])
-            lo = 0
-            for part in z_parts:
-                hi = lo + part.shape[1]
-                nc.scalar.copy(part[:].bitcast(F32)[:, :, word], back[:].rearrange("p i v -> p (i v)")[:, lo:hi])
-                lo = hi
+        def turn_back(rows, block, u):
+            nc.tensor.transpose(back[block][:, u, :], rows.rearrange("v p e -> v (p e)").bitcast(F32), ident[:])
+
+        def copy_out(block, z_block, count):
+            nc.scalar.copy(z_block.bitcast(F32)[:, :, :count], back[block][:].rearrange("p u v -> p v u"))
 
         def second_product(z_grouped, a, b, where, on_vector=False):
-            z_word = keep.tile([P, b - a], U32, name="z_word%d" % a, align_bytes=64)
-            z_scale = keep.tile([P, b - a], U8, name="z_scale%d" % a, align_bytes=64)
             nc.vector.quantize_mx(
-                out=z_word[:].bitcast(FP8X4), scales=z_scale[:], in_=z_grouped.rearrange("p v t -> p (v t)")
+                out=z_word[:, a:b].bitcast(FP8X4), scales=z_scale[:, a:b], in_=z_grouped.rearrange("p v t -> p (v t)")
             )
             acc = bank(where, [P, b - a], "g_acc%d" % a)
-            product(acc[:], w2_word_sb[:], w2_scale_sb[:], z_word[:], z_scale[:])
+            product(acc[:], w2_word_sb[:], w2_scale_sb[:], z_word[:, a:b], z_scale[:, a:b])
             relu(g[:, a:b], acc[:], on_vector)
 
         z = [keep.tile([P, n, 4], BF16, name="z%d" % i, align_bytes=64) for i, n in enumerate((2 * P, P, P))]
 
         low_rows = keep.tile([P, BLOCKS, P, 2], BF16)
-        for j in range(2):
-            acc = bank(6 + j, [P, BLOCKS, P], "low_sum%d" % j)
-            add_terms(j, 0, V, [acc[:, i, :] for i in range(BLOCKS)])
+        back = [bank(i, [P, 2 if i < BLOCKS - 1 else 1, P], "back%d" % i) for i in range(BLOCKS)]
+
+        def low_pairs(j, first_block, count):
+            acc = bank(6 + j, [P, count, P], "low_sum%d_%d" % (j, first_block))
+            blocks = range(first_block, first_block + count)
+            add_terms(j, blocks[0] * P, (blocks[-1] + 1) * P, [acc[:, i, :] for i in range(count)], True)
             nc.scalar.activation(
-                low_rows[:, :, 64 * j : 64 * (j + 1), :], acc[:].rearrange("v i (q e) -> v i q e", e=2), ACT.Copy
+                low_rows[:, first_block : first_block + count, 64 * j : 64 * (j + 1), :],
+                acc[:].rearrange("v i (q e) -> v i q e", e=2),
+                ACT.Copy,
             )
-        turn_back(low_rows[:], 0, z, 0, "low_back")
+            if j == 1:
+                for i in blocks:
+                    turn_back(low_rows[:, i], i, 0)
 
-        rows_a = keep.tile([P, 2, P, 2], BF16)
-        for e in range(2):
-            acc = bank(6 + e, [P, 2, P], "high_sum_a%d" % e)
-            add_terms(2 + e, 0, 2 * P, [acc[:, i, :] for i in range(2)])
-            nc.scalar.activation(rows_a[:, :, :, e], acc[:], ACT.Copy)
-        turn_back(rows_a[:], 2, z[:1], 1, "high_back_a")
-        second_product(z[0][:], 0, 2 * P, 3)
+        high_rows = [keep.tile([P, P, 2], BF16, name="high_rows%d" % i) for i in range(BLOCKS - 2)]
+        high_rows.append(stage.tile([P, P, 2], BF16, name="high_rows2", offset=2048, align_bytes=64))
+        z_blocks = [z[0][:, :P, :], z[0][:, P:, :], z[1][:]]
 
-        third = keep.tile([P, 2 * P], F32)
-        rows_b = third[:, P:].bitcast(BF16).rearrange("v (i p e) -> v i p e", i=1, e=2)
-        for e in range(2):
-            acc = bank(6 + e, [P, P], "high_sum_b%d" % e)
-            add_terms(2 + e, 2 * P, 3 * P, [acc[:]])
-            nc.scalar.activation(rows_b[:, 0, :, e], acc[:], ACT.Copy)
-        turn_back(rows_b, 5, z[1:2], 1, "high_back_b")
+        def high_pairs(blocks):
+            sums = [bank(4 + i, [P, 2, P], "high_sum%d" % i) for i in blocks]
+            for e in range(2):
+                targets = [acc[:, e, :] for acc in sums]
+                add_terms(2 + e, blocks[0] * P, (blocks[-1] + 1) * P, targets, False)
+            for i, acc in zip(blocks, sums):
+                nc.scalar.activation(high_rows[i][:], acc[:].rearrange("v e p -> v p e"), ACT.Copy)
+                turn_back(high_rows[i][:], i, 1)
+                copy_out(i, z_blocks[i], 2)
+
+        low_pairs(0, 0, BLOCKS)
+        low_pairs(1, 0, 2)
+        high_pairs([0, 1])
+        low_pairs(1, 2, 2)
+        copy_out(BLOCKS - 1, z[2][:], 1)
+        high_pairs([2])
 
         last = 3 * P
-        direct = [keep.tile([P, 2, P], F32, name="direct%d" % d) for d in range(D - 1)]
-        direct.append(third[:].rearrange("p (e v) -> p e v", e=2))
-        for d in range(D - 1):
+        halves = (slice(0, P // 2), slice(P // 2, P))
+        direct = [keep.tile([P, 2, P], F32, name="direct%d" % d) for d in range(D)]
+        for d in range(D):
             for e in range(2):
                 weighted_gather(direct[d][:, e, :], 2 + e, d, last, V)
-        weighted_gather(direct[2][:, 0, :], 2, 2, last, V)
         two = keep.tile([P, 2, P], F32)
-        nc.vector.tensor_tensor(two[:], direct[0][:], direct[1][:], ALU.add)
-        for lo in (0, P // 2):
-            weighted_gather(direct[2][:, 1, lo : lo + P // 2], 3, 2, last + lo, last + lo + P // 2)
-        for lo in (0, P // 2):
-            part = slice(lo, lo + P // 2)
+        for part in halves:
+            nc.vector.tensor_tensor(two[:, :, part], direct[0][:, :, part], direct[1][:, :, part], ALU.add)
+        for part in halves:
             nc.vector.tensor_tensor(
                 z[2][:, part, 2:],
                 two[:, :, part].rearrange("p e v -> p v e"),
                 direct[2][:, :, part].rearrange("p e v -> p v e"),
                 ALU.add,
             )
-        second_product(z[1][:], 2 * P, last, 4)
-        second_product(z[2][:], last, V, 1, on_vector=True)
+        z_word = stage.tile([P, V], U32, offset=2048, align_bytes=64)
+        z_scale = keep.tile([P, V], U8, align_bytes=64)
+        second_product(z[0][:], 0, 2 * P, 4)
+        second_product(z[2][:], last, V, 7)
+        second_product(z[1][:], 2 * P, last, 5, on_vector=True)
 
+        halves = (slice(0, U // 2), slice(U // 2, U))
         terms = [keep.tile([P, U], F32, name="root_term%d" % d) for d in range(D)]
-
-        def root_gather(d, a, b):
-            nc.vector.tensor_tensor(
-                terms[d][:, a:b], g[:].indirect(nxt_sb[d][:, a // 16 : b // 16]), gate2_sb[:, d, a:b], ALU.mult
-            )
-
-        root_gather(0, 0, U)
-        root_gather(1, 0, U)
-        root_gather(2, 0, U // 2)
+        for d in range(D):
+            nc.vector.tensor_tensor(terms[d][:], g[:].indirect(nxt_sb[d][:]), gate2_sb[:, d, :], ALU.mult)
         partial = keep.tile([P, U], F32)
-        nc.vector.tensor_tensor(partial[:], terms[0][:], terms[1][:], ALU.add)
-        root_gather(2, U // 2, U)
+        for part in halves:
+            nc.vector.tensor_tensor(partial[:, part], terms[0][:, part], terms[1][:, part], ALU.add)
         result = keep.tile([P, U], F32)
-        for a in (0, U // 2):
-            part = slice(a, a + U // 2)
+        for part in halves:
             nc.vector.tensor_tensor(result[:, part], partial[:, part], terms[2][:, part], ALU.add)
-            nc.sync.dma_start(out[:, part], result[:, part])
+        nc.sync.dma_start(out, result[:])

@@ -181,10 +181,13 @@ def tile_picked_hop2_relu_p_kernel(
             product(acc[:], w2_word_sb[:], w2_scale_sb[:], z_word[:, a:b], z_scale[:, a:b])
             relu(g[:, a:b], acc[:], on_vector)
 
-        z = [keep.tile([P, n, 4], BF16, name="z%d" % i, align_bytes=64) for i, n in enumerate((2 * P, P, P))]
+        z_direct = keep.tile([P, P, 4], BF16, align_bytes=64)
+        z_early = keep.tile([P, 2 * P, 4], BF16, align_bytes=64)
+        z_late = keep.tile([P, P, 4], BF16, align_bytes=64)
+        z_blocks = [z_direct[:], z_early[:, :P, :], z_early[:, P:, :], z_late[:]]
 
         low_rows = keep.tile([P, BLOCKS, P, 2], BF16)
-        back = [bank(i, [P, 2 if i < BLOCKS - 1 else 1, P], "back%d" % i) for i in range(BLOCKS)]
+        back = [bank(i, [P, 2 if i else 1, P], "back%d" % i) for i in range(BLOCKS)]
 
         def low_pairs(j, first_block, count):
             acc = bank(6 + j, [P, count, P], "low_sum%d_%d" % (j, first_block))
@@ -199,12 +202,11 @@ def tile_picked_hop2_relu_p_kernel(
                 for i in blocks:
                     turn_back(low_rows[:, i], i, 0)
 
-        high_rows = [keep.tile([P, P, 2], BF16, name="high_rows%d" % i) for i in range(BLOCKS - 2)]
-        high_rows.append(stage.tile([P, P, 2], BF16, name="high_rows2", offset=2048, align_bytes=64))
-        z_blocks = [z[0][:, :P, :], z[0][:, P:, :], z[1][:]]
+        high_rows = {i: keep.tile([P, P, 2], BF16, name="high_rows%d" % i) for i in (1, 2)}
+        high_rows[3] = stage.tile([P, P, 2], BF16, name="high_rows3", offset=2048, align_bytes=64)
 
         def high_pairs(blocks):
-            sums = [bank(4 + i, [P, 2, P], "high_sum%d" % i) for i in blocks]
+            sums = [bank(3 + i, [P, 2, P], "high_sum%d" % i) for i in blocks]
             for e in range(2):
                 targets = [acc[:, e, :] for acc in sums]
                 add_terms(2 + e, blocks[0] * P, (blocks[-1] + 1) * P, targets, False)
@@ -214,33 +216,32 @@ def tile_picked_hop2_relu_p_kernel(
                 copy_out(i, z_blocks[i], 2)
 
         low_pairs(0, 0, BLOCKS)
-        low_pairs(1, 0, 2)
-        high_pairs([0, 1])
-        low_pairs(1, 2, 2)
-        copy_out(BLOCKS - 1, z[2][:], 1)
-        high_pairs([2])
+        low_pairs(1, 0, BLOCKS - 1)
+        copy_out(0, z_blocks[0], 1)
+        high_pairs([1, 2])
+        low_pairs(1, BLOCKS - 1, 1)
+        high_pairs([3])
 
-        last = 3 * P
         halves = (slice(0, P // 2), slice(P // 2, P))
         direct = [keep.tile([P, 2, P], F32, name="direct%d" % d) for d in range(D)]
         for d in range(D):
             for e in range(2):
-                weighted_gather(direct[d][:, e, :], 2 + e, d, last, V)
+                weighted_gather(direct[d][:, e, :], 2 + e, d, 0, P)
         two = keep.tile([P, 2, P], F32)
         for part in halves:
             nc.vector.tensor_tensor(two[:, :, part], direct[0][:, :, part], direct[1][:, :, part], ALU.add)
         for part in halves:
             nc.vector.tensor_tensor(
-                z[2][:, part, 2:],
+                z_direct[:, part, 2:],
                 two[:, :, part].rearrange("p e v -> p v e"),
                 direct[2][:, :, part].rearrange("p e v -> p v e"),
                 ALU.add,
             )
         z_word = stage.tile([P, V], U32, offset=2048, align_bytes=64)
         z_scale = keep.tile([P, V], U8, align_bytes=64)
-        second_product(z[0][:], 0, 2 * P, 4)
-        second_product(z[2][:], last, V, 7)
-        second_product(z[1][:], 2 * P, last, 5, on_vector=True)
+        second_product(z_early[:], P, 3 * P, 4)
+        second_product(z_direct[:], 0, P, 7, on_vector=True)
+        second_product(z_late[:], 3 * P, V, 5)
 
         halves = (slice(0, U // 2), slice(U // 2, U))
         terms = [keep.tile([P, U], F32, name="root_term%d" % d) for d in range(D)]

@@ -88,7 +88,7 @@ def tile_picked_hop2_relu_p_kernel(
         w1_scale = keep.tile([P, H], U8, align_bytes=64)
 
         def quantize_w1(grouped, first):
-            cols = slice(first * P, first * P + grouped.shape[1] // 4)
+            cols = slice(first, first + grouped.shape[1] // 4)
             nc.vector.quantize_mx(out=w1_word[:, cols].bitcast(FP8X4), scales=w1_scale[:, cols], in_=grouped)
 
         x_scale = keep.tile([P, S], U8, align_bytes=64)
@@ -129,22 +129,21 @@ def tile_picked_hop2_relu_p_kernel(
         first = stage.tile([P, P * 4], BF16, offset=512, align_bytes=64)
         nc.scalar.activation(first[:].rearrange("p (q e t) -> p q t e", e=2, t=4), w1_raw[0][:, 0], ACT.Copy)
         quantize_w1(first[:], 0)
+        planes = stage.tile([P, 4, 2, 64, 4], BF16, offset=1024, align_bytes=64)
+        nc.scalar.activation(planes[:, 2:, 0].rearrange("p e q t -> p q t e"), w1_raw[0][:, 1], ACT.Copy)
         x_late = stage.tile([P, S - EARLY], U32, offset=0, align_bytes=64)
         for i in range(3):
             first_product(0, (256 * i, 256 * (i + 1)), i)
         gather_words(x_late[:], EARLY, S)
-        first_product(0, (EARLY, S), 3, on_vector=True)
-        upper = keep.tile([P, 2 * P * 4], BF16, align_bytes=64)
-        upper_view = upper[:].rearrange("p (e half q t) -> p half q t e", e=2, half=2, t=4)
-        for half in range(2):
-            nc.scalar.activation(upper_view[:, half], w1_raw[half][:, 1], ACT.Copy)
-        second = stage.tile([P, P * 4], BF16, offset=1024, align_bytes=64)
-        nc.vector.tensor_copy(second[:].rearrange("p (q e t) -> p q t e", e=2, t=4), w1_raw[1][:, 0])
-        quantize_w1(upper[:], 2)
-        quantize_w1(second[:], 1)
+        first_product(0, (EARLY, EARLY + P), 3, on_vector=True)
+        first_product(0, (EARLY + P, S), 4)
+        nc.vector.tensor_copy(planes[:, :, 1].rearrange("p c q t -> p q t c"), w1_raw[1].rearrange("p u q t e -> p q t (u e)"))
+        for e in range(2):
+            quantize_w1(planes[:, e, 1].rearrange("p q t -> p (q t)"), P + 64 * e)
+        quantize_w1(planes[:, 2:].rearrange("p c half q t -> p (c half q t)"), 2 * P)
         for j in range(1, TILES):
-            first_product(j, (0, S // 2), (2 * j + 2) % 6)
-            first_product(j, (S // 2, EARLY, S), (2 * j + 3) % 6)
+            first_product(j, (0, S // 2), (2 * j + 3) % 6)
+            first_product(j, (S // 2, EARLY, S), (2 * j + 4) % 6)
 
         g = keep.tile([P, V], F32)
 
@@ -195,7 +194,7 @@ def tile_picked_hop2_relu_p_kernel(
             add_terms(j, blocks[0] * P, (blocks[-1] + 1) * P, [acc[:, i, :] for i in range(count)], True)
             nc.scalar.activation(
                 low_rows[:, first_block : first_block + count, 64 * j : 64 * (j + 1), :],
-                acc[:].rearrange("v i (q e) -> v i q e", e=2),
+                acc[:].rearrange("v i (e q) -> v i q e" if j else "v i (q e) -> v i q e", e=2),
                 ACT.Copy,
             )
             if j == 1:
@@ -203,7 +202,7 @@ def tile_picked_hop2_relu_p_kernel(
                     turn_back(low_rows[:, i], i, 0)
 
         high_rows = {i: keep.tile([P, P, 2], BF16, name="high_rows%d" % i) for i in (1, 2)}
-        high_rows[3] = stage.tile([P, P, 2], BF16, name="high_rows3", offset=2048, align_bytes=64)
+        high_rows[3] = stage.tile([P, P, 2], BF16, name="high_rows3", offset=6144, align_bytes=64)
 
         def high_pairs(blocks):
             sums = [bank(3 + i, [P, 2, P], "high_sum%d" % i) for i in blocks]
@@ -237,7 +236,7 @@ def tile_picked_hop2_relu_p_kernel(
                 direct[2][:, :, part].rearrange("p e v -> p v e"),
                 ALU.add,
             )
-        z_word = stage.tile([P, V], U32, offset=2048, align_bytes=64)
+        z_word = stage.tile([P, V], U32, offset=6144, align_bytes=64)
         z_scale = keep.tile([P, V], U8, align_bytes=64)
         second_product(z_early[:], P, 3 * P, 4)
         second_product(z_direct[:], 0, P, 7, on_vector=True)

@@ -172,16 +172,16 @@ def tile_picked_hop2_relu_p_kernel(
         def copy_out(block, z_block, count):
             nc.scalar.copy(z_block.bitcast(F32)[:, :, :count], back[block][:].rearrange("p u v -> p v u"))
 
-        def second_product(z_grouped, a, b, where, on_vector=False):
+        def second_product(z_grouped, words, a, b, where, on_vector=False):
             nc.vector.quantize_mx(
-                out=z_word[:, a:b].bitcast(FP8X4), scales=z_scale[:, a:b], in_=z_grouped.rearrange("p v t -> p (v t)")
+                out=words.bitcast(FP8X4), scales=z_scale[:, a:b], in_=z_grouped.rearrange("p v t -> p (v t)")
             )
             acc = bank(where, [P, b - a], "g_acc%d" % a)
-            product(acc[:], w2_word_sb[:], w2_scale_sb[:], z_word[:, a:b], z_scale[:, a:b])
+            product(acc[:], w2_word_sb[:], w2_scale_sb[:], words, z_scale[:, a:b])
             relu(g[:, a:b], acc[:], on_vector)
 
         z_direct = keep.tile([P, P, 4], BF16, align_bytes=64)
-        z_early = keep.tile([P, 2 * P, 4], BF16, align_bytes=64)
+        z_early = stage.tile([P, 2 * P, 4], BF16, offset=8192, align_bytes=64)
         z_late = keep.tile([P, P, 4], BF16, align_bytes=64)
         z_blocks = [z_direct[:], z_early[:, :P, :], z_early[:, P:, :], z_late[:]]
 
@@ -204,31 +204,51 @@ def tile_picked_hop2_relu_p_kernel(
         high_rows = {i: keep.tile([P, P, 2], BF16, name="high_rows%d" % i) for i in (1, 2)}
         high_rows[3] = stage.tile([P, P, 2], BF16, name="high_rows3", offset=6144, align_bytes=64)
 
-        def high_pairs(blocks):
-            sums = [bank(3 + i, [P, 2, P], "high_sum%d" % i) for i in blocks]
-            for e in range(2):
-                targets = [acc[:, e, :] for acc in sums]
-                add_terms(2 + e, blocks[0] * P, (blocks[-1] + 1) * P, targets, False)
-            for i, acc in zip(blocks, sums):
-                nc.scalar.activation(high_rows[i][:], acc[:].rearrange("v e p -> v p e"), ACT.Copy)
+        first_terms = keep.tile([P, 2, V], F32)
+        sums = {i: bank(3 + i, [P, 2, P], "high_sum%d" % i) for i in (1, 2, 3)}
+
+        def turn_and_add(i, e, term, start, stop):
+            nc.tensor.matmul(sums[i][:, e, :], term, ident[:], start=start, stop=stop, is_transpose=True)
+
+        def first_term(e):
+            weighted_gather(first_terms[:, e, :], 2 + e, 0, 0, V)
+            for i in (1, 2, 3):
+                turn_and_add(i, e, first_terms[:, e, i * P : (i + 1) * P], e == 0, False)
+
+        def later_terms(e, blocks):
+            a, b = blocks[0] * P, (blocks[-1] + 1) * P
+            for d in (1, 2):
+                term = keep.tile([P, b - a], F32, name="term%d_%d_%d" % (2 + e, d, a))
+                weighted_gather(term[:, :], 2 + e, d, a, b)
+                for n, i in enumerate(blocks):
+                    turn_and_add(i, e, term[:, n * P : (n + 1) * P], False, e == 1 and d == 2)
+
+        def round_and_turn(blocks):
+            for i in blocks:
+                nc.scalar.activation(high_rows[i][:], sums[i][:].rearrange("v e p -> v p e"), ACT.Copy)
                 turn_back(high_rows[i][:], i, 1)
-                copy_out(i, z_blocks[i], 2)
 
         low_pairs(0, 0, BLOCKS)
-        low_pairs(1, 0, BLOCKS - 1)
+        low_pairs(1, 0, BLOCKS)
         copy_out(0, z_blocks[0], 1)
-        high_pairs([1, 2])
-        low_pairs(1, BLOCKS - 1, 1)
-        high_pairs([3])
+        for e in range(2):
+            first_term(e)
+            later_terms(e, [1, 2])
+        round_and_turn([1, 2])
+        for e in range(2):
+            later_terms(e, [3])
+        round_and_turn([3])
+        for i in (1, 2, 3):
+            copy_out(i, z_blocks[i], 2)
 
         halves = (slice(0, P // 2), slice(P // 2, P))
-        direct = [keep.tile([P, 2, P], F32, name="direct%d" % d) for d in range(D)]
-        for d in range(D):
+        direct = {d: keep.tile([P, 2, P], F32, name="direct%d" % d) for d in (1, 2)}
+        for d in (1, 2):
             for e in range(2):
                 weighted_gather(direct[d][:, e, :], 2 + e, d, 0, P)
         two = keep.tile([P, 2, P], F32)
         for part in halves:
-            nc.vector.tensor_tensor(two[:, :, part], direct[0][:, :, part], direct[1][:, :, part], ALU.add)
+            nc.vector.tensor_tensor(two[:, :, part], first_terms[:, :, part], direct[1][:, :, part], ALU.add)
         for part in halves:
             nc.vector.tensor_tensor(
                 z_direct[:, part, 2:],
@@ -236,11 +256,12 @@ def tile_picked_hop2_relu_p_kernel(
                 direct[2][:, :, part].rearrange("p e v -> p v e"),
                 ALU.add,
             )
-        z_word = stage.tile([P, V], U32, offset=6144, align_bytes=64)
+        z_word = stage.tile([P, 3 * P], U32, offset=6144, align_bytes=64)
+        z_word_direct = stage.tile([P, P], U32, offset=8192, align_bytes=64)
         z_scale = keep.tile([P, V], U8, align_bytes=64)
-        second_product(z_early[:], P, 3 * P, 4)
-        second_product(z_direct[:], 0, P, 7, on_vector=True)
-        second_product(z_late[:], 3 * P, V, 5)
+        second_product(z_early[:], z_word[:, : 2 * P], P, 3 * P, 4)
+        second_product(z_direct[:], z_word_direct[:], 0, P, 7)
+        second_product(z_late[:], z_word[:, 2 * P :], 3 * P, V, 5)
 
         halves = (slice(0, U // 2), slice(U // 2, U))
         terms = [keep.tile([P, U], F32, name="root_term%d" % d) for d in range(D)]

@@ -145,7 +145,6 @@ def tile_picked_hop2_relu_p_kernel(
             first_product(j, (0, S // 2), (2 * j + 3) % 6)
             first_product(j, (S // 2, EARLY, S), (2 * j + 4) % 6)
 
-        g = keep.tile([P, V], F32)
 
         def weighted_gather(term, j, d, a, b):
             nc.vector.tensor_tensor(
@@ -180,7 +179,7 @@ def tile_picked_hop2_relu_p_kernel(
             product(acc[:], w2_word_sb[:], w2_scale_sb[:], words, z_scale[:, a:b])
             relu(g[:, a:b], acc[:], on_vector)
 
-        z_direct = keep.tile([P, P, 4], BF16, align_bytes=64)
+        z_direct = stage.tile([P, P, 4], BF16, offset=10240, align_bytes=64)
         z_early = stage.tile([P, 2 * P, 4], BF16, offset=8192, align_bytes=64)
         z_late = keep.tile([P, P, 4], BF16, align_bytes=64)
         z_blocks = [z_direct[:], z_early[:, :P, :], z_early[:, P:, :], z_late[:]]
@@ -204,16 +203,16 @@ def tile_picked_hop2_relu_p_kernel(
         high_rows = {i: keep.tile([P, P, 2], BF16, name="high_rows%d" % i) for i in (1, 2)}
         high_rows[3] = stage.tile([P, P, 2], BF16, name="high_rows3", offset=6144, align_bytes=64)
 
-        first_terms = keep.tile([P, 2, V], F32)
+        first_terms = keep.tile([P, 2, V - P], F32)
         sums = {i: bank(3 + i, [P, 2, P], "high_sum%d" % i) for i in (1, 2, 3)}
 
         def turn_and_add(i, e, term, start, stop):
             nc.tensor.matmul(sums[i][:, e, :], term, ident[:], start=start, stop=stop, is_transpose=True)
 
         def first_term(e):
-            weighted_gather(first_terms[:, e, :], 2 + e, 0, 0, V)
+            weighted_gather(first_terms[:, e, :], 2 + e, 0, P, V)
             for i in (1, 2, 3):
-                turn_and_add(i, e, first_terms[:, e, i * P : (i + 1) * P], e == 0, False)
+                turn_and_add(i, e, first_terms[:, e, (i - 1) * P : i * P], e == 0, False)
 
         def later_terms(e, blocks):
             a, b = blocks[0] * P, (blocks[-1] + 1) * P
@@ -242,13 +241,13 @@ def tile_picked_hop2_relu_p_kernel(
             copy_out(i, z_blocks[i], 2)
 
         halves = (slice(0, P // 2), slice(P // 2, P))
-        direct = {d: keep.tile([P, 2, P], F32, name="direct%d" % d) for d in (1, 2)}
-        for d in (1, 2):
+        direct = [keep.tile([P, 2, P], F32, name="direct%d" % d) for d in range(D)]
+        for d in range(D):
             for e in range(2):
                 weighted_gather(direct[d][:, e, :], 2 + e, d, 0, P)
         two = keep.tile([P, 2, P], F32)
         for part in halves:
-            nc.vector.tensor_tensor(two[:, :, part], first_terms[:, :, part], direct[1][:, :, part], ALU.add)
+            nc.vector.tensor_tensor(two[:, :, part], direct[0][:, :, part], direct[1][:, :, part], ALU.add)
         for part in halves:
             nc.vector.tensor_tensor(
                 z_direct[:, part, 2:],
@@ -259,9 +258,10 @@ def tile_picked_hop2_relu_p_kernel(
         z_word = stage.tile([P, 3 * P], U32, offset=6144, align_bytes=64)
         z_word_direct = stage.tile([P, P], U32, offset=8192, align_bytes=64)
         z_scale = keep.tile([P, V], U8, align_bytes=64)
+        g = stage.tile([P, V], F32, offset=10240, align_bytes=64)
         second_product(z_early[:], z_word[:, : 2 * P], P, 3 * P, 4)
+        second_product(z_late[:], z_word[:, 2 * P :], 3 * P, V, 5, on_vector=True)
         second_product(z_direct[:], z_word_direct[:], 0, P, 7)
-        second_product(z_late[:], z_word[:, 2 * P :], 3 * P, V, 5)
 
         halves = (slice(0, U // 2), slice(U // 2, U))
         terms = [keep.tile([P, U], F32, name="root_term%d" % d) for d in range(D)]

@@ -168,9 +168,6 @@ def tile_picked_hop2_relu_p_kernel(
         def turn_back(rows, block, u):
             nc.tensor.transpose(back[block][:, u, :], rows.rearrange("v p e -> v (p e)").bitcast(F32), ident[:])
 
-        def copy_out(block, z_block, count):
-            nc.scalar.copy(z_block.bitcast(F32)[:, :, :count], back[block][:].rearrange("p u v -> p v u"))
-
         def second_product(z_grouped, words, a, b, where, on_vector=False):
             nc.vector.quantize_mx(
                 out=words.bitcast(FP8X4), scales=z_scale[:, a:b], in_=z_grouped.rearrange("p v t -> p (v t)")
@@ -182,10 +179,12 @@ def tile_picked_hop2_relu_p_kernel(
         z_direct = stage.tile([P, P, 4], BF16, offset=10240, align_bytes=64)
         z_early = stage.tile([P, 2 * P, 4], BF16, offset=8192, align_bytes=64)
         z_late = keep.tile([P, P, 4], BF16, align_bytes=64)
-        z_blocks = [z_direct[:], z_early[:, :P, :], z_early[:, P:, :], z_late[:]]
 
         low_rows = keep.tile([P, BLOCKS, P, 2], BF16)
-        back = [bank(i, [P, 2 if i else 1, P], "back%d" % i) for i in range(BLOCKS)]
+        back_direct = bank(0, [P, 1, P], "back_direct")
+        back_early = bank(1, [P, 2, 2, P], "back_early")
+        back_late = bank(2, [P, 2, P], "back_late")
+        back = [back_direct[:], back_early[:, 0], back_early[:, 1], back_late[:]]
 
         def low_pairs(j, first_block, count):
             acc = bank(6 + j, [P, count, P], "low_sum%d_%d" % (j, first_block))
@@ -200,45 +199,45 @@ def tile_picked_hop2_relu_p_kernel(
                 for i in blocks:
                     turn_back(low_rows[:, i], i, 0)
 
-        high_rows = {i: keep.tile([P, P, 2], BF16, name="high_rows%d" % i) for i in (1, 2)}
-        high_rows[3] = stage.tile([P, P, 2], BF16, name="high_rows3", offset=6144, align_bytes=64)
+        rows_early = keep.tile([P, 2, P, 2], BF16)
+        rows_late = stage.tile([P, P, 2], BF16, offset=6144, align_bytes=64)
+        sum_early = bank(4, [P, 2, 2, P], "sum_early")
+        sum_late = bank(5, [P, 2, P], "sum_late")
+        sums = {1: sum_early[:, 0], 2: sum_early[:, 1], 3: sum_late[:]}
 
-        first_terms = keep.tile([P, 2, V - P], F32)
-        sums = {i: bank(3 + i, [P, 2, P], "high_sum%d" % i) for i in (1, 2, 3)}
-
-        def turn_and_add(i, e, term, start, stop):
-            nc.tensor.matmul(sums[i][:, e, :], term, ident[:], start=start, stop=stop, is_transpose=True)
-
-        def first_term(e):
-            weighted_gather(first_terms[:, e, :], 2 + e, 0, P, V)
-            for i in (1, 2, 3):
-                turn_and_add(i, e, first_terms[:, e, (i - 1) * P : i * P], e == 0, False)
-
-        def later_terms(e, blocks):
+        def high_term(e, d, blocks):
             a, b = blocks[0] * P, (blocks[-1] + 1) * P
-            for d in (1, 2):
-                term = keep.tile([P, b - a], F32, name="term%d_%d_%d" % (2 + e, d, a))
-                weighted_gather(term[:, :], 2 + e, d, a, b)
-                for n, i in enumerate(blocks):
-                    turn_and_add(i, e, term[:, n * P : (n + 1) * P], False, e == 1 and d == 2)
-
-        def round_and_turn(blocks):
-            for i in blocks:
-                nc.scalar.activation(high_rows[i][:], sums[i][:].rearrange("v e p -> v p e"), ACT.Copy)
-                turn_back(high_rows[i][:], i, 1)
+            term = keep.tile([P, b - a], F32, name="term%d_%d_%d" % (2 + e, d, a))
+            weighted_gather(term[:, :], 2 + e, d, a, b)
+            for n, i in enumerate(blocks):
+                nc.tensor.matmul(
+                    sums[i][:, e, :],
+                    term[:, n * P : (n + 1) * P],
+                    ident[:],
+                    start=(e == 0 and d == 0 and i != 2),
+                    stop=(e == 1 and d == D - 1 and i != 1),
+                    is_transpose=True,
+                )
 
         low_pairs(0, 0, BLOCKS)
         low_pairs(1, 0, BLOCKS)
-        copy_out(0, z_blocks[0], 1)
-        for e in range(2):
-            first_term(e)
-            later_terms(e, [1, 2])
-        round_and_turn([1, 2])
-        for e in range(2):
-            later_terms(e, [3])
-        round_and_turn([3])
-        for i in (1, 2, 3):
-            copy_out(i, z_blocks[i], 2)
+        nc.scalar.copy(z_direct[:].bitcast(F32)[:, :, :1], back_direct[:].rearrange("p u v -> p v u"))
+        for d in range(D):
+            high_term(0, d, [1, 2, 3])
+        high_term(1, 0, [1, 2, 3])
+        for d in (1, 2):
+            high_term(1, d, [1, 2])
+        nc.scalar.activation(rows_early[:], sum_early[:].rearrange("v i e p -> v i p e"), ACT.Copy)
+        for i in (1, 2):
+            turn_back(rows_early[:, i - 1], i, 1)
+        for d in (1, 2):
+            high_term(1, d, [3])
+        nc.scalar.activation(rows_late[:], sum_late[:].rearrange("v e p -> v p e"), ACT.Copy)
+        turn_back(rows_late[:], 3, 1)
+        nc.scalar.copy(
+            z_early[:].bitcast(F32).rearrange("p (i v) u -> p i v u", i=2), back_early[:].rearrange("p i u v -> p i v u")
+        )
+        nc.scalar.copy(z_late[:].bitcast(F32), back_late[:].rearrange("p u v -> p v u"))
 
         halves = (slice(0, P // 2), slice(P // 2, P))
         direct = [keep.tile([P, 2, P], F32, name="direct%d" % d) for d in range(D)]
@@ -260,7 +259,7 @@ def tile_picked_hop2_relu_p_kernel(
         z_scale = keep.tile([P, V], U8, align_bytes=64)
         g = stage.tile([P, V], F32, offset=10240, align_bytes=64)
         second_product(z_early[:], z_word[:, : 2 * P], P, 3 * P, 4)
-        second_product(z_late[:], z_word[:, 2 * P :], 3 * P, V, 5, on_vector=True)
+        second_product(z_late[:], z_word[:, 2 * P :], 3 * P, V, 6, on_vector=True)
         second_product(z_direct[:], z_word_direct[:], 0, P, 7)
 
         halves = (slice(0, U // 2), slice(U // 2, U))

@@ -1,7 +1,6 @@
 from contextlib import ExitStack
 
 import concourse.mybir as mybir
-from concourse.masks import make_identity
 
 K, T, S, D, V, H, N, U = 512, 2048, 1024, 3, 512, 512, 128, 256
 P = 128
@@ -21,6 +20,8 @@ TILES = H // P
 BLOCKS = V // P
 BANK = 2048
 EARLY = 768
+ROW_STEP = 9
+GROUP = 60
 
 
 def tile_picked_hop2_relu_p_kernel(
@@ -54,24 +55,19 @@ def tile_picked_hop2_relu_p_kernel(
         def load_w1(a, b):
             raw = keep.tile([P, 4, b - a], F32, name="w1_raw%d" % a)
             nc.sync.dma_start(raw[:], w1_rows[:, :, a:b])
-            return raw[:].rearrange("p t (q u e) -> p u q t e", u=2, e=2)
-
-        def load_gate(d):
-            tile = keep.tile([P, V], F32, name="gate_sb%d" % d)
-            nc.sync.dma_start(tile[:], gate[d])
-            return tile
+            return raw[:].rearrange("p t (q c) -> p q t c", c=4)
 
         offs_sb = load_list(offs, "offs_sb")
         x_scale_table = keep.tile([P, T], U8, align_bytes=64)
         nc.vector.memset(x_scale_table[:].bitcast(I32), 0)
         load_scale_rows(x_scale_table, x_scales, (nc.sync, nc.scalar, nc.sync, nc.scalar))
-        pos_sb = [load_list(pos1, "pos_sb0"), load_list(pos2, "pos_sb1")]
-        x_word_table = keep.tile([P, T], I32, align_bytes=64)
+        gate_rows = keep.tile([P, P], F32)
+        nc.sync.dma_start(gate_rows[:], gate.rearrange("d r (i c) -> (d r i) c", c=P)[0 : ROW_STEP * P : ROW_STEP, :])
+        pos_sb = [load_list(pos1, "pos_sb0")]
+        x_word_table = stage.tile([P, T], I32, offset=4096, align_bytes=64)
         load_words(x_word_table, x_words)
         w1_raw = [load_w1(0, H // 2), load_w1(H // 2, H)]
-        gate_sb = [load_gate(0)]
-        pos_sb.append(load_list(pos3, "pos_sb2"))
-        gate_sb.extend([load_gate(1), load_gate(2)])
+        pos_sb.extend([load_list(pos2, "pos_sb1"), load_list(pos3, "pos_sb2")])
         w2_word_sb = keep.tile([P, N], I32, align_bytes=64)
         load_words(w2_word_sb, w2_words)
         w2_scale_sb = keep.tile([P, N], U8, align_bytes=64)
@@ -82,7 +78,54 @@ def tile_picked_hop2_relu_p_kernel(
         nc.sync.dma_start(gate2_sb[:], gate2.rearrange("d p r -> p d r"))
 
         ident = keep.tile([P, P], F32)
-        make_identity(nc, ident[:])
+        nc.gpsimd.memset(ident[:], 0.0)
+        ones = keep.tile([P, 32], F32)
+        nc.gpsimd.memset(ones[:], 1.0)
+        count = keep.tile([P, 32], F32, align_bytes=64)
+        nc.vector.tensor_tensor_scan(count[:], ones[:], ones[:], 0.0, ALU.mult, ALU.add)
+        count_turned = keep.tile([P, 32], F32, align_bytes=64)
+        nc.vector.transpose(count_turned[:], count[:])
+        for q in range(4):
+            quad = slice(32 * q, 32 * (q + 1))
+            nc.vector.tensor_tensor(ident[quad, quad], count[quad, :], count_turned[quad, :], ALU.is_equal)
+        half = keep.tile([P, 1], F32)
+        nc.gpsimd.memset(half[:], 0.5)
+
+        gate_turned = bank(5, [P, D, GROUP], "gate_turned")
+        nc.tensor.transpose(gate_turned[:].rearrange("v d k -> v (d k)")[:, :P], gate_rows[:], ident[:])
+        gate_col = keep.tile([P, D, BLOCKS], F32)
+        nc.scalar.activation(gate_col[:], gate_turned[:, :, :BLOCKS], ACT.Copy)
+        small = keep.tile([P, BLOCKS, 2], F32)
+        both = keep.tile([P, BLOCKS], F32)
+        for i in range(BLOCKS):
+            nc.scalar.activation(
+                small[:, i, :], gate_turned[:, :2, i], ACT.Abs, scale=2.0**-48, accum_out=both[:, i : i + 1]
+            )
+        sign3 = keep.tile([P, BLOCKS], F32)
+        nc.scalar.activation(sign3[:], gate_turned[:, 2, :BLOCKS], ACT.Sign)
+        least = keep.tile([P, BLOCKS], F32)
+        nc.scalar.activation(least[:], both[:], ACT.Copy, bias=2.0**-100)
+        side = stage.tile([P, BLOCKS], F32, offset=3072)
+        nc.scalar.activation(side[:], sign3[:], ACT.Sign, bias=half[:])
+        factor = keep.tile([P, BLOCKS], F32)
+        for i in range(BLOCKS):
+            col = slice(i, i + 1)
+            nc.scalar.activation(factor[:, col], side[:, col], ACT.Identity, scale=least[:, col], bias=gate_col[:, 2, col])
+        inverse = keep.tile([P, BLOCKS], F32)
+        nc.vector.reciprocal(inverse[:], factor[:])
+        ratio_col = [keep.tile([P, 2], F32, name="ratio_col%d" % i) for i in range(BLOCKS)]
+        ratio = [keep.tile([P, V], F32, name="ratio0"), stage.tile([P, V], F32, name="ratio1", offset=1024)]
+        for i in range(BLOCKS):
+            nc.scalar.activation(ratio_col[i][:], gate_col[:, :2, i], ACT.Copy, scale=inverse[:, i : i + 1])
+        spread = [bank(6 + d, [P, BLOCKS, P], "spread%d" % d) for d in range(2)]
+        for d in range(2):
+            for i in range(BLOCKS):
+                nc.tensor.transpose(spread[d][:, i, :], ratio_col[i][:, d : d + 1].to_broadcast([P, P]), ident[:])
+
+        def copy_ratio(d):
+            nc.scalar.activation(ratio[d][:], spread[d][:].rearrange("p i v -> p (i v)"), ACT.Copy)
+
+        copy_ratio(0)
 
         w1_word = keep.tile([P, H], U32, align_bytes=64)
         w1_scale = keep.tile([P, H], U8, align_bytes=64)
@@ -91,7 +134,10 @@ def tile_picked_hop2_relu_p_kernel(
             cols = slice(first, first + grouped.shape[1] // 4)
             nc.vector.quantize_mx(out=w1_word[:, cols].bitcast(FP8X4), scales=w1_scale[:, cols], in_=grouped)
 
-        x_scale = keep.tile([P, S], U8, align_bytes=64)
+        x_scale = [
+            keep.tile([P, S // 2], U8, name="x_scale0", align_bytes=64),
+            stage.tile([P, S // 2], U8, name="x_scale1", offset=3072, align_bytes=64),
+        ]
         h = [keep.tile([P, S], F32, name="h%d" % j) for j in range(TILES)]
         x_early = keep.tile([P, EARLY], U32, align_bytes=64)
 
@@ -115,157 +161,140 @@ def tile_picked_hop2_relu_p_kernel(
             else:
                 nc.scalar.activation(dst, acc, ACT.Relu)
 
-        def first_product(j, edges, where, on_vector=False):
+        def first_product(j, edges, where):
             a, b = edges[0], edges[-1]
             acc = bank(where, [P, b - a], "h_acc%d_%d" % (j, a))
-            cols = slice(j * P, (j + 1) * P)
+            place = 2 * (j % 2) + j // 2
+            cols = slice(place * P, (place + 1) * P)
             for lo, hi in zip(edges, edges[1:]):
                 words = x_early[:, lo:hi] if lo < EARLY else x_late[:, lo - EARLY : hi - EARLY]
-                product(acc[:, lo - a : hi - a], w1_word[:, cols], w1_scale[:, cols], words, x_scale[:, lo:hi])
-            relu(h[j][:, a:b], acc[:], on_vector)
+                scales = x_scale[lo // (S // 2)][:, lo % (S // 2) : (hi - 1) % (S // 2) + 1]
+                product(acc[:, lo - a : hi - a], w1_word[:, cols], w1_scale[:, cols], words, scales)
+            return h[j][:, a:b], acc[:]
 
-        nc.vector.tensor_copy(x_scale[:], x_scale_table[:].indirect(offs_sb[:]))
+        for n in range(2):
+            nc.vector.tensor_copy(x_scale[n][:], x_scale_table[:].indirect(offs_sb[:, 32 * n : 32 * (n + 1)]))
         gather_words(x_early[:], 0, EARLY)
-        first = stage.tile([P, P * 4], BF16, offset=512, align_bytes=64)
-        nc.scalar.activation(first[:].rearrange("p (q e t) -> p q t e", e=2, t=4), w1_raw[0][:, 0], ACT.Copy)
-        quantize_w1(first[:], 0)
-        planes = stage.tile([P, 4, 2, 64, 4], BF16, offset=1024, align_bytes=64)
-        nc.scalar.activation(planes[:, 2:, 0].rearrange("p e q t -> p q t e"), w1_raw[0][:, 1], ACT.Copy)
+        first = stage.tile([P, 2, 64, 4], BF16, offset=512, align_bytes=64)
+        nc.scalar.activation(first[:].rearrange("p c q t -> p q t c"), w1_raw[0][:, :, :, :2], ACT.Copy)
+        quantize_w1(first[:].rearrange("p c q t -> p (c q t)"), 0)
+        second = keep.tile([P, 2, 64, 4], BF16, align_bytes=64)
+        nc.scalar.activation(second[:].rearrange("p c q t -> p q t c"), w1_raw[0][:, :, :, 2:], ACT.Copy)
+        copy_ratio(1)
         x_late = stage.tile([P, S - EARLY], U32, offset=0, align_bytes=64)
         for i in range(3):
-            first_product(0, (256 * i, 256 * (i + 1)), i)
+            relu(*first_product(0, (256 * i, 256 * (i + 1)), i), False)
         gather_words(x_late[:], EARLY, S)
-        first_product(0, (EARLY, EARLY + P), 3, on_vector=True)
-        first_product(0, (EARLY + P, S), 4)
-        nc.vector.tensor_copy(planes[:, :, 1].rearrange("p c q t -> p q t c"), w1_raw[1].rearrange("p u q t e -> p q t (u e)"))
-        for e in range(2):
-            quantize_w1(planes[:, e, 1].rearrange("p q t -> p (q t)"), P + 64 * e)
-        quantize_w1(planes[:, 2:].rearrange("p c half q t -> p (c half q t)"), 2 * P)
-        for j in range(1, TILES):
-            first_product(j, (0, S // 2), (2 * j + 3) % 6)
-            first_product(j, (S // 2, EARLY, S), (2 * j + 4) % 6)
+        relu(*first_product(0, (EARLY, EARLY + P), 3), True)
+        relu(*first_product(0, (EARLY + P, S), 4), False)
+        rest = stage.tile([P, 4, 64, 4], BF16, offset=4096, align_bytes=64)
+        nc.vector.tensor_copy(rest[:].rearrange("p c q t -> p q t c"), w1_raw[1])
+        quantize_w1(second[:].rearrange("p c q t -> p (c q t)"), P)
+        quantize_w1(rest[:].rearrange("p c q t -> p (c q t)"), 2 * P)
+        waiting = {
+            j: [first_product(j, (0, S // 2), (2 * j + 3) % 6), first_product(j, (S // 2, EARLY, S), (2 * j + 4) % 6)]
+            for j in range(1, TILES)
+        }
 
+        def finish(j):
+            for dst, acc in waiting[j]:
+                relu(dst, acc, False)
 
-        def weighted_gather(term, j, d, a, b):
-            nc.vector.tensor_tensor(
-                term, h[j][:].indirect(pos_sb[d][:, a // 16 : b // 16]), gate_sb[d][:, a:b], ALU.mult
-            )
+        low_sum = [bank(6 + n, [P, 2, 2, P], "low_sum%d" % n) for n in range(2)]
+        high_pair = bank(5, [P, 2, 2, P], "high_pair")
+        high_one = [bank(n, [P, 2, P], "high_one%d" % n) for n in range(2)]
+        sums = [
+            [low_sum[0][:, 0], low_sum[0][:, 1], low_sum[1][:, 0], low_sum[1][:, 1]],
+            [high_pair[:, 0], high_pair[:, 1], high_one[0][:], high_one[1][:]],
+        ]
+        group = [[0, 0, 1, 1], [2, 2, 3, 4]]
+        left = [12, 12, 12, 6, 6]
+        size = list(left)
 
-        def add_terms(j, a, b, targets, one_bank):
-            for d in range(D):
-                term = keep.tile([P, b - a], F32, name="term%d_%d_%d" % (j, d, a))
-                weighted_gather(term[:, :], j, d, a, b)
-                for i, target in enumerate(targets):
-                    nc.tensor.matmul(
-                        target,
-                        term[:, i * P : (i + 1) * P],
-                        ident[:],
-                        start=(d == 0 and (i == 0 or not one_bank)),
-                        stop=(d == D - 1 and (i == len(targets) - 1 or not one_bank)),
-                        is_transpose=True,
-                    )
-
-        def turn_back(rows, block, u):
-            nc.tensor.transpose(back[block][:, u, :], rows.rearrange("v p e -> v (p e)").bitcast(F32), ident[:])
-
-        def second_product(z_grouped, words, a, b, where, on_vector=False):
-            nc.vector.quantize_mx(
-                out=words.bitcast(FP8X4), scales=z_scale[:, a:b], in_=z_grouped.rearrange("p v t -> p (v t)")
-            )
-            acc = bank(where, [P, b - a], "g_acc%d" % a)
-            product(acc[:], w2_word_sb[:], w2_scale_sb[:], words, z_scale[:, a:b])
-            relu(g[:, a:b], acc[:], on_vector)
-
-        z_direct = stage.tile([P, P, 4], BF16, offset=10240, align_bytes=64)
-        z_early = stage.tile([P, 2 * P, 4], BF16, offset=8192, align_bytes=64)
-        z_late = keep.tile([P, P, 4], BF16, align_bytes=64)
-
-        low_rows = keep.tile([P, BLOCKS, P, 2], BF16)
-        back_direct = bank(0, [P, 1, P], "back_direct")
-        back_early = bank(1, [P, 2, 2, P], "back_early")
-        back_late = bank(2, [P, 2, P], "back_late")
-        back = [back_direct[:], back_early[:, 0], back_early[:, 1], back_late[:]]
-
-        def low_pairs(j, first_block, count):
-            acc = bank(6 + j, [P, count, P], "low_sum%d_%d" % (j, first_block))
-            blocks = range(first_block, first_block + count)
-            add_terms(j, blocks[0] * P, (blocks[-1] + 1) * P, [acc[:, i, :] for i in range(count)], True)
-            nc.scalar.activation(
-                low_rows[:, first_block : first_block + count, 64 * j : 64 * (j + 1), :],
-                acc[:].rearrange("v i (e q) -> v i q e" if j else "v i (q e) -> v i q e", e=2),
-                ACT.Copy,
-            )
-            if j == 1:
-                for i in blocks:
-                    turn_back(low_rows[:, i], i, 0)
-
-        rows_early = keep.tile([P, 2, P, 2], BF16)
-        rows_late = stage.tile([P, P, 2], BF16, offset=6144, align_bytes=64)
-        sum_early = bank(4, [P, 2, 2, P], "sum_early")
-        sum_late = bank(5, [P, 2, P], "sum_late")
-        sums = {1: sum_early[:, 0], 2: sum_early[:, 1], 3: sum_late[:]}
-
-        def high_term(e, d, blocks):
-            a, b = blocks[0] * P, (blocks[-1] + 1) * P
-            term = keep.tile([P, b - a], F32, name="term%d_%d_%d" % (2 + e, d, a))
-            weighted_gather(term[:, :], 2 + e, d, a, b)
-            for n, i in enumerate(blocks):
+        def term(j, d, a, b):
+            if (j, d) == (0, 0):
+                values = stage.tile([P, b - a], F32, name="term_first", offset=4096)
+            else:
+                values = keep.tile([P, b - a], F32, name="term%d_%d_%d" % (j, d, a))
+            window = h[j][:].indirect(pos_sb[d][:, a // 16 : b // 16])
+            if d == 2:
+                nc.scalar.activation(values[:], window, ACT.Copy)
+            else:
+                nc.vector.tensor_tensor(values[:], window, ratio[d][:, a:b], ALU.mult)
+            for i in range(a // P, b // P):
+                n = group[j // 2][i]
                 nc.tensor.matmul(
-                    sums[i][:, e, :],
-                    term[:, n * P : (n + 1) * P],
+                    sums[j // 2][i][:, j % 2, :],
+                    values[:, i * P - a : (i + 1) * P - a],
                     ident[:],
-                    start=(e == 0 and d == 0 and i != 2),
-                    stop=(e == 1 and d == D - 1 and i != 1),
+                    start=(left[n] == size[n]),
+                    stop=(left[n] == 1),
                     is_transpose=True,
                 )
+                left[n] = left[n] - 1
 
-        low_pairs(0, 0, BLOCKS)
-        low_pairs(1, 0, BLOCKS)
-        nc.scalar.copy(z_direct[:].bitcast(F32)[:, :, :1], back_direct[:].rearrange("p u v -> p v u"))
-        for d in range(D):
-            high_term(0, d, [1, 2, 3])
-        high_term(1, 0, [1, 2, 3])
-        for d in (1, 2):
-            high_term(1, d, [1, 2])
-        nc.scalar.activation(rows_early[:], sum_early[:].rearrange("v i e p -> v i p e"), ACT.Copy)
-        for i in (1, 2):
-            turn_back(rows_early[:, i - 1], i, 1)
-        for d in (1, 2):
-            high_term(1, d, [3])
-        nc.scalar.activation(rows_late[:], sum_late[:].rearrange("v e p -> v p e"), ACT.Copy)
-        turn_back(rows_late[:], 3, 1)
-        nc.scalar.copy(
-            z_early[:].bitcast(F32).rearrange("p (i v) u -> p i v u", i=2), back_early[:].rearrange("p i u v -> p i v u")
-        )
-        nc.scalar.copy(z_late[:].bitcast(F32), back_late[:].rearrange("p u v -> p v u"))
+        rows = keep.tile([P, 2, BLOCKS, P, 2], BF16)
+        back_pair = bank(2, [P, 2, 2, P], "back_pair")
+        back_one = [bank(3 + n, [P, 2, P], "back_one%d" % n) for n in range(2)]
+        back = [back_pair[:, 0], back_pair[:, 1], back_one[0][:], back_one[1][:]]
 
-        halves = (slice(0, P // 2), slice(P // 2, P))
-        direct = [keep.tile([P, 2, P], F32, name="direct%d" % d) for d in range(D)]
-        for d in range(D):
-            for e in range(2):
-                weighted_gather(direct[d][:, e, :], 2 + e, d, 0, P)
-        two = keep.tile([P, 2, P], F32)
-        for part in halves:
-            nc.vector.tensor_tensor(two[:, :, part], direct[0][:, :, part], direct[1][:, :, part], ALU.add)
-        for part in halves:
-            nc.vector.tensor_tensor(
-                z_direct[:, part, 2:],
-                two[:, :, part].rearrange("p e v -> p v e"),
-                direct[2][:, :, part].rearrange("p e v -> p v e"),
-                ALU.add,
-            )
-        z_word = stage.tile([P, 3 * P], U32, offset=6144, align_bytes=64)
-        z_word_direct = stage.tile([P, P], U32, offset=8192, align_bytes=64)
+        def round_and_turn(u, i, on_vector=False):
+            dst = rows[:, u, i].rearrange("v (j q) e -> v j q e", j=2)
+            src = sums[u][i].rearrange("v j (e q) -> v j q e", e=2)
+            if on_vector:
+                nc.vector.tensor_scalar(dst, src, factor[:, i : i + 1], None, ALU.mult)
+            else:
+                nc.scalar.activation(dst, src, ACT.Copy, scale=factor[:, i : i + 1])
+            nc.tensor.transpose(back[i][:, u, :], rows[:, u, i].rearrange("v p e -> v (p e)").bitcast(F32), ident[:])
+
+        term(0, 0, 0, V)
+        term(0, 1, 0, V)
+        finish(1)
+        term(0, 2, 0, V)
+        term(1, 0, 0, V)
+        term(1, 1, 0, V)
+        finish(2)
+        term(1, 2, 0, V)
+        term(2, 0, 0, V)
+        term(2, 1, 0, V)
+        term(2, 2, 0, V)
+        finish(3)
+        term(3, 0, 0, V // 2)
+        term(3, 2, 0, V)
+        term(3, 1, 0, V // 2)
+        term(3, 0, V // 2, V)
+        term(3, 1, V // 2, V)
+        for i in range(BLOCKS):
+            round_and_turn(0, i)
+        for i in range(BLOCKS):
+            round_and_turn(1, i, on_vector=(i == 3))
+
+        z = [keep.tile([P, P, 4], BF16, name="z%d" % i, align_bytes=64) for i in range(BLOCKS)]
+        z_word = keep.tile([P, V], U32, align_bytes=64)
         z_scale = keep.tile([P, V], U8, align_bytes=64)
-        g = stage.tile([P, V], F32, offset=10240, align_bytes=64)
-        second_product(z_early[:], z_word[:, : 2 * P], P, 3 * P, 4)
-        second_product(z_late[:], z_word[:, 2 * P :], 3 * P, V, 6, on_vector=True)
-        second_product(z_direct[:], z_word_direct[:], 0, P, 7)
+        g = keep.tile([P, V], F32)
+        for i in range(BLOCKS):
+            src = back[i].rearrange("p u v -> p v u")
+            if i % 2:
+                nc.scalar.copy(z[i][:].bitcast(F32), src)
+            else:
+                nc.vector.tensor_copy(z[i][:].bitcast(F32), src)
+        for i in range(BLOCKS):
+            cols = slice(i * P, (i + 1) * P)
+            nc.vector.quantize_mx(
+                out=z_word[:, cols].bitcast(FP8X4), scales=z_scale[:, cols], in_=z[i][:].rearrange("p v t -> p (v t)")
+            )
+            acc = bank((6, 7, 5, 0)[i], [P, P], "g_acc%d" % i)
+            product(acc[:], w2_word_sb[:], w2_scale_sb[:], z_word[:, cols], z_scale[:, cols])
+            relu(g[:, cols], acc[:], False)
 
         halves = (slice(0, U // 2), slice(U // 2, U))
         terms = [keep.tile([P, U], F32, name="root_term%d" % d) for d in range(D)]
-        for d in range(D):
+        plain = keep.tile([P, U], F32)
+        nc.scalar.activation(plain[:], g[:].indirect(nxt_sb[2][:]), ACT.Copy)
+        for d in range(2):
             nc.vector.tensor_tensor(terms[d][:], g[:].indirect(nxt_sb[d][:]), gate2_sb[:, d, :], ALU.mult)
+        nc.vector.tensor_tensor(terms[2][:], plain[:], gate2_sb[:, 2, :], ALU.mult)
         partial = keep.tile([P, U], F32)
         for part in halves:
             nc.vector.tensor_tensor(partial[:, part], terms[0][:, part], terms[1][:, part], ALU.add)

@@ -105,7 +105,7 @@ def tile_picked_hop2_relu_p_kernel(
         nc.scalar.activation(sign3[:], gate_turned[:, 2, :BLOCKS], ACT.Sign)
         least = keep.tile([P, BLOCKS], F32)
         nc.scalar.activation(least[:], both[:], ACT.Copy, bias=2.0**-100)
-        side = stage.tile([P, BLOCKS], F32, offset=3072)
+        side = keep.tile([P, BLOCKS], F32)
         nc.scalar.activation(side[:], sign3[:], ACT.Sign, bias=half[:])
         factor = keep.tile([P, BLOCKS], F32)
         for i in range(BLOCKS):
@@ -114,7 +114,7 @@ def tile_picked_hop2_relu_p_kernel(
         inverse = keep.tile([P, BLOCKS], F32)
         nc.vector.reciprocal(inverse[:], factor[:])
         ratio_col = [keep.tile([P, 2], F32, name="ratio_col%d" % i) for i in range(BLOCKS)]
-        ratio = [keep.tile([P, V], F32, name="ratio0"), stage.tile([P, V], F32, name="ratio1", offset=1024)]
+        ratio = [stage.tile([P, V], F32, name="ratio%d" % d, offset=(1024, 7168)[d]) for d in range(2)]
         for i in range(BLOCKS):
             nc.scalar.activation(ratio_col[i][:], gate_col[:, :2, i], ACT.Copy, scale=inverse[:, i : i + 1])
         spread = [bank(6 + d, [P, BLOCKS, P], "spread%d" % d) for d in range(2)]
@@ -125,8 +125,6 @@ def tile_picked_hop2_relu_p_kernel(
         def copy_ratio(d):
             nc.scalar.activation(ratio[d][:], spread[d][:].rearrange("p i v -> p (i v)"), ACT.Copy)
 
-        copy_ratio(0)
-
         w1_word = keep.tile([P, H], U32, align_bytes=64)
         w1_scale = keep.tile([P, H], U8, align_bytes=64)
 
@@ -134,10 +132,7 @@ def tile_picked_hop2_relu_p_kernel(
             cols = slice(first, first + grouped.shape[1] // 4)
             nc.vector.quantize_mx(out=w1_word[:, cols].bitcast(FP8X4), scales=w1_scale[:, cols], in_=grouped)
 
-        x_scale = [
-            keep.tile([P, S // 2], U8, name="x_scale0", align_bytes=64),
-            stage.tile([P, S // 2], U8, name="x_scale1", offset=3072, align_bytes=64),
-        ]
+        x_scale = keep.tile([P, S], U8, align_bytes=64)
         h = [keep.tile([P, S], F32, name="h%d" % j) for j in range(TILES)]
         x_early = keep.tile([P, EARLY], U32, align_bytes=64)
 
@@ -168,29 +163,28 @@ def tile_picked_hop2_relu_p_kernel(
             cols = slice(place * P, (place + 1) * P)
             for lo, hi in zip(edges, edges[1:]):
                 words = x_early[:, lo:hi] if lo < EARLY else x_late[:, lo - EARLY : hi - EARLY]
-                scales = x_scale[lo // (S // 2)][:, lo % (S // 2) : (hi - 1) % (S // 2) + 1]
-                product(acc[:, lo - a : hi - a], w1_word[:, cols], w1_scale[:, cols], words, scales)
+                product(acc[:, lo - a : hi - a], w1_word[:, cols], w1_scale[:, cols], words, x_scale[:, lo:hi])
             return h[j][:, a:b], acc[:]
 
-        for n in range(2):
-            nc.vector.tensor_copy(x_scale[n][:], x_scale_table[:].indirect(offs_sb[:, 32 * n : 32 * (n + 1)]))
+        nc.vector.tensor_copy(x_scale[:], x_scale_table[:].indirect(offs_sb[:]))
         gather_words(x_early[:], 0, EARLY)
         first = stage.tile([P, 2, 64, 4], BF16, offset=512, align_bytes=64)
         nc.scalar.activation(first[:].rearrange("p c q t -> p q t c"), w1_raw[0][:, :, :, :2], ACT.Copy)
         quantize_w1(first[:].rearrange("p c q t -> p (c q t)"), 0)
         second = keep.tile([P, 2, 64, 4], BF16, align_bytes=64)
         nc.scalar.activation(second[:].rearrange("p c q t -> p q t c"), w1_raw[0][:, :, :, 2:], ACT.Copy)
-        copy_ratio(1)
+        copy_ratio(0)
         x_late = stage.tile([P, S - EARLY], U32, offset=0, align_bytes=64)
         for i in range(3):
             relu(*first_product(0, (256 * i, 256 * (i + 1)), i), False)
         gather_words(x_late[:], EARLY, S)
         relu(*first_product(0, (EARLY, EARLY + P), 3), True)
         relu(*first_product(0, (EARLY + P, S), 4), False)
-        rest = stage.tile([P, 4, 64, 4], BF16, offset=4096, align_bytes=64)
+        rest = stage.tile([P, 4, 64, 4], BF16, offset=6144, align_bytes=64)
         nc.vector.tensor_copy(rest[:].rearrange("p c q t -> p q t c"), w1_raw[1])
         quantize_w1(second[:].rearrange("p c q t -> p (c q t)"), P)
         quantize_w1(rest[:].rearrange("p c q t -> p (c q t)"), 2 * P)
+        copy_ratio(1)
         waiting = {
             j: [first_product(j, (0, S // 2), (2 * j + 3) % 6), first_product(j, (S // 2, EARLY, S), (2 * j + 4) % 6)]
             for j in range(1, TILES)
@@ -213,7 +207,7 @@ def tile_picked_hop2_relu_p_kernel(
 
         def term(j, d, a, b):
             if (j, d) == (0, 0):
-                values = stage.tile([P, b - a], F32, name="term_first", offset=4096)
+                values = stage.tile([P, b - a], F32, name="term_first", offset=5120)
             else:
                 values = keep.tile([P, b - a], F32, name="term%d_%d_%d" % (j, d, a))
             window = h[j][:].indirect(pos_sb[d][:, a // 16 : b // 16])
@@ -257,17 +251,14 @@ def tile_picked_hop2_relu_p_kernel(
         term(1, 2, 0, V)
         term(2, 0, 0, V)
         term(2, 1, 0, V)
-        term(2, 2, 0, V)
         finish(3)
-        term(3, 0, 0, V // 2)
-        term(3, 2, 0, V)
-        term(3, 1, 0, V // 2)
-        term(3, 0, V // 2, V)
-        term(3, 1, V // 2, V)
-        for i in range(BLOCKS):
-            round_and_turn(0, i)
-        for i in range(BLOCKS):
-            round_and_turn(1, i, on_vector=(i == 3))
+        for a in (0, V // 2):
+            for d in range(2):
+                term(2 + d, 2, a, a + V // 2)
+                term(3, d, a, a + V // 2)
+        for u in range(2):
+            for i in range(BLOCKS):
+                round_and_turn(u, i, on_vector=(u == 1))
 
         z = [keep.tile([P, P, 4], BF16, name="z%d" % i, align_bytes=64) for i in range(BLOCKS)]
         z_word = keep.tile([P, V], U32, align_bytes=64)
@@ -275,10 +266,7 @@ def tile_picked_hop2_relu_p_kernel(
         g = keep.tile([P, V], F32)
         for i in range(BLOCKS):
             src = back[i].rearrange("p u v -> p v u")
-            if i % 2:
-                nc.scalar.copy(z[i][:].bitcast(F32), src)
-            else:
-                nc.vector.tensor_copy(z[i][:].bitcast(F32), src)
+            nc.scalar.copy(z[i][:].bitcast(F32), src)
         for i in range(BLOCKS):
             cols = slice(i * P, (i + 1) * P)
             nc.vector.quantize_mx(

@@ -19,7 +19,6 @@ ACT = mybir.ActivationFunctionType
 TILES = H // P
 BLOCKS = V // P
 BANK = 2048
-EARLY = 768
 ROW_STEP = 9
 GROUP = 60
 
@@ -53,7 +52,7 @@ def tile_picked_hop2_relu_p_kernel(
         w1_rows = w1.rearrange("(p t) c -> p t c", t=4)
 
         def load_w1(a, b):
-            raw = keep.tile([P, 4, b - a], F32, name="w1_raw%d" % a)
+            raw = stage.tile([P, 4, b - a], F32, name="w1_raw%d" % a, offset=16 * a)
             nc.sync.dma_start(raw[:], w1_rows[:, :, a:b])
             return raw[:].rearrange("p t (q c) -> p q t c", c=4)
 
@@ -64,7 +63,7 @@ def tile_picked_hop2_relu_p_kernel(
         gate_rows = keep.tile([P, P], F32)
         nc.sync.dma_start(gate_rows[:], gate.rearrange("d r (i c) -> (d r i) c", c=P)[0 : ROW_STEP * P : ROW_STEP, :])
         pos_sb = [load_list(pos1, "pos_sb0")]
-        x_word_table = stage.tile([P, T], I32, offset=4096, align_bytes=64)
+        x_word_table = keep.tile([P, T], I32, align_bytes=64)
         load_words(x_word_table, x_words)
         w1_raw = [load_w1(0, H // 2), load_w1(H // 2, H)]
         pos_sb.extend([load_list(pos2, "pos_sb1"), load_list(pos3, "pos_sb2")])
@@ -73,6 +72,8 @@ def tile_picked_hop2_relu_p_kernel(
         w2_scale_sb = keep.tile([P, N], U8, align_bytes=64)
         nc.vector.memset(w2_scale_sb[:].bitcast(I32), 0)
         load_scale_rows(w2_scale_sb, w2_scales, (nc.sync,) * 4)
+        gate_direct = keep.tile([P, D, P], F32)
+        nc.sync.dma_start(gate_direct[:], gate.rearrange("d p v -> p d v")[:, :, :P])
         nxt_sb = [load_list(src, "nxt_sb%d" % d) for d, src in enumerate((nxt1, nxt2, nxt3))]
         gate2_sb = keep.tile([P, D, U], F32)
         nc.sync.dma_start(gate2_sb[:], gate2.rearrange("d p r -> p d r"))
@@ -114,7 +115,7 @@ def tile_picked_hop2_relu_p_kernel(
         inverse = keep.tile([P, BLOCKS], F32)
         nc.vector.reciprocal(inverse[:], factor[:])
         ratio_col = [keep.tile([P, 2], F32, name="ratio_col%d" % i) for i in range(BLOCKS)]
-        ratio = [stage.tile([P, V], F32, name="ratio%d" % d, offset=(1024, 7168)[d]) for d in range(2)]
+        ratio = [stage.tile([P, V], F32, name="ratio%d" % d, offset=2048 * d) for d in range(2)]
         for i in range(BLOCKS):
             nc.scalar.activation(ratio_col[i][:], gate_col[:, :2, i], ACT.Copy, scale=inverse[:, i : i + 1])
         spread = [bank(6 + d, [P, BLOCKS, P], "spread%d" % d) for d in range(2)]
@@ -134,10 +135,7 @@ def tile_picked_hop2_relu_p_kernel(
 
         x_scale = keep.tile([P, S], U8, align_bytes=64)
         h = [keep.tile([P, S], F32, name="h%d" % j) for j in range(TILES)]
-        x_early = keep.tile([P, EARLY], U32, align_bytes=64)
-
-        def gather_words(words, a, b):
-            nc.vector.tensor_copy(words, x_word_table[:].bitcast(U32).indirect(offs_sb[:, a // 16 : b // 16]))
+        x_word = keep.tile([P, S], U32, align_bytes=64)
 
         def product(acc, lhs_word, lhs_scale, rhs_word, rhs_scale):
             nc.tensor.matmul_mx(
@@ -156,37 +154,30 @@ def tile_picked_hop2_relu_p_kernel(
             else:
                 nc.scalar.activation(dst, acc, ACT.Relu)
 
-        def first_product(j, edges, where):
-            a, b = edges[0], edges[-1]
+        def first_product(j, a, b, where):
             acc = bank(where, [P, b - a], "h_acc%d_%d" % (j, a))
-            place = 2 * (j % 2) + j // 2
-            cols = slice(place * P, (place + 1) * P)
-            for lo, hi in zip(edges, edges[1:]):
-                words = x_early[:, lo:hi] if lo < EARLY else x_late[:, lo - EARLY : hi - EARLY]
-                product(acc[:, lo - a : hi - a], w1_word[:, cols], w1_scale[:, cols], words, x_scale[:, lo:hi])
+            cols = slice(j * P, (j + 1) * P)
+            product(acc[:], w1_word[:, cols], w1_scale[:, cols], x_word[:, a:b], x_scale[:, a:b])
             return h[j][:, a:b], acc[:]
 
         nc.vector.tensor_copy(x_scale[:], x_scale_table[:].indirect(offs_sb[:]))
-        gather_words(x_early[:], 0, EARLY)
-        first = stage.tile([P, 2, 64, 4], BF16, offset=512, align_bytes=64)
-        nc.scalar.activation(first[:].rearrange("p c q t -> p q t c"), w1_raw[0][:, :, :, :2], ACT.Copy)
-        quantize_w1(first[:].rearrange("p c q t -> p (c q t)"), 0)
-        second = keep.tile([P, 2, 64, 4], BF16, align_bytes=64)
-        nc.scalar.activation(second[:].rearrange("p c q t -> p q t c"), w1_raw[0][:, :, :, 2:], ACT.Copy)
+        nc.vector.tensor_copy(x_word[:], x_word_table[:].bitcast(U32).indirect(offs_sb[:]))
+        grouped = stage.tile([P, 2048], BF16, offset=8192, align_bytes=64)
+        planes = grouped[:].rearrange("p (c half q t) -> p c half q t", c=4, half=2, t=4)
+        first = grouped[:, 256:768]
+        nc.scalar.activation(first.rearrange("p (c q t) -> p q t c", c=2, t=4), w1_raw[0][:, :, :, :2], ACT.Copy)
+        quantize_w1(first, 0)
+        nc.scalar.activation(planes[:, 2:, 0].rearrange("p c q t -> p q t c"), w1_raw[0][:, :, :, 2:], ACT.Copy)
         copy_ratio(0)
-        x_late = stage.tile([P, S - EARLY], U32, offset=0, align_bytes=64)
-        for i in range(3):
-            relu(*first_product(0, (256 * i, 256 * (i + 1)), i), False)
-        gather_words(x_late[:], EARLY, S)
-        relu(*first_product(0, (EARLY, EARLY + P), 3), True)
-        relu(*first_product(0, (EARLY + P, S), 4), False)
-        rest = stage.tile([P, 4, 64, 4], BF16, offset=6144, align_bytes=64)
-        nc.vector.tensor_copy(rest[:].rearrange("p c q t -> p q t c"), w1_raw[1])
-        quantize_w1(second[:].rearrange("p c q t -> p (c q t)"), P)
-        quantize_w1(rest[:].rearrange("p c q t -> p (c q t)"), 2 * P)
         copy_ratio(1)
+        nc.vector.tensor_copy(planes[:, :, 1].rearrange("p c q t -> p q t c"), w1_raw[1])
+        for i in range(4):
+            relu(*first_product(0, 256 * i, 256 * (i + 1), i), i == 1)
+        for c in range(2):
+            quantize_w1(planes[:, c, 1].rearrange("p q t -> p (q t)"), P + 64 * c)
+        quantize_w1(grouped[:, 1024:], 2 * P)
         waiting = {
-            j: [first_product(j, (0, S // 2), (2 * j + 3) % 6), first_product(j, (S // 2, EARLY, S), (2 * j + 4) % 6)]
+            j: [first_product(j, n * S // 2, (n + 1) * S // 2, (2 * j + 2 + n) % 6) for n in range(2)]
             for j in range(1, TILES)
         }
 
@@ -195,26 +186,31 @@ def tile_picked_hop2_relu_p_kernel(
                 relu(dst, acc, False)
 
         low_sum = [bank(6 + n, [P, 2, 2, P], "low_sum%d" % n) for n in range(2)]
-        high_pair = bank(5, [P, 2, 2, P], "high_pair")
-        high_one = [bank(n, [P, 2, P], "high_one%d" % n) for n in range(2)]
+        high_pair = bank(4, [P, 2, 2, P], "high_pair")
+        high_one = bank(5, [P, 2, P], "high_one")
         sums = [
             [low_sum[0][:, 0], low_sum[0][:, 1], low_sum[1][:, 0], low_sum[1][:, 1]],
-            [high_pair[:, 0], high_pair[:, 1], high_one[0][:], high_one[1][:]],
+            [None, high_pair[:, 0], high_pair[:, 1], high_one[:]],
         ]
-        group = [[0, 0, 1, 1], [2, 2, 3, 4]]
-        left = [12, 12, 12, 6, 6]
+        group = [[0, 0, 1, 1], [None, 2, 2, 3]]
+        left = [12, 12, 12, 6]
         size = list(left)
+
+        def gather(values, j, d, a, b, weights):
+            window = h[j][:].indirect(pos_sb[d][:, a // 16 : b // 16])
+            if weights is None:
+                nc.scalar.activation(values, window, ACT.Copy)
+            else:
+                nc.vector.tensor_tensor(values, window, weights, ALU.mult)
 
         def term(j, d, a, b):
             if (j, d) == (0, 0):
-                values = stage.tile([P, b - a], F32, name="term_first", offset=5120)
+                values = stage.tile([P, b - a], F32, name="term_first", offset=8192)
+            elif (j, d) == (3, 0):
+                values = stage.tile([P, 2 * (b - a)], F32, name="term_held", offset=4096)[:, : b - a]
             else:
                 values = keep.tile([P, b - a], F32, name="term%d_%d_%d" % (j, d, a))
-            window = h[j][:].indirect(pos_sb[d][:, a // 16 : b // 16])
-            if d == 2:
-                nc.scalar.activation(values[:], window, ACT.Copy)
-            else:
-                nc.vector.tensor_tensor(values[:], window, ratio[d][:, a:b], ALU.mult)
+            gather(values[:], j, d, a, b, ratio[d][:, a:b] if d < 2 else None)
             for i in range(a // P, b // P):
                 n = group[j // 2][i]
                 nc.tensor.matmul(
@@ -226,19 +222,22 @@ def tile_picked_hop2_relu_p_kernel(
                     is_transpose=True,
                 )
                 left[n] = left[n] - 1
+            return values
 
         rows = keep.tile([P, 2, BLOCKS, P, 2], BF16)
-        back_pair = bank(2, [P, 2, 2, P], "back_pair")
-        back_one = [bank(3 + n, [P, 2, P], "back_one%d" % n) for n in range(2)]
-        back = [back_pair[:, 0], back_pair[:, 1], back_one[0][:], back_one[1][:]]
+        back_direct = bank(0, [P, 1, P], "back_direct")
+        back_pair = bank(1, [P, 2, 2, P], "back_pair")
+        back_one = bank(2, [P, 2, P], "back_one")
+        back = [back_direct[:], back_pair[:, 0], back_pair[:, 1], back_one[:]]
 
-        def round_and_turn(u, i, on_vector=False):
-            dst = rows[:, u, i].rearrange("v (j q) e -> v j q e", j=2)
-            src = sums[u][i].rearrange("v j (e q) -> v j q e", e=2)
-            if on_vector:
-                nc.vector.tensor_scalar(dst, src, factor[:, i : i + 1], None, ALU.mult)
+        def round_and_turn(u, i):
+            if u == 0:
+                dst = rows[:, u, i].rearrange("v (j q) e -> v j q e", j=2)
+                src = sums[u][i].rearrange("v j (e q) -> v j q e", e=2)
             else:
-                nc.scalar.activation(dst, src, ACT.Copy, scale=factor[:, i : i + 1])
+                dst = rows[:, u, i]
+                src = sums[u][i].rearrange("v e p -> v p e")
+            nc.scalar.activation(dst, src, ACT.Copy, scale=factor[:, i : i + 1])
             nc.tensor.transpose(back[i][:, u, :], rows[:, u, i].rearrange("v p e -> v (p e)").bitcast(F32), ident[:])
 
         term(0, 0, 0, V)
@@ -249,32 +248,57 @@ def tile_picked_hop2_relu_p_kernel(
         term(1, 1, 0, V)
         finish(2)
         term(1, 2, 0, V)
-        term(2, 0, 0, V)
-        term(2, 1, 0, V)
+        term(2, 0, P, V)
+        term(2, 1, P, V)
         finish(3)
-        for a in (0, V // 2):
-            for d in range(2):
-                term(2 + d, 2, a, a + V // 2)
-                term(3, d, a, a + V // 2)
-        for u in range(2):
-            for i in range(BLOCKS):
-                round_and_turn(u, i, on_vector=(u == 1))
+        term(2, 2, P, V)
+        term(3, 0, P, V)
+        term(3, 2, P, V)
+        term(3, 1, P, V)
+        for i in (1, 2, 3, 0):
+            round_and_turn(0, i)
+        for i in (1, 2, 3):
+            round_and_turn(1, i)
 
-        z = [keep.tile([P, P, 4], BF16, name="z%d" % i, align_bytes=64) for i in range(BLOCKS)]
+        z_direct = keep.tile([P, P, 4], BF16, align_bytes=64)
+        z_pair = keep.tile([P, 2 * P, 4], BF16, align_bytes=64)
+        z_one = keep.tile([P, P, 4], BF16, align_bytes=64)
+        nc.scalar.copy(
+            z_pair[:].bitcast(F32).rearrange("p (i v) u -> p i v u", i=2), back_pair[:].rearrange("p i u v -> p i v u")
+        )
+        nc.scalar.copy(z_one[:].bitcast(F32), back_one[:].rearrange("p u v -> p v u"))
+        nc.scalar.copy(z_direct[:].bitcast(F32)[:, :, :1], back_direct[:].rearrange("p u v -> p v u"))
+
+        halves = (slice(0, P // 2), slice(P // 2, P))
+        direct = [stage.tile([P, 2, P], F32, name="direct%d" % d, offset=4096 + 1024 * d) for d in range(D)]
+        for d in range(D):
+            for e in range(2):
+                gather(direct[d][:, e, :], 2 + e, d, 0, P, gate_direct[:, d, :])
+        two = keep.tile([P, 2, P], F32)
+        for part in halves:
+            nc.vector.tensor_tensor(two[:, :, part], direct[0][:, :, part], direct[1][:, :, part], ALU.add)
+        for part in halves:
+            nc.vector.tensor_tensor(
+                z_direct[:, part, 2:],
+                two[:, :, part].rearrange("p e v -> p v e"),
+                direct[2][:, :, part].rearrange("p e v -> p v e"),
+                ALU.add,
+            )
         z_word = keep.tile([P, V], U32, align_bytes=64)
         z_scale = keep.tile([P, V], U8, align_bytes=64)
         g = keep.tile([P, V], F32)
-        for i in range(BLOCKS):
-            src = back[i].rearrange("p u v -> p v u")
-            nc.scalar.copy(z[i][:].bitcast(F32), src)
-        for i in range(BLOCKS):
-            cols = slice(i * P, (i + 1) * P)
+
+        def second_product(z, a, b, where):
             nc.vector.quantize_mx(
-                out=z_word[:, cols].bitcast(FP8X4), scales=z_scale[:, cols], in_=z[i][:].rearrange("p v t -> p (v t)")
+                out=z_word[:, a:b].bitcast(FP8X4), scales=z_scale[:, a:b], in_=z.rearrange("p v t -> p (v t)")
             )
-            acc = bank((6, 7, 5, 0)[i], [P, P], "g_acc%d" % i)
-            product(acc[:], w2_word_sb[:], w2_scale_sb[:], z_word[:, cols], z_scale[:, cols])
-            relu(g[:, cols], acc[:], False)
+            acc = bank(where, [P, b - a], "g_acc%d" % a)
+            product(acc[:], w2_word_sb[:], w2_scale_sb[:], z_word[:, a:b], z_scale[:, a:b])
+            relu(g[:, a:b], acc[:], False)
+
+        second_product(z_pair[:], P, 3 * P, 6)
+        second_product(z_one[:], 3 * P, V, 7)
+        second_product(z_direct[:], 0, P, 3)
 
         halves = (slice(0, U // 2), slice(U // 2, U))
         terms = [keep.tile([P, U], F32, name="root_term%d" % d) for d in range(D)]

@@ -261,8 +261,8 @@ def tile_picked_hop2_relu_p_kernel(
             round_and_turn(1, i)
 
         z_direct = keep.tile([P, P, 4], BF16, align_bytes=64)
-        z_pair = keep.tile([P, 2 * P, 4], BF16, align_bytes=64)
-        z_one = keep.tile([P, P, 4], BF16, align_bytes=64)
+        z_pair = stage.tile([P, 2 * P, 4], BF16, offset=12288, align_bytes=64)
+        z_one = stage.tile([P, P, 4], BF16, offset=14336, align_bytes=64)
         nc.scalar.copy(
             z_pair[:].bitcast(F32).rearrange("p (i v) u -> p i v u", i=2), back_pair[:].rearrange("p i u v -> p i v u")
         )
@@ -284,21 +284,23 @@ def tile_picked_hop2_relu_p_kernel(
                 direct[2][:, :, part].rearrange("p e v -> p v e"),
                 ALU.add,
             )
-        z_word = keep.tile([P, V], U32, align_bytes=64)
+        z_word = keep.tile([P, V - P], U32, align_bytes=64)
+        z_word_direct = stage.tile([P, P], U32, offset=12288, align_bytes=64)
         z_scale = keep.tile([P, V], U8, align_bytes=64)
-        g = keep.tile([P, V], F32)
+        g = stage.tile([P, V], F32, offset=14336)
 
-        def second_product(z, a, b, where):
-            nc.vector.quantize_mx(
-                out=z_word[:, a:b].bitcast(FP8X4), scales=z_scale[:, a:b], in_=z.rearrange("p v t -> p (v t)")
-            )
+        def second_product(z, words, a, b, where):
+            nc.vector.quantize_mx(out=words.bitcast(FP8X4), scales=z_scale[:, a:b], in_=z.rearrange("p v t -> p (v t)"))
             acc = bank(where, [P, b - a], "g_acc%d" % a)
-            product(acc[:], w2_word_sb[:], w2_scale_sb[:], z_word[:, a:b], z_scale[:, a:b])
-            relu(g[:, a:b], acc[:], False)
+            product(acc[:], w2_word_sb[:], w2_scale_sb[:], words, z_scale[:, a:b])
+            return g[:, a:b], acc[:]
 
-        second_product(z_pair[:], P, 3 * P, 6)
-        second_product(z_one[:], 3 * P, V, 7)
-        second_product(z_direct[:], 0, P, 3)
+        pair = second_product(z_pair[:], z_word[:, : 2 * P], P, 3 * P, 6)
+        summed = second_product(z_direct[:], z_word_direct[:], 0, P, 3)
+        one = second_product(z_one[:], z_word[:, 2 * P :], 3 * P, V, 7)
+        relu(*pair, True)
+        relu(*summed, False)
+        relu(*one, False)
 
         halves = (slice(0, U // 2), slice(U // 2, U))
         terms = [keep.tile([P, U], F32, name="root_term%d" % d) for d in range(D)]

@@ -230,14 +230,17 @@ def tile_picked_hop2_relu_p_kernel(
         back_one = bank(2, [P, 2, P], "back_one")
         back = [back_direct[:], back_pair[:, 0], back_pair[:, 1], back_one[:]]
 
-        def round_and_turn(u, i):
+        def round_and_turn(u, i, on_vector=False):
             if u == 0:
                 dst = rows[:, u, i].rearrange("v (j q) e -> v j q e", j=2)
                 src = sums[u][i].rearrange("v j (e q) -> v j q e", e=2)
             else:
                 dst = rows[:, u, i]
                 src = sums[u][i].rearrange("v e p -> v p e")
-            nc.scalar.activation(dst, src, ACT.Copy, scale=factor[:, i : i + 1])
+            if on_vector:
+                nc.vector.tensor_scalar(dst, src, factor[:, i : i + 1], None, ALU.mult)
+            else:
+                nc.scalar.activation(dst, src, ACT.Copy, scale=factor[:, i : i + 1])
             nc.tensor.transpose(back[i][:, u, :], rows[:, u, i].rearrange("v p e -> v (p e)").bitcast(F32), ident[:])
 
         term(0, 0, 0, V)
@@ -256,7 +259,7 @@ def tile_picked_hop2_relu_p_kernel(
         term(3, 2, P, V)
         term(3, 1, P, V)
         for i in (1, 2, 3, 0):
-            round_and_turn(0, i)
+            round_and_turn(0, i, on_vector=(i == 0))
         for i in (1, 2, 3):
             round_and_turn(1, i)
 

@@ -318,4 +318,4 @@ def tile_picked_hop2_relu_p_kernel(
         result = keep.tile([P, U], F32)
         for part in halves:
             nc.vector.tensor_tensor(result[:, part], partial[:, part], terms[2][:, part], ALU.add)
-        nc.sync.dma_start(out, result[:])
+            nc.sync.dma_start(out[:, part], result[:, part])

@@ -56,17 +56,17 @@ def tile_picked_hop2_relu_p_kernel(
             nc.sync.dma_start(raw[:], w1_rows[:, :, a:b])
             return raw[:].rearrange("p t (q c) -> p q t c", c=4)
 
-        offs_sb = load_list(offs, "offs_sb")
         x_scale_table = keep.tile([P, T], U8, align_bytes=64)
         nc.vector.memset(x_scale_table[:].bitcast(I32), 0)
         load_scale_rows(x_scale_table, x_scales, (nc.sync, nc.scalar, nc.sync, nc.scalar))
         gate_rows = keep.tile([P, P], F32)
         nc.sync.dma_start(gate_rows[:], gate.rearrange("d r (i c) -> (d r i) c", c=P)[0 : ROW_STEP * P : ROW_STEP, :])
-        pos_sb = [load_list(pos1, "pos_sb0")]
+        offs_sb = load_list(offs, "offs_sb")
+        w1_raw = [load_w1(0, H // 2)]
         x_word_table = keep.tile([P, T], I32, align_bytes=64)
         load_words(x_word_table, x_words)
-        w1_raw = [load_w1(0, H // 2), load_w1(H // 2, H)]
-        pos_sb.extend([load_list(pos2, "pos_sb1"), load_list(pos3, "pos_sb2")])
+        w1_raw.append(load_w1(H // 2, H))
+        pos_sb = [load_list(src, "pos_sb%d" % d) for d, src in enumerate((pos1, pos2, pos3))]
         w2_word_sb = keep.tile([P, N], I32, align_bytes=64)
         load_words(w2_word_sb, w2_words)
         w2_scale_sb = keep.tile([P, N], U8, align_bytes=64)
@@ -108,14 +108,16 @@ def tile_picked_hop2_relu_p_kernel(
         nc.scalar.activation(least[:], both[:], ACT.Copy, bias=2.0**-100)
         side = keep.tile([P, BLOCKS], F32)
         nc.scalar.activation(side[:], sign3[:], ACT.Sign, bias=half[:])
-        factor = keep.tile([P, BLOCKS], F32)
+        divisor = stage.tile([P, BLOCKS], F32, offset=16384)
         for i in range(BLOCKS):
             col = slice(i, i + 1)
-            nc.scalar.activation(factor[:, col], side[:, col], ACT.Identity, scale=least[:, col], bias=gate_col[:, 2, col])
+            nc.scalar.activation(divisor[:, col], side[:, col], ACT.Identity, scale=least[:, col], bias=gate_col[:, 2, col])
         inverse = keep.tile([P, BLOCKS], F32)
-        nc.vector.reciprocal(inverse[:], factor[:])
+        nc.vector.reciprocal(inverse[:], divisor[:])
+        factor = keep.tile([P, BLOCKS], F32)
+        nc.scalar.activation(factor[:], divisor[:], ACT.Copy)
         ratio_col = [keep.tile([P, 2], F32, name="ratio_col%d" % i) for i in range(BLOCKS)]
-        ratio = [stage.tile([P, V], F32, name="ratio%d" % d, offset=2048 * d) for d in range(2)]
+        ratio = [keep.tile([P, V], F32, name="ratio%d" % d) for d in range(2)]
         for i in range(BLOCKS):
             nc.scalar.activation(ratio_col[i][:], gate_col[:, :2, i], ACT.Copy, scale=inverse[:, i : i + 1])
         spread = [bank(6 + d, [P, BLOCKS, P], "spread%d" % d) for d in range(2)]
@@ -133,7 +135,10 @@ def tile_picked_hop2_relu_p_kernel(
             cols = slice(first, first + grouped.shape[1] // 4)
             nc.vector.quantize_mx(out=w1_word[:, cols].bitcast(FP8X4), scales=w1_scale[:, cols], in_=grouped)
 
-        x_scale = keep.tile([P, S], U8, align_bytes=64)
+        x_scale = [
+            keep.tile([P, S // 2], U8, name="x_scale0", align_bytes=64),
+            stage.tile([P, S // 2], U8, name="x_scale1", offset=16384, align_bytes=64),
+        ]
         h = [keep.tile([P, S], F32, name="h%d" % j) for j in range(TILES)]
         x_word = keep.tile([P, S], U32, align_bytes=64)
 
@@ -157,25 +162,29 @@ def tile_picked_hop2_relu_p_kernel(
         def first_product(j, a, b, where):
             acc = bank(where, [P, b - a], "h_acc%d_%d" % (j, a))
             cols = slice(j * P, (j + 1) * P)
-            product(acc[:], w1_word[:, cols], w1_scale[:, cols], x_word[:, a:b], x_scale[:, a:b])
+            product(acc[:], w1_word[:, cols], w1_scale[:, cols], x_word[:, a:b], x_scale[a // 512][:, a % 512 : a % 512 + b - a])
             return h[j][:, a:b], acc[:]
 
-        nc.vector.tensor_copy(x_scale[:], x_scale_table[:].indirect(offs_sb[:]))
-        nc.vector.tensor_copy(x_word[:], x_word_table[:].bitcast(U32).indirect(offs_sb[:]))
-        grouped = stage.tile([P, 2048], BF16, offset=8192, align_bytes=64)
-        planes = grouped[:].rearrange("p (c half q t) -> p c half q t", c=4, half=2, t=4)
-        first = grouped[:, 256:768]
-        nc.scalar.activation(first.rearrange("p (c q t) -> p q t c", c=2, t=4), w1_raw[0][:, :, :, :2], ACT.Copy)
-        quantize_w1(first, 0)
-        nc.scalar.activation(planes[:, 2:, 0].rearrange("p c q t -> p q t c"), w1_raw[0][:, :, :, 2:], ACT.Copy)
+        for n in range(2):
+            nc.vector.tensor_copy(x_scale[n][:], x_scale_table[:].indirect(offs_sb[:, 32 * n : 32 * (n + 1)]))
+        low = [keep.tile([P, 512], BF16, name="w1_low%d" % n, align_bytes=64) for n in range(2)]
+        grouped = stage.tile([P, 1024], BF16, offset=8192, align_bytes=64)
+        planes = grouped[:].rearrange("p (c half q t) -> p half q t c", c=2, half=2, t=4)
+        nc.scalar.activation(low[0][:].rearrange("p (c q t) -> p q t c", c=2, t=4), w1_raw[0][:, :, :, :2], ACT.Copy)
+        quantize_w1(low[0][:], 0)
+        nc.scalar.activation(planes[:, 0], w1_raw[0][:, :, :, 2:], ACT.Copy)
         copy_ratio(0)
         copy_ratio(1)
-        nc.vector.tensor_copy(planes[:, :, 1].rearrange("p c q t -> p q t c"), w1_raw[1])
         for i in range(4):
-            relu(*first_product(0, 256 * i, 256 * (i + 1), i), i == 1)
-        for c in range(2):
-            quantize_w1(planes[:, c, 1].rearrange("p q t -> p (q t)"), P + 64 * c)
-        quantize_w1(grouped[:, 1024:], 2 * P)
+            nc.vector.tensor_copy(
+                x_word[:, 256 * i : 256 * (i + 1)],
+                x_word_table[:].bitcast(U32).indirect(offs_sb[:, 16 * i : 16 * (i + 1)]),
+            )
+            relu(*first_product(0, 256 * i, 256 * (i + 1), i), False)
+        nc.vector.tensor_copy(low[1][:].rearrange("p (c q t) -> p q t c", c=2, t=4), w1_raw[1][:, :, :, :2])
+        nc.vector.tensor_copy(planes[:, 1], w1_raw[1][:, :, :, 2:])
+        quantize_w1(low[1][:], P)
+        quantize_w1(grouped[:], 2 * P)
         waiting = {
             j: [first_product(j, n * S // 2, (n + 1) * S // 2, (2 * j + 2 + n) % 6) for n in range(2)]
             for j in range(1, TILES)

@@ -21,6 +21,7 @@ BLOCKS = V // P
 BANK = 2048
 ROW_STEP = 9
 GROUP = 60
+EARLY = 256
 
 
 def tile_picked_hop2_relu_p_kernel(
@@ -51,8 +52,8 @@ def tile_picked_hop2_relu_p_kernel(
 
         w1_rows = w1.rearrange("(p t) c -> p t c", t=4)
 
-        def load_w1(a, b):
-            raw = stage.tile([P, 4, b - a], F32, name="w1_raw%d" % a, offset=16 * a)
+        def load_w1(a, b, offset):
+            raw = stage.tile([P, 4, b - a], F32, name="w1_raw%d" % a, offset=offset)
             nc.sync.dma_start(raw[:], w1_rows[:, :, a:b])
             return raw[:].rearrange("p t (q c) -> p q t c", c=4)
 
@@ -61,11 +62,12 @@ def tile_picked_hop2_relu_p_kernel(
         load_scale_rows(x_scale_table, x_scales, (nc.sync, nc.scalar, nc.sync, nc.scalar))
         gate_rows = keep.tile([P, P], F32)
         nc.sync.dma_start(gate_rows[:], gate.rearrange("d r (i c) -> (d r i) c", c=P)[0 : ROW_STEP * P : ROW_STEP, :])
-        offs_sb = load_list(offs, "offs_sb")
-        w1_raw = [load_w1(0, H // 2)]
         x_word_table = keep.tile([P, T], I32, align_bytes=64)
-        load_words(x_word_table, x_words)
-        w1_raw.append(load_w1(H // 2, H))
+        x_word_rows = x_words[0].rearrange("p n t -> p (n t)").bitcast(I32)
+        nc.sync.dma_start(x_word_table[:, :EARLY], x_word_rows[:, :EARLY])
+        offs_sb = load_list(offs, "offs_sb")
+        nc.sync.dma_start(x_word_table[:, EARLY:], x_word_rows[:, EARLY:])
+        w1_raw = [load_w1(0, H // 2, 1024), load_w1(H // 2, H, 20480)]
         pos_sb = [load_list(src, "pos_sb%d" % d) for d, src in enumerate((pos1, pos2, pos3))]
         w2_word_sb = keep.tile([P, N], I32, align_bytes=64)
         load_words(w2_word_sb, w2_words)
@@ -108,16 +110,14 @@ def tile_picked_hop2_relu_p_kernel(
         nc.scalar.activation(least[:], both[:], ACT.Copy, bias=2.0**-100)
         side = keep.tile([P, BLOCKS], F32)
         nc.scalar.activation(side[:], sign3[:], ACT.Sign, bias=half[:])
-        divisor = stage.tile([P, BLOCKS], F32, offset=16384)
+        factor = keep.tile([P, BLOCKS], F32)
         for i in range(BLOCKS):
             col = slice(i, i + 1)
-            nc.scalar.activation(divisor[:, col], side[:, col], ACT.Identity, scale=least[:, col], bias=gate_col[:, 2, col])
+            nc.scalar.activation(factor[:, col], side[:, col], ACT.Identity, scale=least[:, col], bias=gate_col[:, 2, col])
         inverse = keep.tile([P, BLOCKS], F32)
-        nc.vector.reciprocal(inverse[:], divisor[:])
-        factor = keep.tile([P, BLOCKS], F32)
-        nc.scalar.activation(factor[:], divisor[:], ACT.Copy)
+        nc.vector.reciprocal(inverse[:], factor[:])
         ratio_col = [keep.tile([P, 2], F32, name="ratio_col%d" % i) for i in range(BLOCKS)]
-        ratio = [keep.tile([P, V], F32, name="ratio%d" % d) for d in range(2)]
+        ratio = [stage.tile([P, V], F32, name="ratio0", offset=0), stage.tile([P, V], F32, name="ratio1", offset=3328)]
         for i in range(BLOCKS):
             nc.scalar.activation(ratio_col[i][:], gate_col[:, :2, i], ACT.Copy, scale=inverse[:, i : i + 1])
         spread = [bank(6 + d, [P, BLOCKS, P], "spread%d" % d) for d in range(2)]
@@ -128,19 +128,20 @@ def tile_picked_hop2_relu_p_kernel(
         def copy_ratio(d):
             nc.scalar.activation(ratio[d][:], spread[d][:].rearrange("p i v -> p (i v)"), ACT.Copy)
 
-        w1_word = keep.tile([P, H], U32, align_bytes=64)
+        w1_word = [
+            keep.tile([P, P], U32, name="w1_word0", align_bytes=64),
+            stage.tile([P, P], U32, name="w1_word1", offset=11264, align_bytes=64),
+            keep.tile([P, 2 * P], U32, name="w1_word2", align_bytes=64),
+        ]
         w1_scale = keep.tile([P, H], U8, align_bytes=64)
 
         def quantize_w1(grouped, first):
             cols = slice(first, first + grouped.shape[1] // 4)
-            nc.vector.quantize_mx(out=w1_word[:, cols].bitcast(FP8X4), scales=w1_scale[:, cols], in_=grouped)
+            nc.vector.quantize_mx(out=w1_word[first // P][:].bitcast(FP8X4), scales=w1_scale[:, cols], in_=grouped)
 
-        x_scale = [
-            keep.tile([P, S // 2], U8, name="x_scale0", align_bytes=64),
-            stage.tile([P, S // 2], U8, name="x_scale1", offset=16384, align_bytes=64),
-        ]
+        x_scale = keep.tile([P, 768], U8, align_bytes=64)
         h = [keep.tile([P, S], F32, name="h%d" % j) for j in range(TILES)]
-        x_word = keep.tile([P, S], U32, align_bytes=64)
+        x_word = keep.tile([P, 768], U32, align_bytes=64)
 
         def product(acc, lhs_word, lhs_scale, rhs_word, rhs_scale):
             nc.tensor.matmul_mx(
@@ -162,31 +163,47 @@ def tile_picked_hop2_relu_p_kernel(
         def first_product(j, a, b, where):
             acc = bank(where, [P, b - a], "h_acc%d_%d" % (j, a))
             cols = slice(j * P, (j + 1) * P)
-            product(acc[:], w1_word[:, cols], w1_scale[:, cols], x_word[:, a:b], x_scale[a // 512][:, a % 512 : a % 512 + b - a])
+            for c, e in ((a, min(b, 768)), (max(a, 768), b)):
+                if c < e:
+                    words = x_word[:, c:e] if c < 768 else x_late[:, c - 768 : e - 768]
+                    scales = x_scale[:, c:e] if c < 768 else x_scale_late[:, c - 768 : e - 768]
+                    product(acc[:, c - a : e - a], w1_word[min(j, 2)][:, (j // 3) * P : (j // 3 + 1) * P], w1_scale[:, cols], words, scales)
             return h[j][:, a:b], acc[:]
 
-        for n in range(2):
-            nc.vector.tensor_copy(x_scale[n][:], x_scale_table[:].indirect(offs_sb[:, 32 * n : 32 * (n + 1)]))
-        low = [keep.tile([P, 512], BF16, name="w1_low%d" % n, align_bytes=64) for n in range(2)]
-        grouped = stage.tile([P, 1024], BF16, offset=8192, align_bytes=64)
+        nc.vector.tensor_copy(x_scale[:], x_scale_table[:].indirect(offs_sb[:, :48]))
+        low = [
+            keep.tile([P, 512], BF16, name="w1_low0", align_bytes=64),
+            keep.tile([P, 512], BF16, name="w1_low1", align_bytes=64),
+        ]
+        grouped = stage.tile([P, 1024], BF16, offset=9216, align_bytes=64)
         planes = grouped[:].rearrange("p (c half q t) -> p half q t c", c=2, half=2, t=4)
         nc.scalar.activation(low[0][:].rearrange("p (c q t) -> p q t c", c=2, t=4), w1_raw[0][:, :, :, :2], ACT.Copy)
+        nc.vector.tensor_copy(x_word[:], x_word_table[:].bitcast(U32).indirect(offs_sb[:, :48]))
         quantize_w1(low[0][:], 0)
-        nc.scalar.activation(planes[:, 0], w1_raw[0][:, :, :, 2:], ACT.Copy)
         copy_ratio(0)
         copy_ratio(1)
-        for i in range(4):
+
+        def round_on_gpsimd(dst, src):
+            nc.gpsimd.tensor_scalar(dst, src.rearrange("p q t c -> p c q t"), 1.0, 0.0, ALU.mult, ALU.add)
+
+        round_on_gpsimd(planes[:, 0].rearrange("p q t c -> p c q t"), w1_raw[0][:, :, :, 2:])
+        round_on_gpsimd(planes[:, 1].rearrange("p q t c -> p c q t"), w1_raw[1][:, :, :, 2:])
+        x_scale_late = stage.tile([P, 256], U8, offset=3072, align_bytes=64)
+        nc.vector.tensor_copy(x_scale_late[:], x_scale_table[:].indirect(offs_sb[:, 48:]))
+        x_late = stage.tile([P, 256], U32, offset=2048, align_bytes=64)
+        for n in range(2):
             nc.vector.tensor_copy(
-                x_word[:, 256 * i : 256 * (i + 1)],
-                x_word_table[:].bitcast(U32).indirect(offs_sb[:, 16 * i : 16 * (i + 1)]),
+                x_late[:, n * P : (n + 1) * P], x_word_table[:].bitcast(U32).indirect(offs_sb[:, 48 + 8 * n : 56 + 8 * n])
             )
-            relu(*first_product(0, 256 * i, 256 * (i + 1), i), False)
+        cuts = (0, 256, 512, 768, 896, 1024)
+        pieces = [first_product(0, cuts[i], cuts[i + 1], i) for i in range(5)]
         nc.vector.tensor_copy(low[1][:].rearrange("p (c q t) -> p q t c", c=2, t=4), w1_raw[1][:, :, :, :2])
-        nc.vector.tensor_copy(planes[:, 1], w1_raw[1][:, :, :, 2:])
+        for i in range(5):
+            relu(*pieces[i], i == 3)
         quantize_w1(low[1][:], P)
         quantize_w1(grouped[:], 2 * P)
         waiting = {
-            j: [first_product(j, n * S // 2, (n + 1) * S // 2, (2 * j + 2 + n) % 6) for n in range(2)]
+            j: [first_product(j, n * S // 2, (n + 1) * S // 2, (2 * j + 3 + n) % 6) for n in range(2)]
             for j in range(1, TILES)
         }
 
@@ -213,10 +230,10 @@ def tile_picked_hop2_relu_p_kernel(
                 nc.vector.tensor_tensor(values, window, weights, ALU.mult)
 
         def term(j, d, a, b):
-            if (j, d) == (0, 0):
-                values = stage.tile([P, b - a], F32, name="term_first", offset=8192)
+            if j == 0 and d != 1:
+                values = stage.tile([P, b - a], F32, name="term_first%d_%d" % (d, a), offset=8192 + 1024 * d + 4 * a)
             elif (j, d) == (3, 0):
-                values = stage.tile([P, 2 * (b - a)], F32, name="term_held", offset=4096)[:, : b - a]
+                values = stage.tile([P, 2 * (b - a)], F32, name="term_held", offset=16384)[:, : b - a]
             else:
                 values = keep.tile([P, b - a], F32, name="term%d_%d_%d" % (j, d, a))
             gather(values[:], j, d, a, b, ratio[d][:, a:b] if d < 2 else None)
@@ -253,16 +270,17 @@ def tile_picked_hop2_relu_p_kernel(
             nc.tensor.transpose(back[i][:, u, :], rows[:, u, i].rearrange("v p e -> v (p e)").bitcast(F32), ident[:])
 
         term(0, 0, 0, V)
-        term(0, 1, 0, V)
+        term(0, 2, 0, V // 2)
         finish(1)
-        term(0, 2, 0, V)
+        term(0, 1, 0, V)
+        term(0, 2, V // 2, V)
+        finish(2)
         term(1, 0, 0, V)
         term(1, 1, 0, V)
-        finish(2)
         term(1, 2, 0, V)
+        finish(3)
         term(2, 0, P, V)
         term(2, 1, P, V)
-        finish(3)
         term(2, 2, P, V)
         term(3, 0, P, V)
         term(3, 2, P, V)
@@ -282,7 +300,7 @@ def tile_picked_hop2_relu_p_kernel(
         nc.scalar.copy(z_direct[:].bitcast(F32)[:, :, :1], back_direct[:].rearrange("p u v -> p v u"))
 
         halves = (slice(0, P // 2), slice(P // 2, P))
-        direct = [stage.tile([P, 2, P], F32, name="direct%d" % d, offset=4096 + 1024 * d) for d in range(D)]
+        direct = [stage.tile([P, 2, P], F32, name="direct%d" % d, offset=16384 + 1024 * d) for d in range(D)]
         for d in range(D):
             for e in range(2):
                 gather(direct[d][:, e, :], 2 + e, d, 0, P, gate_direct[:, d, :])
@@ -327,4 +345,4 @@ def tile_picked_hop2_relu_p_kernel(
         result = keep.tile([P, U], F32)
         for part in halves:
             nc.vector.tensor_tensor(result[:, part], partial[:, part], terms[2][:, part], ALU.add)
-            nc.sync.dma_start(out[:, part], result[:, part])
+        nc.sync.dma_start(out, result[:])

@@ -22,6 +22,7 @@ BANK = 2048
 ROW_STEP = 9
 GROUP = 60
 EARLY = 256
+FIRST = 640
 
 
 def tile_picked_hop2_relu_p_kernel(
@@ -116,13 +117,13 @@ def tile_picked_hop2_relu_p_kernel(
             nc.scalar.activation(factor[:, col], side[:, col], ACT.Identity, scale=least[:, col], bias=gate_col[:, 2, col])
         inverse = keep.tile([P, BLOCKS], F32)
         nc.vector.reciprocal(inverse[:], factor[:])
-        ratio_col = [keep.tile([P, 2], F32, name="ratio_col%d" % i) for i in range(BLOCKS)]
-        ratio = [stage.tile([P, V], F32, name="ratio0", offset=0), stage.tile([P, V], F32, name="ratio1", offset=3328)]
+        ratio_col = [stage.tile([P, 2], F32, name="ratio_col%d" % i, offset=(0, 64, 512, 576)[i]) for i in range(BLOCKS)]
+        ratio = [stage.tile([P, V], F32, name="ratio%d" % d, offset=2560 + 2048 * d) for d in range(2)]
         for i in range(BLOCKS):
             nc.scalar.activation(ratio_col[i][:], gate_col[:, :2, i], ACT.Copy, scale=inverse[:, i : i + 1])
         spread = [bank(6 + d, [P, BLOCKS, P], "spread%d" % d) for d in range(2)]
-        for d in range(2):
-            for i in range(BLOCKS):
+        for i in range(BLOCKS):
+            for d in range(2):
                 nc.tensor.transpose(spread[d][:, i, :], ratio_col[i][:, d : d + 1].to_broadcast([P, P]), ident[:])
 
         def copy_ratio(d):
@@ -139,9 +140,9 @@ def tile_picked_hop2_relu_p_kernel(
             cols = slice(first, first + grouped.shape[1] // 4)
             nc.vector.quantize_mx(out=w1_word[first // P][:].bitcast(FP8X4), scales=w1_scale[:, cols], in_=grouped)
 
-        x_scale = keep.tile([P, 768], U8, align_bytes=64)
+        x_scale = keep.tile([P, FIRST], U8, align_bytes=64)
         h = [keep.tile([P, S], F32, name="h%d" % j) for j in range(TILES)]
-        x_word = keep.tile([P, 768], U32, align_bytes=64)
+        x_word = keep.tile([P, FIRST], U32, align_bytes=64)
 
         def product(acc, lhs_word, lhs_scale, rhs_word, rhs_scale):
             nc.tensor.matmul_mx(
@@ -163,43 +164,43 @@ def tile_picked_hop2_relu_p_kernel(
         def first_product(j, a, b, where):
             acc = bank(where, [P, b - a], "h_acc%d_%d" % (j, a))
             cols = slice(j * P, (j + 1) * P)
-            for c, e in ((a, min(b, 768)), (max(a, 768), b)):
-                if c < e:
-                    words = x_word[:, c:e] if c < 768 else x_late[:, c - 768 : e - 768]
-                    scales = x_scale[:, c:e] if c < 768 else x_scale_late[:, c - 768 : e - 768]
-                    product(acc[:, c - a : e - a], w1_word[min(j, 2)][:, (j // 3) * P : (j // 3 + 1) * P], w1_scale[:, cols], words, scales)
+            lhs = w1_word[min(j, 2)][:, (j // 3) * P : (j // 3 + 1) * P]
+            for c, e in ((a, b),) if b <= 512 else zip(cuts[2:-1], cuts[3:]):
+                if a <= c and e <= b:
+                    words = x_word[:, c:e] if c < FIRST else x_late[:, c - FIRST : e - FIRST]
+                    scales = x_scale[:, c:e] if c < FIRST else x_scale_late[:, c - FIRST : e - FIRST]
+                    product(acc[:, c - a : e - a], lhs, w1_scale[:, cols], words, scales)
             return h[j][:, a:b], acc[:]
 
-        nc.vector.tensor_copy(x_scale[:], x_scale_table[:].indirect(offs_sb[:, :48]))
-        low = [
-            keep.tile([P, 512], BF16, name="w1_low0", align_bytes=64),
-            keep.tile([P, 512], BF16, name="w1_low1", align_bytes=64),
-        ]
-        grouped = stage.tile([P, 1024], BF16, offset=9216, align_bytes=64)
+        cuts = (0, 256, 512, FIRST, 896, S)
+        nc.vector.tensor_copy(x_scale[:], x_scale_table[:].indirect(offs_sb[:, : FIRST // 16]))
+        low = [keep.tile([P, 512], BF16, name="w1_low%d" % n, align_bytes=64) for n in range(2)]
+        grouped = keep.tile([P, 1024], BF16, align_bytes=64)
         planes = grouped[:].rearrange("p (c half q t) -> p half q t c", c=2, half=2, t=4)
-        nc.scalar.activation(low[0][:].rearrange("p (c q t) -> p q t c", c=2, t=4), w1_raw[0][:, :, :, :2], ACT.Copy)
-        nc.vector.tensor_copy(x_word[:], x_word_table[:].bitcast(U32).indirect(offs_sb[:, :48]))
-        quantize_w1(low[0][:], 0)
         copy_ratio(0)
+        nc.scalar.activation(low[0][:].rearrange("p (c q t) -> p q t c", c=2, t=4), w1_raw[0][:, :, :, :2], ACT.Copy)
         copy_ratio(1)
-
-        def round_on_gpsimd(dst, src):
-            nc.gpsimd.tensor_scalar(dst, src.rearrange("p q t c -> p c q t"), 1.0, 0.0, ALU.mult, ALU.add)
-
-        round_on_gpsimd(planes[:, 0].rearrange("p q t c -> p c q t"), w1_raw[0][:, :, :, 2:])
-        round_on_gpsimd(planes[:, 1].rearrange("p q t c -> p c q t"), w1_raw[1][:, :, :, 2:])
-        x_scale_late = stage.tile([P, 256], U8, offset=3072, align_bytes=64)
-        nc.vector.tensor_copy(x_scale_late[:], x_scale_table[:].indirect(offs_sb[:, 48:]))
-        x_late = stage.tile([P, 256], U32, offset=2048, align_bytes=64)
-        for n in range(2):
+        nc.gpsimd.tensor_scalar(
+            planes[:, 0].rearrange("p q t c -> p c q t"),
+            w1_raw[0][:, :, :, 2:].rearrange("p q t c -> p c q t"),
+            1.0,
+            0.0,
+            ALU.mult,
+            ALU.add,
+        )
+        nc.vector.tensor_copy(x_word[:], x_word_table[:].bitcast(U32).indirect(offs_sb[:, : FIRST // 16]))
+        x_scale_late = stage.tile([P, S - FIRST], U8, offset=0, align_bytes=64)
+        nc.vector.tensor_copy(x_scale_late[:], x_scale_table[:].indirect(offs_sb[:, FIRST // 16 :]))
+        quantize_w1(low[0][:], 0)
+        x_late = stage.tile([P, S - FIRST], U32, offset=1024, align_bytes=64)
+        for a, b in zip(cuts[3:-1], cuts[4:]):
             nc.vector.tensor_copy(
-                x_late[:, n * P : (n + 1) * P], x_word_table[:].bitcast(U32).indirect(offs_sb[:, 48 + 8 * n : 56 + 8 * n])
+                x_late[:, a - FIRST : b - FIRST], x_word_table[:].bitcast(U32).indirect(offs_sb[:, a // 16 : b // 16])
             )
-        cuts = (0, 256, 512, 768, 896, 1024)
-        pieces = [first_product(0, cuts[i], cuts[i + 1], i) for i in range(5)]
-        nc.vector.tensor_copy(low[1][:].rearrange("p (c q t) -> p q t c", c=2, t=4), w1_raw[1][:, :, :, :2])
         for i in range(5):
-            relu(*pieces[i], i == 3)
+            relu(*first_product(0, cuts[i], cuts[i + 1], i), False)
+        nc.vector.tensor_copy(low[1][:].rearrange("p (c q t) -> p q t c", c=2, t=4), w1_raw[1][:, :, :, :2])
+        nc.vector.tensor_copy(planes[:, 1], w1_raw[1][:, :, :, 2:])
         quantize_w1(low[1][:], P)
         quantize_w1(grouped[:], 2 * P)
         waiting = {
@@ -231,7 +232,7 @@ def tile_picked_hop2_relu_p_kernel(
 
         def term(j, d, a, b):
             if j == 0 and d != 1:
-                values = stage.tile([P, b - a], F32, name="term_first%d_%d" % (d, a), offset=8192 + 1024 * d + 4 * a)
+                values = stage.tile([P, b - a], F32, name="term_first%d_%d" % (d, a), offset=(20480 + 1024 * d, 11264)[a // 256])
             elif (j, d) == (3, 0):
                 values = stage.tile([P, 2 * (b - a)], F32, name="term_held", offset=16384)[:, : b - a]
             else:
@@ -286,7 +287,7 @@ def tile_picked_hop2_relu_p_kernel(
         term(3, 2, P, V)
         term(3, 1, P, V)
         for i in (1, 2, 3, 0):
-            round_and_turn(0, i, on_vector=(i == 0))
+            round_and_turn(0, i)
         for i in (1, 2, 3):
             round_and_turn(1, i)
 

@@ -22,7 +22,7 @@ BANK = 2048
 ROW_STEP = 9
 GROUP = 60
 EARLY = 256
-FIRST = 640
+FIRST = 768
 
 
 def tile_picked_hop2_relu_p_kernel(
@@ -117,13 +117,13 @@ def tile_picked_hop2_relu_p_kernel(
             nc.scalar.activation(factor[:, col], side[:, col], ACT.Identity, scale=least[:, col], bias=gate_col[:, 2, col])
         inverse = keep.tile([P, BLOCKS], F32)
         nc.vector.reciprocal(inverse[:], factor[:])
-        ratio_col = [stage.tile([P, 2], F32, name="ratio_col%d" % i, offset=(0, 64, 512, 576)[i]) for i in range(BLOCKS)]
+        ratio_col = [stage.tile([P, 2], F32, name="ratio_col%d" % i, offset=(0, 512, 576, 640)[i]) for i in range(BLOCKS)]
         ratio = [stage.tile([P, V], F32, name="ratio%d" % d, offset=2560 + 2048 * d) for d in range(2)]
         for i in range(BLOCKS):
             nc.scalar.activation(ratio_col[i][:], gate_col[:, :2, i], ACT.Copy, scale=inverse[:, i : i + 1])
         spread = [bank(6 + d, [P, BLOCKS, P], "spread%d" % d) for d in range(2)]
-        for i in range(BLOCKS):
-            for d in range(2):
+        for d in range(2):
+            for i in range(BLOCKS):
                 nc.tensor.transpose(spread[d][:, i, :], ratio_col[i][:, d : d + 1].to_broadcast([P, P]), ident[:])
 
         def copy_ratio(d):
@@ -197,10 +197,11 @@ def tile_picked_hop2_relu_p_kernel(
             nc.vector.tensor_copy(
                 x_late[:, a - FIRST : b - FIRST], x_word_table[:].bitcast(U32).indirect(offs_sb[:, a // 16 : b // 16])
             )
-        for i in range(5):
-            relu(*first_product(0, cuts[i], cuts[i + 1], i), False)
+        pieces = [first_product(0, cuts[i], cuts[i + 1], i) for i in range(5)]
         nc.vector.tensor_copy(low[1][:].rearrange("p (c q t) -> p q t c", c=2, t=4), w1_raw[1][:, :, :, :2])
         nc.vector.tensor_copy(planes[:, 1], w1_raw[1][:, :, :, 2:])
+        for i in range(5):
+            relu(*pieces[i], i == 2)
         quantize_w1(low[1][:], P)
         quantize_w1(grouped[:], 2 * P)
         waiting = {
@@ -333,17 +334,20 @@ def tile_picked_hop2_relu_p_kernel(
         relu(*summed, False)
         relu(*one, False)
 
-        halves = (slice(0, U // 2), slice(U // 2, U))
+        front, rear = slice(0, U // 2), slice(U // 2, U)
+        third = keep.tile([P, U], F32)
+        nc.scalar.activation(third[:], g[:].indirect(nxt_sb[2][:]), ACT.Copy)
+        second_rear = keep.tile([P, U // 2], F32)
+        nc.scalar.activation(second_rear[:], g[:].indirect(nxt_sb[1][:, U // 32 :]), ACT.Copy)
         terms = [keep.tile([P, U], F32, name="root_term%d" % d) for d in range(D)]
-        plain = keep.tile([P, U], F32)
-        nc.scalar.activation(plain[:], g[:].indirect(nxt_sb[2][:]), ACT.Copy)
-        for d in range(2):
-            nc.vector.tensor_tensor(terms[d][:], g[:].indirect(nxt_sb[d][:]), gate2_sb[:, d, :], ALU.mult)
-        nc.vector.tensor_tensor(terms[2][:], plain[:], gate2_sb[:, 2, :], ALU.mult)
+        nc.vector.tensor_tensor(terms[0][:], g[:].indirect(nxt_sb[0][:]), gate2_sb[:, 0, :], ALU.mult)
+        nc.vector.tensor_tensor(terms[1][:, front], g[:].indirect(nxt_sb[1][:, : U // 32]), gate2_sb[:, 1, front], ALU.mult)
+        nc.vector.tensor_tensor(terms[2][:], third[:], gate2_sb[:, 2, :], ALU.mult)
         partial = keep.tile([P, U], F32)
-        for part in halves:
-            nc.vector.tensor_tensor(partial[:, part], terms[0][:, part], terms[1][:, part], ALU.add)
         result = keep.tile([P, U], F32)
-        for part in halves:
-            nc.vector.tensor_tensor(result[:, part], partial[:, part], terms[2][:, part], ALU.add)
+        nc.vector.tensor_tensor(partial[:, front], terms[0][:, front], terms[1][:, front], ALU.add)
+        nc.vector.tensor_tensor(partial[:, rear], terms[0][:, rear], terms[2][:, rear], ALU.add)
+        nc.vector.tensor_tensor(terms[1][:, rear], second_rear[:], gate2_sb[:, 1, rear], ALU.mult)
+        nc.vector.tensor_tensor(result[:, front], partial[:, front], terms[2][:, front], ALU.add)
+        nc.vector.tensor_tensor(result[:, rear], partial[:, rear], terms[1][:, rear], ALU.add)
         nc.sync.dma_start(out, result[:])

@@ -23,6 +23,7 @@ ROW_STEP = 9
 GROUP = 60
 EARLY = 256
 FIRST = 768
+FIRST_BYTES = 640
 
 
 def tile_picked_hop2_relu_p_kernel(
@@ -107,7 +108,7 @@ def tile_picked_hop2_relu_p_kernel(
             )
         sign3 = keep.tile([P, BLOCKS], F32)
         nc.scalar.activation(sign3[:], gate_turned[:, 2, :BLOCKS], ACT.Sign)
-        least = keep.tile([P, BLOCKS], F32)
+        least = stage.tile([P, BLOCKS], F32, offset=0)
         nc.scalar.activation(least[:], both[:], ACT.Copy, bias=2.0**-100)
         side = keep.tile([P, BLOCKS], F32)
         nc.scalar.activation(side[:], sign3[:], ACT.Sign, bias=half[:])
@@ -117,7 +118,7 @@ def tile_picked_hop2_relu_p_kernel(
             nc.scalar.activation(factor[:, col], side[:, col], ACT.Identity, scale=least[:, col], bias=gate_col[:, 2, col])
         inverse = keep.tile([P, BLOCKS], F32)
         nc.vector.reciprocal(inverse[:], factor[:])
-        ratio_col = [stage.tile([P, 2], F32, name="ratio_col%d" % i, offset=(0, 512, 576, 640)[i]) for i in range(BLOCKS)]
+        ratio_col = [keep.tile([P, 2], F32, name="ratio_col%d" % i) for i in range(BLOCKS)]
         ratio = [stage.tile([P, V], F32, name="ratio%d" % d, offset=2560 + 2048 * d) for d in range(2)]
         for i in range(BLOCKS):
             nc.scalar.activation(ratio_col[i][:], gate_col[:, :2, i], ACT.Copy, scale=inverse[:, i : i + 1])
@@ -140,7 +141,7 @@ def tile_picked_hop2_relu_p_kernel(
             cols = slice(first, first + grouped.shape[1] // 4)
             nc.vector.quantize_mx(out=w1_word[first // P][:].bitcast(FP8X4), scales=w1_scale[:, cols], in_=grouped)
 
-        x_scale = keep.tile([P, FIRST], U8, align_bytes=64)
+        x_scale = keep.tile([P, FIRST_BYTES], U8, align_bytes=64)
         h = [keep.tile([P, S], F32, name="h%d" % j) for j in range(TILES)]
         x_word = keep.tile([P, FIRST], U32, align_bytes=64)
 
@@ -165,15 +166,15 @@ def tile_picked_hop2_relu_p_kernel(
             acc = bank(where, [P, b - a], "h_acc%d_%d" % (j, a))
             cols = slice(j * P, (j + 1) * P)
             lhs = w1_word[min(j, 2)][:, (j // 3) * P : (j // 3 + 1) * P]
-            for c, e in ((a, b),) if b <= 512 else zip(cuts[2:-1], cuts[3:]):
+            for c, e in ((a, b),) if b <= 512 else ((512, 640), (640, 768), (768, 896), (896, S)):
                 if a <= c and e <= b:
                     words = x_word[:, c:e] if c < FIRST else x_late[:, c - FIRST : e - FIRST]
-                    scales = x_scale[:, c:e] if c < FIRST else x_scale_late[:, c - FIRST : e - FIRST]
+                    scales = x_scale[:, c:e] if c < FIRST_BYTES else x_scale_late[:, c - FIRST_BYTES : e - FIRST_BYTES]
                     product(acc[:, c - a : e - a], lhs, w1_scale[:, cols], words, scales)
             return h[j][:, a:b], acc[:]
 
         cuts = (0, 256, 512, FIRST, 896, S)
-        nc.vector.tensor_copy(x_scale[:], x_scale_table[:].indirect(offs_sb[:, : FIRST // 16]))
+        nc.vector.tensor_copy(x_scale[:], x_scale_table[:].indirect(offs_sb[:, : FIRST_BYTES // 16]))
         low = [keep.tile([P, 512], BF16, name="w1_low%d" % n, align_bytes=64) for n in range(2)]
         grouped = keep.tile([P, 1024], BF16, align_bytes=64)
         planes = grouped[:].rearrange("p (c half q t) -> p half q t c", c=2, half=2, t=4)
@@ -188,9 +189,9 @@ def tile_picked_hop2_relu_p_kernel(
             ALU.mult,
             ALU.add,
         )
+        x_scale_late = stage.tile([P, S - FIRST_BYTES], U8, offset=0, align_bytes=64)
+        nc.vector.tensor_copy(x_scale_late[:], x_scale_table[:].indirect(offs_sb[:, FIRST_BYTES // 16 :]))
         nc.vector.tensor_copy(x_word[:], x_word_table[:].bitcast(U32).indirect(offs_sb[:, : FIRST // 16]))
-        x_scale_late = stage.tile([P, S - FIRST], U8, offset=0, align_bytes=64)
-        nc.vector.tensor_copy(x_scale_late[:], x_scale_table[:].indirect(offs_sb[:, FIRST // 16 :]))
         quantize_w1(low[0][:], 0)
         x_late = stage.tile([P, S - FIRST], U32, offset=1024, align_bytes=64)
         for a, b in zip(cuts[3:-1], cuts[4:]):
@@ -201,7 +202,7 @@ def tile_picked_hop2_relu_p_kernel(
         nc.vector.tensor_copy(low[1][:].rearrange("p (c q t) -> p q t c", c=2, t=4), w1_raw[1][:, :, :, :2])
         nc.vector.tensor_copy(planes[:, 1], w1_raw[1][:, :, :, 2:])
         for i in range(5):
-            relu(*pieces[i], i == 2)
+            relu(*pieces[i], i == 1)
         quantize_w1(low[1][:], P)
         quantize_w1(grouped[:], 2 * P)
         waiting = {

@@ -202,7 +202,7 @@ def tile_picked_hop2_relu_p_kernel(
         nc.vector.tensor_copy(low[1][:].rearrange("p (c q t) -> p q t c", c=2, t=4), w1_raw[1][:, :, :, :2])
         nc.vector.tensor_copy(planes[:, 1], w1_raw[1][:, :, :, 2:])
         for i in range(5):
-            relu(*pieces[i], i == 1)
+            relu(*pieces[i], False)
         quantize_w1(low[1][:], P)
         quantize_w1(grouped[:], 2 * P)
         waiting = {

@@ -23,7 +23,7 @@ ROW_STEP = 9
 GROUP = 60
 EARLY = 256
 FIRST = 768
-FIRST_BYTES = 640
+FIRST_BYTES = 512
 
 
 def tile_picked_hop2_relu_p_kernel(
@@ -100,22 +100,19 @@ def tile_picked_hop2_relu_p_kernel(
         nc.tensor.transpose(gate_turned[:].rearrange("v d k -> v (d k)")[:, :P], gate_rows[:], ident[:])
         gate_col = keep.tile([P, D, BLOCKS], F32)
         nc.scalar.activation(gate_col[:], gate_turned[:, :, :BLOCKS], ACT.Copy)
-        small = keep.tile([P, BLOCKS, 2], F32)
-        both = keep.tile([P, BLOCKS], F32)
-        for i in range(BLOCKS):
-            nc.scalar.activation(
-                small[:, i, :], gate_turned[:, :2, i], ACT.Abs, scale=2.0**-48, accum_out=both[:, i : i + 1]
-            )
+        small = keep.tile([P, 2, BLOCKS], F32)
+        both = keep.tile([P, 1], F32)
+        nc.scalar.activation(small[:], gate_turned[:, :2, :BLOCKS], ACT.Abs, scale=2.0**-56, accum_out=both[:])
         sign3 = keep.tile([P, BLOCKS], F32)
         nc.scalar.activation(sign3[:], gate_turned[:, 2, :BLOCKS], ACT.Sign)
-        least = stage.tile([P, BLOCKS], F32, offset=0)
+        least = stage.tile([P, 1], F32, offset=0)
         nc.scalar.activation(least[:], both[:], ACT.Copy, bias=2.0**-100)
         side = keep.tile([P, BLOCKS], F32)
         nc.scalar.activation(side[:], sign3[:], ACT.Sign, bias=half[:])
         factor = keep.tile([P, BLOCKS], F32)
         for i in range(BLOCKS):
             col = slice(i, i + 1)
-            nc.scalar.activation(factor[:, col], side[:, col], ACT.Identity, scale=least[:, col], bias=gate_col[:, 2, col])
+            nc.scalar.activation(factor[:, col], side[:, col], ACT.Identity, scale=least[:], bias=gate_col[:, 2, col])
         inverse = keep.tile([P, BLOCKS], F32)
         nc.vector.reciprocal(inverse[:], factor[:])
         ratio_col = [keep.tile([P, 2], F32, name="ratio_col%d" % i) for i in range(BLOCKS)]
@@ -123,8 +120,8 @@ def tile_picked_hop2_relu_p_kernel(
         for i in range(BLOCKS):
             nc.scalar.activation(ratio_col[i][:], gate_col[:, :2, i], ACT.Copy, scale=inverse[:, i : i + 1])
         spread = [bank(6 + d, [P, BLOCKS, P], "spread%d" % d) for d in range(2)]
-        for d in range(2):
-            for i in range(BLOCKS):
+        for i in range(BLOCKS):
+            for d in range(2):
                 nc.tensor.transpose(spread[d][:, i, :], ratio_col[i][:, d : d + 1].to_broadcast([P, P]), ident[:])
 
         def copy_ratio(d):
@@ -166,7 +163,7 @@ def tile_picked_hop2_relu_p_kernel(
             acc = bank(where, [P, b - a], "h_acc%d_%d" % (j, a))
             cols = slice(j * P, (j + 1) * P)
             lhs = w1_word[min(j, 2)][:, (j // 3) * P : (j // 3 + 1) * P]
-            for c, e in ((a, b),) if b <= 512 else ((512, 640), (640, 768), (768, 896), (896, S)):
+            for c, e in ((a, b),) if b <= 512 else zip(cuts[2:-1], cuts[3:]):
                 if a <= c and e <= b:
                     words = x_word[:, c:e] if c < FIRST else x_late[:, c - FIRST : e - FIRST]
                     scales = x_scale[:, c:e] if c < FIRST_BYTES else x_scale_late[:, c - FIRST_BYTES : e - FIRST_BYTES]

@@ -1,6 +1,7 @@
 from contextlib import ExitStack
 
 import concourse.mybir as mybir
+from concourse.masks import make_identity
 
 K, T, S, D, V, H, N, U = 512, 2048, 1024, 3, 512, 512, 128, 256
 P = 128
@@ -22,7 +23,7 @@ BANK = 2048
 ROW_STEP = 9
 GROUP = 60
 EARLY = 256
-FIRST = 768
+FIRST = 640
 FIRST_BYTES = 512
 
 
@@ -93,6 +94,8 @@ def tile_picked_hop2_relu_p_kernel(
         for q in range(4):
             quad = slice(32 * q, 32 * (q + 1))
             nc.vector.tensor_tensor(ident[quad, quad], count[quad, :], count_turned[quad, :], ALU.is_equal)
+        ident_late = keep.tile([P, P], F32)
+        make_identity(nc, ident_late[:])
         half = keep.tile([P, 1], F32)
         nc.gpsimd.memset(half[:], 0.5)
 
@@ -116,13 +119,13 @@ def tile_picked_hop2_relu_p_kernel(
         inverse = keep.tile([P, BLOCKS], F32)
         nc.vector.reciprocal(inverse[:], factor[:])
         ratio_col = [keep.tile([P, 2], F32, name="ratio_col%d" % i) for i in range(BLOCKS)]
-        ratio = [stage.tile([P, V], F32, name="ratio%d" % d, offset=2560 + 2048 * d) for d in range(2)]
+        ratio = [keep.tile([P, V], F32, name="ratio%d" % d) for d in range(2)]
         for i in range(BLOCKS):
             nc.scalar.activation(ratio_col[i][:], gate_col[:, :2, i], ACT.Copy, scale=inverse[:, i : i + 1])
         spread = [bank(6 + d, [P, BLOCKS, P], "spread%d" % d) for d in range(2)]
         for i in range(BLOCKS):
             for d in range(2):
-                nc.tensor.transpose(spread[d][:, i, :], ratio_col[i][:, d : d + 1].to_broadcast([P, P]), ident[:])
+                nc.tensor.transpose(spread[d][:, i, :], ratio_col[i][:, d : d + 1].to_broadcast([P, P]), ident_late[:])
 
         def copy_ratio(d):
             nc.scalar.activation(ratio[d][:], spread[d][:].rearrange("p i v -> p (i v)"), ACT.Copy)
@@ -175,12 +178,12 @@ def tile_picked_hop2_relu_p_kernel(
         low = [keep.tile([P, 512], BF16, name="w1_low%d" % n, align_bytes=64) for n in range(2)]
         grouped = keep.tile([P, 1024], BF16, align_bytes=64)
         planes = grouped[:].rearrange("p (c half q t) -> p half q t c", c=2, half=2, t=4)
-        copy_ratio(0)
         nc.scalar.activation(low[0][:].rearrange("p (c q t) -> p q t c", c=2, t=4), w1_raw[0][:, :, :, :2], ACT.Copy)
+        copy_ratio(0)
         copy_ratio(1)
         nc.gpsimd.tensor_scalar(
-            planes[:, 0].rearrange("p q t c -> p c q t"),
-            w1_raw[0][:, :, :, 2:].rearrange("p q t c -> p c q t"),
+            planes[:, 0].rearrange("p q t c -> p q c t"),
+            w1_raw[0][:, :, :, 2:].rearrange("p q t c -> p q c t"),
             1.0,
             0.0,
             ALU.mult,
@@ -290,9 +293,9 @@ def tile_picked_hop2_relu_p_kernel(
         for i in (1, 2, 3):
             round_and_turn(1, i)
 
-        z_direct = keep.tile([P, P, 4], BF16, align_bytes=64)
+        z_direct = stage.tile([P, P, 4], BF16, offset=14336, align_bytes=64)
         z_pair = stage.tile([P, 2 * P, 4], BF16, offset=12288, align_bytes=64)
-        z_one = stage.tile([P, P, 4], BF16, offset=14336, align_bytes=64)
+        z_one = keep.tile([P, P, 4], BF16, align_bytes=64)
         nc.scalar.copy(
             z_pair[:].bitcast(F32).rearrange("p (i v) u -> p i v u", i=2), back_pair[:].rearrange("p i u v -> p i v u")
         )
@@ -326,11 +329,11 @@ def tile_picked_hop2_relu_p_kernel(
             return g[:, a:b], acc[:]
 
         pair = second_product(z_pair[:], z_word[:, : 2 * P], P, 3 * P, 6)
-        summed = second_product(z_direct[:], z_word_direct[:], 0, P, 3)
         one = second_product(z_one[:], z_word[:, 2 * P :], 3 * P, V, 7)
+        summed = second_product(z_direct[:], z_word_direct[:], 0, P, 3)
         relu(*pair, True)
-        relu(*summed, False)
         relu(*one, False)
+        relu(*summed, False)
 
         front, rear = slice(0, U // 2), slice(U // 2, U)
         third = keep.tile([P, U], F32)

@@ -125,7 +125,14 @@ def tile_picked_hop2_relu_p_kernel(
         spread = [bank(6 + d, [P, BLOCKS, P], "spread%d" % d) for d in range(2)]
         for i in range(BLOCKS):
             for d in range(2):
-                nc.tensor.transpose(spread[d][:, i, :], ratio_col[i][:, d : d + 1].to_broadcast([P, P]), ident_late[:])
+                nc.tensor.matmul(
+                    spread[d][:, i, :],
+                    ratio_col[i][:, d : d + 1].to_broadcast([P, P]),
+                    ident_late[:],
+                    start=(i == 0),
+                    stop=(i == BLOCKS - 1),
+                    is_transpose=True,
+                )
 
         def copy_ratio(d):
             nc.scalar.activation(ratio[d][:], spread[d][:].rearrange("p i v -> p (i v)"), ACT.Copy)
@@ -145,15 +152,15 @@ def tile_picked_hop2_relu_p_kernel(
         h = [keep.tile([P, S], F32, name="h%d" % j) for j in range(TILES)]
         x_word = keep.tile([P, FIRST], U32, align_bytes=64)
 
-        def product(acc, lhs_word, lhs_scale, rhs_word, rhs_scale):
+        def product(acc, lhs_word, lhs_scale, rhs_word, rhs_scale, start=True, stop=True):
             nc.tensor.matmul_mx(
                 out=acc,
                 lhsT=lhs_word.bitcast(FP8X4),
                 lhsT_scale=lhs_scale,
                 rhs=rhs_word.bitcast(FP8X4),
                 rhs_scale=rhs_scale,
-                start=True,
-                stop=True,
+                start=start,
+                stop=stop,
             )
 
         def relu(dst, acc, on_vector):
@@ -170,7 +177,7 @@ def tile_picked_hop2_relu_p_kernel(
                 if a <= c and e <= b:
                     words = x_word[:, c:e] if c < FIRST else x_late[:, c - FIRST : e - FIRST]
                     scales = x_scale[:, c:e] if c < FIRST_BYTES else x_scale_late[:, c - FIRST_BYTES : e - FIRST_BYTES]
-                    product(acc[:, c - a : e - a], lhs, w1_scale[:, cols], words, scales)
+                    product(acc[:, c - a : e - a], lhs, w1_scale[:, cols], words, scales, c == a, e == b)
             return h[j][:, a:b], acc[:]
 
         cuts = (0, 256, 512, FIRST, 896, S)
@@ -240,7 +247,10 @@ def tile_picked_hop2_relu_p_kernel(
             else:
                 values = keep.tile([P, b - a], F32, name="term%d_%d_%d" % (j, d, a))
             gather(values[:], j, d, a, b, ratio[d][:, a:b] if d < 2 else None)
-            for i in range(a // P, b // P):
+            blocks = range(a // P, b // P)
+            if (j, d) != (3, 1):
+                blocks = sorted(blocks, key=lambda block: (block + j // 2) % 2)
+            for i in blocks:
                 n = group[j // 2][i]
                 nc.tensor.matmul(
                     sums[j // 2][i][:, j % 2, :],

@@ -22,7 +22,7 @@ BLOCKS = V // P
 BANK = 2048
 ROW_STEP = 9
 GROUP = 60
-EARLY = 256
+EARLY = 512
 FIRST = 640
 FIRST_BYTES = 512
 

@@ -265,9 +265,9 @@ def tile_picked_hop2_relu_p_kernel(
 
         rows = keep.tile([P, 2, BLOCKS, P, 2], BF16)
         back_direct = bank(0, [P, 1, P], "back_direct")
-        back_pair = bank(1, [P, 2, 2, P], "back_pair")
+        back_pair = [bank(1 + 2 * n, [P, 2, P], "back_pair%d" % n) for n in range(2)]
         back_one = bank(2, [P, 2, P], "back_one")
-        back = [back_direct[:], back_pair[:, 0], back_pair[:, 1], back_one[:]]
+        back = [back_direct[:], back_pair[0][:], back_pair[1][:], back_one[:]]
 
         def round_and_turn(u, i, on_vector=False):
             if u == 0:
@@ -306,9 +306,8 @@ def tile_picked_hop2_relu_p_kernel(
         z_direct = stage.tile([P, P, 4], BF16, offset=14336, align_bytes=64)
         z_pair = stage.tile([P, 2 * P, 4], BF16, offset=12288, align_bytes=64)
         z_one = keep.tile([P, P, 4], BF16, align_bytes=64)
-        nc.scalar.copy(
-            z_pair[:].bitcast(F32).rearrange("p (i v) u -> p i v u", i=2), back_pair[:].rearrange("p i u v -> p i v u")
-        )
+        for n in range(2):
+            nc.scalar.copy(z_pair[:, n * P : (n + 1) * P].bitcast(F32), back_pair[n][:].rearrange("p u v -> p v u"))
         nc.scalar.copy(z_one[:].bitcast(F32), back_one[:].rearrange("p u v -> p v u"))
         nc.scalar.copy(z_direct[:].bitcast(F32)[:, :, :1], back_direct[:].rearrange("p u v -> p v u"))
 
@@ -330,7 +329,7 @@ def tile_picked_hop2_relu_p_kernel(
         z_word = keep.tile([P, V - P], U32, align_bytes=64)
         z_word_direct = stage.tile([P, P], U32, offset=12288, align_bytes=64)
         z_scale = keep.tile([P, V], U8, align_bytes=64)
-        g = stage.tile([P, V], F32, offset=14336)
+        g = keep.tile([P, V], F32)
 
         def second_product(z, words, a, b, where):
             nc.vector.quantize_mx(out=words.bitcast(FP8X4), scales=z_scale[:, a:b], in_=z.rearrange("p v t -> p (v t)"))
@@ -338,11 +337,15 @@ def tile_picked_hop2_relu_p_kernel(
             product(acc[:], w2_word_sb[:], w2_scale_sb[:], words, z_scale[:, a:b])
             return g[:, a:b], acc[:]
 
-        pair = second_product(z_pair[:], z_word[:, : 2 * P], P, 3 * P, 6)
+        pair = [
+            second_product(z_pair[:, n * P : (n + 1) * P], z_word[:, n * P : (n + 1) * P], (n + 1) * P, (n + 2) * P, (6, 4)[n])
+            for n in range(2)
+        ]
         one = second_product(z_one[:], z_word[:, 2 * P :], 3 * P, V, 7)
-        summed = second_product(z_direct[:], z_word_direct[:], 0, P, 3)
-        relu(*pair, True)
-        relu(*one, False)
+        summed = second_product(z_direct[:], z_word_direct[:], 0, P, 0)
+        relu(*pair[0], False)
+        relu(*pair[1], False)
+        relu(*one, True)
         relu(*summed, False)
 
         front, rear = slice(0, U // 2), slice(U // 2, U)

@@ -299,7 +299,7 @@ def tile_picked_hop2_relu_p_kernel(
         term(3, 2, P, V)
         term(3, 1, P, V)
         for i in (1, 2, 3, 0):
-            round_and_turn(0, i)
+            round_and_turn(0, i, on_vector=(i == 0))
         for i in (1, 2, 3):
             round_and_turn(1, i)
 

from contextlib import ExitStack

import concourse.mybir as mybir
from concourse.masks import make_identity

K, T, S, D, V, H, N, U = 512, 2048, 1024, 3, 512, 512, 128, 256
P = 128
FLOPS = 2 * K * H * S + 2 * H * N * V

F32 = mybir.dt.float32
BF16 = mybir.dt.bfloat16
I32 = mybir.dt.int32
U32 = mybir.dt.uint32
U16 = mybir.dt.uint16
U8 = mybir.dt.uint8
FP8X4 = mybir.dt.float8_e4m3fn_x4
ALU = mybir.AluOpType
ACT = mybir.ActivationFunctionType

TILES = H // P
BLOCKS = V // P
BANK = 2048
ROW_STEP = 9
GROUP = 60
EARLY = 512
FIRST = 640
FIRST_BYTES = 512


def tile_picked_hop2_relu_p_kernel(
    tc, x_words, x_scales, w1, w2_words, w2_scales, gate, gate2, offs, pos1, pos2, pos3, nxt1, nxt2, nxt3, out
):
    nc = tc.nc
    with ExitStack() as ctx:
        keep = ctx.enter_context(tc.tile_pool(name="keep", bufs=1))
        stage = ctx.enter_context(tc.tile_pool(name="stage", bufs=1))
        psum = ctx.enter_context(tc.psum_pool(name="psum", bufs=1))

        def bank(b, shape, name):
            return psum.tile(shape, F32, name=name, offset=b * BANK)

        def load_list(src, name):
            tile = keep.tile(list(src.shape), U16, name=name)
            nc.sync.dma_start(tile[:], src)
            return tile

        def load_scale_rows(plane, src, queues):
            for q in range(4):
                queues[q].dma_start(
                    plane[32 * q : 32 * q + 4, :].bitcast(I32), src[0, 4 * q : 4 * q + 4, :].bitcast(I32)
                )

        def load_words(words, src):
            nc.sync.dma_start(words[:], src[0].rearrange("p n t -> p (n t)").bitcast(I32))

        w1_rows = w1.rearrange("(p t) c -> p t c", t=4)

        def load_w1(a, b, offset):
            raw = stage.tile([P, 4, b - a], F32, name="w1_raw%d" % a, offset=offset)
            nc.sync.dma_start(raw[:], w1_rows[:, :, a:b])
            return raw[:].rearrange("p t (q c) -> p q t c", c=4)

        x_scale_table = keep.tile([P, T], U8, align_bytes=64)
        nc.vector.memset(x_scale_table[:].bitcast(I32), 0)
        load_scale_rows(x_scale_table, x_scales, (nc.sync, nc.scalar, nc.sync, nc.scalar))
        gate_rows = keep.tile([P, P], F32)
        nc.sync.dma_start(gate_rows[:], gate.rearrange("d r (i c) -> (d r i) c", c=P)[0 : ROW_STEP * P : ROW_STEP, :])
        x_word_table = keep.tile([P, T], I32, align_bytes=64)
        x_word_rows = x_words[0].rearrange("p n t -> p (n t)").bitcast(I32)
        nc.sync.dma_start(x_word_table[:, :EARLY], x_word_rows[:, :EARLY])
        offs_sb = load_list(offs, "offs_sb")
        nc.sync.dma_start(x_word_table[:, EARLY:], x_word_rows[:, EARLY:])
        w1_raw = [load_w1(0, H // 2, 1024), load_w1(H // 2, H, 20480)]
        pos_sb = [load_list(src, "pos_sb%d" % d) for d, src in enumerate((pos1, pos2, pos3))]
        w2_word_sb = keep.tile([P, N], I32, align_bytes=64)
        load_words(w2_word_sb, w2_words)
        w2_scale_sb = keep.tile([P, N], U8, align_bytes=64)
        nc.vector.memset(w2_scale_sb[:].bitcast(I32), 0)
        load_scale_rows(w2_scale_sb, w2_scales, (nc.sync,) * 4)
        gate_direct = keep.tile([P, D, P], F32)
        nc.sync.dma_start(gate_direct[:], gate.rearrange("d p v -> p d v")[:, :, :P])
        nxt_sb = [load_list(src, "nxt_sb%d" % d) for d, src in enumerate((nxt1, nxt2, nxt3))]
        gate2_sb = keep.tile([P, D, U], F32)
        nc.sync.dma_start(gate2_sb[:], gate2.rearrange("d p r -> p d r"))

        ident = keep.tile([P, P], F32)
        nc.gpsimd.memset(ident[:], 0.0)
        ones = keep.tile([P, 32], F32)
        nc.gpsimd.memset(ones[:], 1.0)
        count = keep.tile([P, 32], F32, align_bytes=64)
        nc.vector.tensor_tensor_scan(count[:], ones[:], ones[:], 0.0, ALU.mult, ALU.add)
        count_turned = keep.tile([P, 32], F32, align_bytes=64)
        nc.vector.transpose(count_turned[:], count[:])
        for q in range(4):
            quad = slice(32 * q, 32 * (q + 1))
            nc.vector.tensor_tensor(ident[quad, quad], count[quad, :], count_turned[quad, :], ALU.is_equal)
        ident_late = keep.tile([P, P], F32)
        make_identity(nc, ident_late[:])
        half = keep.tile([P, 1], F32)
        nc.gpsimd.memset(half[:], 0.5)

        gate_turned = bank(5, [P, D, GROUP], "gate_turned")
        nc.tensor.transpose(gate_turned[:].rearrange("v d k -> v (d k)")[:, :P], gate_rows[:], ident[:])
        gate_col = keep.tile([P, D, BLOCKS], F32)
        nc.scalar.activation(gate_col[:], gate_turned[:, :, :BLOCKS], ACT.Copy)
        small = keep.tile([P, 2, BLOCKS], F32)
        both = keep.tile([P, 1], F32)
        nc.scalar.activation(small[:], gate_turned[:, :2, :BLOCKS], ACT.Abs, scale=2.0**-56, accum_out=both[:])
        sign3 = keep.tile([P, BLOCKS], F32)
        nc.scalar.activation(sign3[:], gate_turned[:, 2, :BLOCKS], ACT.Sign)
        least = stage.tile([P, 1], F32, offset=0)
        nc.scalar.activation(least[:], both[:], ACT.Copy, bias=2.0**-100)
        side = keep.tile([P, BLOCKS], F32)
        nc.scalar.activation(side[:], sign3[:], ACT.Sign, bias=half[:])
        factor = keep.tile([P, BLOCKS], F32)
        for i in range(BLOCKS):
            col = slice(i, i + 1)
            nc.scalar.activation(factor[:, col], side[:, col], ACT.Identity, scale=least[:], bias=gate_col[:, 2, col])
        inverse = keep.tile([P, BLOCKS], F32)
        nc.vector.reciprocal(inverse[:], factor[:])
        ratio_col = [keep.tile([P, 2], F32, name="ratio_col%d" % i) for i in range(BLOCKS)]
        ratio = [keep.tile([P, V], F32, name="ratio%d" % d) for d in range(2)]
        for i in range(BLOCKS):
            nc.scalar.activation(ratio_col[i][:], gate_col[:, :2, i], ACT.Copy, scale=inverse[:, i : i + 1])
        spread = [bank(6 + d, [P, BLOCKS, P], "spread%d" % d) for d in range(2)]
        for i in range(BLOCKS):
            for d in range(2):
                nc.tensor.matmul(
                    spread[d][:, i, :],
                    ratio_col[i][:, d : d + 1].to_broadcast([P, P]),
                    ident_late[:],
                    start=(i == 0),
                    stop=(i == BLOCKS - 1),
                    is_transpose=True,
                )

        def copy_ratio(d):
            nc.scalar.activation(ratio[d][:], spread[d][:].rearrange("p i v -> p (i v)"), ACT.Copy)

        w1_word = [
            keep.tile([P, P], U32, name="w1_word0", align_bytes=64),
            stage.tile([P, P], U32, name="w1_word1", offset=11264, align_bytes=64),
            keep.tile([P, 2 * P], U32, name="w1_word2", align_bytes=64),
        ]
        w1_scale = keep.tile([P, H], U8, align_bytes=64)

        def quantize_w1(grouped, first):
            cols = slice(first, first + grouped.shape[1] // 4)
            nc.vector.quantize_mx(out=w1_word[first // P][:].bitcast(FP8X4), scales=w1_scale[:, cols], in_=grouped)

        x_scale = keep.tile([P, FIRST_BYTES], U8, align_bytes=64)
        h = [keep.tile([P, S], F32, name="h%d" % j) for j in range(TILES)]
        x_word = keep.tile([P, FIRST], U32, align_bytes=64)

        def product(acc, lhs_word, lhs_scale, rhs_word, rhs_scale, start=True, stop=True):
            nc.tensor.matmul_mx(
                out=acc,
                lhsT=lhs_word.bitcast(FP8X4),
                lhsT_scale=lhs_scale,
                rhs=rhs_word.bitcast(FP8X4),
                rhs_scale=rhs_scale,
                start=start,
                stop=stop,
            )

        def relu(dst, acc, on_vector):
            if on_vector:
                nc.vector.tensor_scalar(dst, acc, 0.0, None, ALU.max)
            else:
                nc.scalar.activation(dst, acc, ACT.Relu)

        def first_product(j, a, b, where):
            acc = bank(where, [P, b - a], "h_acc%d_%d" % (j, a))
            cols = slice(j * P, (j + 1) * P)
            lhs = w1_word[min(j, 2)][:, (j // 3) * P : (j // 3 + 1) * P]
            for c, e in ((a, b),) if b <= 512 else zip(cuts[2:-1], cuts[3:]):
                if a <= c and e <= b:
                    words = x_word[:, c:e] if c < FIRST else x_late[:, c - FIRST : e - FIRST]
                    scales = x_scale[:, c:e] if c < FIRST_BYTES else x_scale_late[:, c - FIRST_BYTES : e - FIRST_BYTES]
                    product(acc[:, c - a : e - a], lhs, w1_scale[:, cols], words, scales, c == a, e == b)
            return h[j][:, a:b], acc[:]

        cuts = (0, 256, 512, FIRST, 896, S)
        nc.vector.tensor_copy(x_scale[:], x_scale_table[:].indirect(offs_sb[:, : FIRST_BYTES // 16]))
        low = [keep.tile([P, 512], BF16, name="w1_low%d" % n, align_bytes=64) for n in range(2)]
        grouped = keep.tile([P, 1024], BF16, align_bytes=64)
        planes = grouped[:].rearrange("p (c half q t) -> p half q t c", c=2, half=2, t=4)
        nc.scalar.activation(low[0][:].rearrange("p (c q t) -> p q t c", c=2, t=4), w1_raw[0][:, :, :, :2], ACT.Copy)
        copy_ratio(0)
        copy_ratio(1)
        nc.gpsimd.tensor_scalar(
            planes[:, 0].rearrange("p q t c -> p q c t"),
            w1_raw[0][:, :, :, 2:].rearrange("p q t c -> p q c t"),
            1.0,
            0.0,
            ALU.mult,
            ALU.add,
        )
        x_scale_late = stage.tile([P, S - FIRST_BYTES], U8, offset=0, align_bytes=64)
        nc.vector.tensor_copy(x_scale_late[:], x_scale_table[:].indirect(offs_sb[:, FIRST_BYTES // 16 :]))
        nc.vector.tensor_copy(x_word[:], x_word_table[:].bitcast(U32).indirect(offs_sb[:, : FIRST // 16]))
        quantize_w1(low[0][:], 0)
        x_late = stage.tile([P, S - FIRST], U32, offset=1024, align_bytes=64)
        for a, b in zip(cuts[3:-1], cuts[4:]):
            nc.vector.tensor_copy(
                x_late[:, a - FIRST : b - FIRST], x_word_table[:].bitcast(U32).indirect(offs_sb[:, a // 16 : b // 16])
            )
        pieces = [first_product(0, cuts[i], cuts[i + 1], i) for i in range(5)]
        nc.vector.tensor_copy(low[1][:].rearrange("p (c q t) -> p q t c", c=2, t=4), w1_raw[1][:, :, :, :2])
        nc.vector.tensor_copy(planes[:, 1], w1_raw[1][:, :, :, 2:])
        for i in range(5):
            relu(*pieces[i], False)
        quantize_w1(low[1][:], P)
        quantize_w1(grouped[:], 2 * P)
        waiting = {
            j: [first_product(j, n * S // 2, (n + 1) * S // 2, (2 * j + 3 + n) % 6) for n in range(2)]
            for j in range(1, TILES)
        }

        def finish(j):
            for dst, acc in waiting[j]:
                relu(dst, acc, False)

        low_sum = [bank(6 + n, [P, 2, 2, P], "low_sum%d" % n) for n in range(2)]
        high_pair = bank(4, [P, 2, 2, P], "high_pair")
        high_one = bank(5, [P, 2, P], "high_one")
        sums = [
            [low_sum[0][:, 0], low_sum[0][:, 1], low_sum[1][:, 0], low_sum[1][:, 1]],
            [None, high_pair[:, 0], high_pair[:, 1], high_one[:]],
        ]
        group = [[0, 0, 1, 1], [None, 2, 2, 3]]
        left = [12, 12, 12, 6]
        size = list(left)

        def gather(values, j, d, a, b, weights):
            window = h[j][:].indirect(pos_sb[d][:, a // 16 : b // 16])
            if weights is None:
                nc.scalar.activation(values, window, ACT.Copy)
            else:
                nc.vector.tensor_tensor(values, window, weights, ALU.mult)

        def term(j, d, a, b):
            if j == 0 and d != 1:
                values = stage.tile([P, b - a], F32, name="term_first%d_%d" % (d, a), offset=(20480 + 1024 * d, 11264)[a // 256])
            elif (j, d) == (3, 0):
                values = stage.tile([P, 2 * (b - a)], F32, name="term_held", offset=16384)[:, : b - a]
            else:
                values = keep.tile([P, b - a], F32, name="term%d_%d_%d" % (j, d, a))
            gather(values[:], j, d, a, b, ratio[d][:, a:b] if d < 2 else None)
            blocks = range(a // P, b // P)
            if (j, d) != (3, 1):
                blocks = sorted(blocks, key=lambda block: (block + j // 2) % 2)
            for i in blocks:
                n = group[j // 2][i]
                nc.tensor.matmul(
                    sums[j // 2][i][:, j % 2, :],
                    values[:, i * P - a : (i + 1) * P - a],
                    ident[:],
                    start=(left[n] == size[n]),
                    stop=(left[n] == 1),
                    is_transpose=True,
                )
                left[n] = left[n] - 1
            return values

        rows = keep.tile([P, 2, BLOCKS, P, 2], BF16)
        back_direct = bank(0, [P, 1, P], "back_direct")
        back_pair = [bank(1 + 2 * n, [P, 2, P], "back_pair%d" % n) for n in range(2)]
        back_one = bank(2, [P, 2, P], "back_one")
        back = [back_direct[:], back_pair[0][:], back_pair[1][:], back_one[:]]

        def round_and_turn(u, i, on_vector=False):
            if u == 0:
                dst = rows[:, u, i].rearrange("v (j q) e -> v j q e", j=2)
                src = sums[u][i].rearrange("v j (e q) -> v j q e", e=2)
            else:
                dst = rows[:, u, i]
                src = sums[u][i].rearrange("v e p -> v p e")
            if on_vector:
                nc.vector.tensor_scalar(dst, src, factor[:, i : i + 1], None, ALU.mult)
            else:
                nc.scalar.activation(dst, src, ACT.Copy, scale=factor[:, i : i + 1])
            nc.tensor.transpose(back[i][:, u, :], rows[:, u, i].rearrange("v p e -> v (p e)").bitcast(F32), ident[:])

        term(0, 0, 0, V)
        term(0, 2, 0, V // 2)
        finish(1)
        term(0, 1, 0, V)
        term(0, 2, V // 2, V)
        finish(2)
        term(1, 0, 0, V)
        term(1, 1, 0, V)
        term(1, 2, 0, V)
        finish(3)
        term(2, 0, P, V)
        term(2, 1, P, V)
        term(2, 2, P, V)
        term(3, 0, P, V)
        term(3, 2, P, V)
        term(3, 1, P, V)
        for i in (1, 2, 3, 0):
            round_and_turn(0, i, on_vector=(i == 0))
        for i in (1, 2, 3):
            round_and_turn(1, i)

        z_direct = stage.tile([P, P, 4], BF16, offset=14336, align_bytes=64)
        z_pair = stage.tile([P, 2 * P, 4], BF16, offset=12288, align_bytes=64)
        z_one = keep.tile([P, P, 4], BF16, align_bytes=64)
        for n in range(2):
            nc.scalar.copy(z_pair[:, n * P : (n + 1) * P].bitcast(F32), back_pair[n][:].rearrange("p u v -> p v u"))
        nc.scalar.copy(z_one[:].bitcast(F32), back_one[:].rearrange("p u v -> p v u"))
        nc.scalar.copy(z_direct[:].bitcast(F32)[:, :, :1], back_direct[:].rearrange("p u v -> p v u"))

        halves = (slice(0, P // 2), slice(P // 2, P))
        direct = [stage.tile([P, 2, P], F32, name="direct%d" % d, offset=16384 + 1024 * d) for d in range(D)]
        for d in range(D):
            for e in range(2):
                gather(direct[d][:, e, :], 2 + e, d, 0, P, gate_direct[:, d, :])
        two = keep.tile([P, 2, P], F32)
        for part in halves:
            nc.vector.tensor_tensor(two[:, :, part], direct[0][:, :, part], direct[1][:, :, part], ALU.add)
        for part in halves:
            nc.vector.tensor_tensor(
                z_direct[:, part, 2:],
                two[:, :, part].rearrange("p e v -> p v e"),
                direct[2][:, :, part].rearrange("p e v -> p v e"),
                ALU.add,
            )
        z_word = keep.tile([P, V - P], U32, align_bytes=64)
        z_word_direct = stage.tile([P, P], U32, offset=12288, align_bytes=64)
        z_scale = keep.tile([P, V], U8, align_bytes=64)
        g = keep.tile([P, V], F32)

        def second_product(z, words, a, b, where):
            nc.vector.quantize_mx(out=words.bitcast(FP8X4), scales=z_scale[:, a:b], in_=z.rearrange("p v t -> p (v t)"))
            acc = bank(where, [P, b - a], "g_acc%d" % a)
            product(acc[:], w2_word_sb[:], w2_scale_sb[:], words, z_scale[:, a:b])
            return g[:, a:b], acc[:]

        pair = [
            second_product(z_pair[:, n * P : (n + 1) * P], z_word[:, n * P : (n + 1) * P], (n + 1) * P, (n + 2) * P, (6, 4)[n])
            for n in range(2)
        ]
        one = second_product(z_one[:], z_word[:, 2 * P :], 3 * P, V, 7)
        summed = second_product(z_direct[:], z_word_direct[:], 0, P, 0)
        relu(*pair[0], False)
        relu(*pair[1], False)
        relu(*one, True)
        relu(*summed, False)

        front, rear = slice(0, U // 2), slice(U // 2, U)
        third = keep.tile([P, U], F32)
        nc.scalar.activation(third[:], g[:].indirect(nxt_sb[2][:]), ACT.Copy)
        second_rear = keep.tile([P, U // 2], F32)
        nc.scalar.activation(second_rear[:], g[:].indirect(nxt_sb[1][:, U // 32 :]), ACT.Copy)
        terms = [keep.tile([P, U], F32, name="root_term%d" % d) for d in range(D)]
        nc.vector.tensor_tensor(terms[0][:], g[:].indirect(nxt_sb[0][:]), gate2_sb[:, 0, :], ALU.mult)
        nc.vector.tensor_tensor(terms[1][:, front], g[:].indirect(nxt_sb[1][:, : U // 32]), gate2_sb[:, 1, front], ALU.mult)
        nc.vector.tensor_tensor(terms[2][:], third[:], gate2_sb[:, 2, :], ALU.mult)
        partial = keep.tile([P, U], F32)
        result = keep.tile([P, U], F32)
        nc.vector.tensor_tensor(partial[:, front], terms[0][:, front], terms[1][:, front], ALU.add)
        nc.vector.tensor_tensor(partial[:, rear], terms[0][:, rear], terms[2][:, rear], ALU.add)
        nc.vector.tensor_tensor(terms[1][:, rear], second_rear[:], gate2_sb[:, 1, rear], ALU.mult)
        nc.vector.tensor_tensor(result[:, front], partial[:, front], terms[2][:, front], ALU.add)
        nc.vector.tensor_tensor(result[:, rear], partial[:, rear], terms[1][:, rear], ALU.add)
        nc.sync.dma_start(out, result[:])
